import numpy as np
import ml_dtypes


def mxq(x, axis, fmt="e4m3"):
    dtype, down = {"e4m3": (ml_dtypes.float8_e4m3fn, 7), "e5m2": (ml_dtypes.float8_e5m2, 14)}[fmt]
    v = np.moveaxis(np.asarray(x, np.float32).astype(ml_dtypes.bfloat16).astype(np.float64), axis, -1)
    blocks = v.reshape(v.shape[:-1] + (-1, 32))
    amax = np.abs(blocks).max(-1, keepdims=True)
    byte = np.maximum(np.where(amax > 0, np.frexp(amax)[1] - 1 + 127, 0) - down, 1)
    scale = np.exp2(byte - 127.0)
    codes = (blocks / scale).astype(np.float32).astype(dtype).astype(np.float64)
    return np.moveaxis((codes * scale).reshape(v.shape), -1, axis)


WIDE = False


def mx_kscale(k):
    if not WIDE:
        return np.ones(k)
    levels = np.array([10, -10, 5, -5, 0])
    if k % 512:
        return np.exp2(np.random.permutation(np.resize(levels, k // 32))).repeat(32)
    a = np.empty((k // 512, 16))
    for p in range(k // 512):
        a[p, :8] = np.random.permutation(np.resize(levels, 8))
        for g in range(8):
            far = levels[np.abs(levels - a[p, g]) >= 10]
            a[p, g + 8] = far[np.random.randint(len(far))]
    return np.exp2(a.ravel()).repeat(32)


def f64(x):
    return np.asarray(x).astype(np.float64)


def striped(idx):
    return np.tile(idx.reshape(-1, 16).T, (8, 1)).astype(np.uint16)


def unstriped(offs):
    return offs[:16].T.reshape(-1).astype(np.int64)


def d_relu2(v):
    return 2.0 * np.maximum(v, 0.0)


K, T, E, C, H, N = 512, 768, 12, 128, 512, 512


def by_expert(wq, xq):
    return np.concatenate([wq[e].T @ xq[:, e * C:(e + 1) * C] for e in range(E)], axis=1)


def setup_inputs():
    n = np.random.standard_normal
    s = mx_kscale(N)[:, None]
    u = mx_kscale(H)
    first = np.random.permutation(np.repeat(np.arange(E), T // E))
    second = (first + 1 + np.random.permutation(np.repeat(np.arange(E - 1), -(-T // (E - 1)))[:T])) % E
    while np.bincount(second, minlength=E).max() != T // E:
        load = np.bincount(second, minlength=E); hi, lo = int(load.argmax()), int(load.argmin())
        t = np.flatnonzero((second == hi) & (first != lo))[0]; second[t] = lo
    slot_token = np.empty(E * C, np.int64); pos = np.empty((2, T), np.int64); fill = np.zeros(E, np.int64)
    place = np.stack([np.random.permutation(C) for _ in range(E)])
    for r, deal in enumerate((first, second)):
        for t in np.random.permutation(T):
            e = deal[t]; j = e * C + place[e, fill[e]]; fill[e] += 1; slot_token[j] = t; pos[r, t] = j
    g = np.random.uniform(0.2, 0.8, T)
    w_slot = np.empty(E * C); w_slot[pos[0]] = g; w_slot[pos[1]] = 1.0 - g
    return {
        "dyT": (n((N, T)) * s).astype(np.float32),
        "a": n((H, E * C)).astype(np.float32),
        "w2": (n((E, N, H)) / np.sqrt(N) / s[None] * u[None, None, :]).astype(np.float32),
        "w1": (n((E, H, K)) / np.sqrt(H) / u[None, :, None]).astype(np.float32),
        "gate": np.tile(w_slot, (N, 1)).astype(np.float32),
        "offs": striped(slot_token),
        "pos1": striped(pos[0]),
        "pos2": striped(pos[1]),
    }


def reference(dyT, a, w2, w1, gate, offs, pos1, pos2):
    idx = unstriped(offs)
    gq = mxq(f64(gate) * f64(dyT)[:, idx], 0, "e4m3")
    dh = by_expert(mxq(f64(w2), 1, "e4m3"), gq)
    da = dh * d_relu2(f64(a))
    dx = by_expert(mxq(f64(w1), 1, "e4m3"), mxq(da, 0, "e4m3"))
    return dx[:, unstriped(pos1)] + dx[:, unstriped(pos2)]

@@ -1,0 +1,282 @@
+from contextlib import ExitStack
+
+import concourse.mybir as mybir
+
+K, T, E, C, H, N = 512, 768, 12, 128, 512, 512
+S = E * C
+
+F32 = mybir.dt.float32
+BF16 = mybir.dt.bfloat16
+U32 = mybir.dt.uint32
+U16 = mybir.dt.uint16
+U8 = mybir.dt.uint8
+FP8X4 = mybir.dt.float8_e4m3fn_x4
+MULT = mybir.AluOpType.mult
+ADD = mybir.AluOpType.add
+MAX = mybir.AluOpType.max
+COPY = mybir.ActivationFunctionType.Copy
+
+FLOPS = 2 * 2 * S * N * H
+BYTES = 4 * (N * T + H * S + 2 * E * N * H + S + K * T) + 2 * 128 * (S + 2 * T) // 16
+
+P = 128
+PACK = 4
+G_W = 512
+A_W = 256
+GROUPS = S // G_W
+GPSIMD_COLS = 24
+QUAD = 4
+UNITS = 2 * E
+
+
+def tile_moe_bdx_mlp_relu2_kernel(tc, dyT, a, w2, w1, gate, offs, pos1, pos2, out):
+    nc = tc.nc
+    with ExitStack() as ctx:
+        held = ctx.enter_context(tc.tile_pool(name="held", bufs=1))
+        work = ctx.enter_context(tc.tile_pool(name="work", bufs=2))
+        psum = ctx.enter_context(tc.psum_pool(name="psum", bufs=4))
+
+        offs_t = held.tile([P, S // 16], U16)
+        pos1_t = held.tile([P, T // 16], U16)
+        pos2_t = held.tile([P, T // 16], U16)
+        gate_t = []
+        g_q = []
+        for g in range(GROUPS):
+            gt = held.tile([P, G_W], F32, name=f"gate{g}")
+            gate_t.append(gt)
+            gc = held.tile([P, G_W], U32, name=f"gc{g}", align_bytes=64)
+            gs = held.tile([P, G_W], U8, name=f"gs{g}", align_bytes=64)
+            g_q.append((gc, gs))
+        dx = {}
+
+        nc.sync.dma_start(offs_t[:], offs)
+
+        def load_gate(g):
+            nc.sync.dma_start(gate_t[g][:], gate[0:P, g * G_W : (g + 1) * G_W])
+
+        load_gate(0)
+        dy_rows = dyT.rearrange("(p j) t -> p j t", j=PACK)
+        dy = []
+        for j in range(PACK):
+            d = held.tile([P, T], F32, name=f"dy{j}", tag="plane", bufs=4)
+            dy.append(d)
+
+        a_rows = a.rearrange("(p j) s -> p j s", j=PACK)
+        raw = {}
+        a_t = {}
+
+        def load_a(g):
+            at = work.tile([P, PACK, A_W], F32, name="a_t", bufs=6)
+            nc.sync.dma_start(at[:], a_rows[:, :, g * A_W : (g + 1) * A_W])
+            a_t[g] = at
+
+        def load_unit(u):
+            wr = work.tile([P, PACK, H], F32, name="raw", bufs=12)
+            if u < E:
+                rows = w2[u].rearrange("(p j) i -> p j i", j=PACK)
+                for j in range(0, PACK, 2):
+                    nc.sync.dma_start(wr[:, j : j + 2, :], rows[:, j : j + 2, :])
+            else:
+                q, quad = divmod(u - E, E // QUAD)
+                for s in range(QUAD):
+                    rows = w1[quad * QUAD + s].rearrange("(p j) k -> p j k", j=PACK)
+                    nc.sync.dma_start(wr[:, :, s * P : (s + 1) * P], rows[:, :, q * P : (q + 1) * P])
+            raw[u] = wr
+
+        def load_pos():
+            nc.sync.dma_start(pos1_t[:], pos1)
+            nc.sync.dma_start(pos2_t[:], pos2)
+
+        for j in range(PACK):
+            nc.sync.dma_start(dy[j][:], dy_rows[:, j, :])
+        loads = []
+        for u in range(UNITS):
+            loads.append(lambda u=u: load_unit(u))
+            if u < E and u % 2 == 0:
+                loads.append(lambda u=u: load_a(u // 2))
+            if u in (1, 3):
+                loads.append(lambda u=u: load_gate(u // 2 + 1))
+            if u == 10:
+                loads.append(load_pos)
+
+        def advance(n):
+            for _ in range(n):
+                if loads:
+                    loads.pop(0)()
+
+        g32 = {}
+        gb = {}
+
+        def gather(g, j):
+            if j == 0:
+                gt = work.tile([P, PACK, G_W], F32, name="g32", tag="g32")
+                g32[g] = gt
+            lst = offs_t[:, g * G_W // 16 : (g + 1) * G_W // 16]
+            nc.vector.tensor_tensor(g32[g][:, j, :], dy[j][:].indirect(lst), gate_t[g][:], MULT)
+
+        def interleave(dst, src, copy, c0=0, c1=H // 4):
+            copy(
+                dst[:].rearrange("p (c i j) -> p c j i", i=4, j=PACK)[:, c0:c1],
+                src[:].rearrange("p j (c i) -> p c j i", i=4)[:, c0:c1],
+            )
+
+        def pack_g(g):
+            gt = work.tile([P, G_W * PACK], BF16, name="gb", bufs=1, align_bytes=64)
+            interleave(gt, g32.pop(g), nc.vector.tensor_copy)
+            gb[g] = gt
+
+        def quant_g(g):
+            nc.vector.quantize_mx(out=g_q[g][0][:].bitcast(FP8X4), scales=g_q[g][1][:], in_=gb.pop(g)[:])
+
+        wb = {}
+        w_q = {}
+
+        def gpsimd_copy(dst, src):
+            nc.gpsimd.tensor_scalar(dst, src, 1.0, 0.0, MULT, ADD)
+
+        def pack(u):
+            while u not in raw:
+                advance(1)
+            wt = work.tile([P, H * PACK], BF16, name="wb", bufs=5, align_bytes=64)
+            if u < E:
+                nc.scalar.copy(
+                    wt[:].rearrange("p (t m j) -> p m j t", t=PACK, j=PACK),
+                    raw[u][:].rearrange("p j (m t) -> p m j t", t=PACK),
+                )
+            else:
+                interleave(wt, raw[u], gpsimd_copy, c1=GPSIMD_COLS)
+                interleave(wt, raw[u], nc.scalar.copy, c0=GPSIMD_COLS)
+            wb[u] = wt
+
+        def quant(u):
+            wc = work.tile([P, H], U32, name="wc", bufs=3, align_bytes=64)
+            ws = work.tile([P, H], U8, name="ws", bufs=3, align_bytes=64)
+            nc.vector.quantize_mx(out=wc[:].bitcast(FP8X4), scales=ws[:], in_=wb.pop(u)[:])
+            w_q[u] = (wc, ws)
+
+        bank = {}
+        da_q = {}
+
+        def multiply(u):
+            wc, ws = w_q.pop(u)
+            bk = psum.tile([P, QUAD, C], F32, name="bank", bufs=6)
+            for t in range(QUAD):
+                if u < E:
+                    e = u
+                    mc, ms = g_q[e // QUAD]
+                    cols = slice(e % QUAD * C, e % QUAD * C + C)
+                else:
+                    e = (u - E) % (E // QUAD) * QUAD + t
+                    mc, ms = da_q[e // 2]
+                    cols = slice(e % 2 * C, e % 2 * C + C)
+                nc.tensor.matmul_mx(
+                    out=bk[:, t, :],
+                    lhsT=wc[:, t * P : (t + 1) * P].bitcast(FP8X4),
+                    lhsT_scale=ws[:, t * P : (t + 1) * P],
+                    rhs=mc[:, cols].bitcast(FP8X4),
+                    rhs_scale=ms[:, cols],
+                    start=True,
+                    stop=True,
+                )
+            bank[u] = bk
+
+        db = {}
+
+        def make_da(e):
+            if e % 2 == 0:
+                dt = work.tile([P, 2 * C * PACK], BF16, name="db", align_bytes=64)
+                db[e // 2] = dt
+            c0 = e % 2 * C
+            nc.vector.scalar_tensor_tensor(
+                db[e // 2][:, c0 * PACK : (c0 + C) * PACK].rearrange("p (n t) -> p n t", t=PACK),
+                a_t[e // 2][:, :, c0 : c0 + C].rearrange("p t n -> p n t"),
+                0.0,
+                bank.pop(e)[:].rearrange("p t n -> p n t"),
+                MAX,
+                MULT,
+            )
+
+        def quant_da(pair):
+            dc = held.tile([P, 2 * C], U32, name=f"dc{pair}", align_bytes=64)
+            ds = held.tile([P, 2 * C], U8, name=f"ds{pair}", align_bytes=64)
+            nc.vector.quantize_mx(out=dc[:].bitcast(FP8X4), scales=ds[:], in_=db.pop(pair)[:])
+            da_q[pair] = (dc, ds)
+
+        def store_dx(u):
+            q, quad = divmod(u - E, E // QUAD)
+            if quad == 0:
+                d = held.tile([P, S], F32, name=f"dx{q}", tag="plane", bufs=4)
+                dx[q] = d
+            dst = dx[q][:, quad * QUAD * C : (quad + 1) * QUAD * C]
+            src = bank.pop(u)[:].rearrange("p s c -> p (s c)")
+            nc.scalar.activation(dst, src, COPY, scale=2.0)
+
+        picked = {}
+
+        def first(q):
+            def step():
+                rt = work.tile([P, 2, T], F32, name="picked", tag="g32")
+                nc.vector.tensor_copy(rt[:, 0, :], dx[q][:].indirect(pos1_t[:]))
+                picked[q] = rt
+            return step
+
+        def second(q):
+            def step():
+                nc.vector.tensor_copy(picked[q][:, 1, :], dx[q][:].indirect(pos2_t[:]))
+            return step
+
+        def finish(q):
+            def step():
+                rt = work.tile([P, T], F32, name="res")
+                nc.vector.tensor_tensor(rt[:], picked[q][:, 0, :], picked[q][:, 1, :], ADD)
+                nc.sync.dma_start(out[q * P : (q + 1) * P, :], rt[:])
+            return step
+
+        combine = {16: [first(0)], 17: [second(0)], 18: [finish(0)], 19: [first(1)], 20: [second(1)], 21: [finish(1)], 22: [first(2)], 23: [second(2)], 24: [finish(2)]}
+
+        advance(6)
+        for j in range(PACK):
+            gather(0, j)
+        pack(0)
+        pack_g(0)
+        quant_g(0)
+        quant(0)
+        pack(1)
+        pack(2)
+        for u in range(UNITS + 1):
+            if u < UNITS:
+                advance(2)
+                multiply(u)
+            if u - 1 >= E:
+                store_dx(u - 1)
+            if u + 3 < UNITS:
+                pack(u + 3)
+            if u + 1 < UNITS:
+                quant(u + 1)
+            if u == 0:
+                for j in range(PACK):
+                    gather(1, j)
+                pack_g(1)
+            if u == 1:
+                quant_g(1)
+            if 2 <= u < 2 + PACK:
+                gather(2, u - 2)
+            if u == 1 + PACK:
+                pack_g(2)
+            if u == 2 + PACK:
+                quant_g(2)
+            if 0 < u <= E:
+                make_da(u - 1)
+            if u % 2 == 1 and 3 <= u <= E + 1:
+                quant_da((u - 3) // 2)
+            for step in combine.get(u, ()):
+                step()
+        q = K // P - 1
+        first(q)()
+        st = work.tile([P, T], F32, name="res")
+        for half in range(2):
+            cols = slice(half * T // 2, (half + 1) * T // 2)
+            lst = pos2_t[:, half * T // 32 : (half + 1) * T // 32]
+            nc.vector.tensor_copy(picked[q][:, 1, cols], dx[q][:].indirect(lst))
+            nc.vector.tensor_tensor(st[:, cols], picked[q][:, 0, cols], picked[q][:, 1, cols], ADD)
+            nc.sync.dma_start(out[q * P : (q + 1) * P, cols], st[:, cols])

@@ -24,9 +24,13 @@ PACK = 4
 G_W = 512
 A_W = 256
 GROUPS = S // G_W
-GPSIMD_COLS = 24
 QUAD = 4
+QUARTERS = K // P
+PER_Q = E // QUAD
 UNITS = 2 * E
+RING = 12
+AHEAD = 6
+VECTOR_EXPERTS = 3
 
 
 def tile_moe_bdx_mlp_relu2_kernel(tc, dyT, a, w2, w1, gate, offs, pos1, pos2, out):
@@ -34,96 +38,71 @@ def tile_moe_bdx_mlp_relu2_kernel(tc, dyT, a, w2, w1, gate, offs, pos1, pos2, ou
     with ExitStack() as ctx:
         held = ctx.enter_context(tc.tile_pool(name="held", bufs=1))
         work = ctx.enter_context(tc.tile_pool(name="work", bufs=2))
-        psum = ctx.enter_context(tc.psum_pool(name="psum", bufs=4))
+        psum = ctx.enter_context(tc.psum_pool(name="psum", bufs=8))
 
         offs_t = held.tile([P, S // 16], U16)
         pos1_t = held.tile([P, T // 16], U16)
         pos2_t = held.tile([P, T // 16], U16)
-        gate_t = []
-        g_q = []
-        for g in range(GROUPS):
-            gt = held.tile([P, G_W], F32, name=f"gate{g}")
-            gate_t.append(gt)
-            gc = held.tile([P, G_W], U32, name=f"gc{g}", align_bytes=64)
-            gs = held.tile([P, G_W], U8, name=f"gs{g}", align_bytes=64)
-            g_q.append((gc, gs))
-        dx = {}
+        gate_t = [held.tile([P, G_W], F32, name=f"gate{g}") for g in range(GROUPS)]
+        g_q = [
+            (
+                held.tile([P, G_W], U32, name=f"gc{g}", align_bytes=64),
+                held.tile([P, G_W], U8, name=f"gs{g}", align_bytes=64),
+            )
+            for g in range(GROUPS)
+        ]
+        dy = [work.tile([P, T], F32, name=f"dy{j}", tag="tok", bufs=PACK) for j in range(PACK)]
+        dy_rows = dyT.rearrange("(p j) t -> p j t", j=PACK)
+        a_rows = a.rearrange("(p j) s -> p j s", j=PACK)
 
         nc.sync.dma_start(offs_t[:], offs)
-
-        def load_gate(g):
+        nc.sync.dma_start(gate_t[0][:], gate[0:P, 0:G_W])
+        for j in range(PACK):
+            nc.sync.dma_start(dy[j][:], dy_rows[:, j, :])
+        for g in range(1, GROUPS):
             nc.sync.dma_start(gate_t[g][:], gate[0:P, g * G_W : (g + 1) * G_W])
 
-        load_gate(0)
-        dy_rows = dyT.rearrange("(p j) t -> p j t", j=PACK)
-        dy = []
-        for j in range(PACK):
-            d = held.tile([P, T], F32, name=f"dy{j}", tag="plane", bufs=4)
-            dy.append(d)
-
-        a_rows = a.rearrange("(p j) s -> p j s", j=PACK)
         raw = {}
         a_t = {}
 
-        def load_a(g):
-            at = work.tile([P, PACK, A_W], F32, name="a_t", bufs=6)
-            nc.sync.dma_start(at[:], a_rows[:, :, g * A_W : (g + 1) * A_W])
-            a_t[g] = at
+        def planes(u):
+            return raw[u][:].rearrange("p (j c) -> p j c", j=PACK)
 
-        def load_unit(u):
-            wr = work.tile([P, PACK, H], F32, name="raw", bufs=12)
+        def load(u):
+            raw[u] = held.tile([P, PACK * H], F32, name=f"raw{u}", tag=f"raw{u % RING}", align_bytes=64)
             if u < E:
-                rows = w2[u].rearrange("(p j) i -> p j i", j=PACK)
-                for j in range(0, PACK, 2):
-                    nc.sync.dma_start(wr[:, j : j + 2, :], rows[:, j : j + 2, :])
+                nc.sync.dma_start(raw[u][:], w2[u].rearrange("(p j) i -> p (j i)", j=PACK))
+                if u % 2 == 1:
+                    pair = u // 2
+                    a_t[pair] = held.tile([P, PACK, A_W], F32, name=f"a{pair}")
+                    nc.sync.dma_start(a_t[pair][:], a_rows[:, :, pair * A_W : (pair + 1) * A_W])
+                if u == E - 1:
+                    nc.sync.dma_start(pos1_t[:], pos1)
+                    nc.sync.dma_start(pos2_t[:], pos2)
             else:
-                q, quad = divmod(u - E, E // QUAD)
+                q, quad = divmod(u - E, PER_Q)
                 for s in range(QUAD):
                     rows = w1[quad * QUAD + s].rearrange("(p j) k -> p j k", j=PACK)
-                    nc.sync.dma_start(wr[:, :, s * P : (s + 1) * P], rows[:, :, q * P : (q + 1) * P])
-            raw[u] = wr
+                    nc.sync.dma_start(planes(u)[:, :, s * P : (s + 1) * P], rows[:, :, q * P : (q + 1) * P])
 
-        def load_pos():
-            nc.sync.dma_start(pos1_t[:], pos1)
-            nc.sync.dma_start(pos2_t[:], pos2)
-
-        for j in range(PACK):
-            nc.sync.dma_start(dy[j][:], dy_rows[:, j, :])
-        loads = []
-        for u in range(UNITS):
-            loads.append(lambda u=u: load_unit(u))
-            if u < E and u % 2 == 0:
-                loads.append(lambda u=u: load_a(u // 2))
-            if u in (1, 3):
-                loads.append(lambda u=u: load_gate(u // 2 + 1))
-            if u == 10:
-                loads.append(load_pos)
-
-        def advance(n):
-            for _ in range(n):
-                if loads:
-                    loads.pop(0)()
+        def interleave(dst, src, copy, c0=0, c1=H // 4):
+            copy(
+                dst[:].rearrange("p (c i j) -> p c j i", i=4, j=PACK)[:, c0:c1],
+                src.rearrange("p j (c i) -> p c j i", i=4)[:, c0:c1],
+            )
 
         g32 = {}
         gb = {}
 
         def gather(g, j):
             if j == 0:
-                gt = work.tile([P, PACK, G_W], F32, name="g32", tag="g32")
-                g32[g] = gt
+                g32[g] = work.tile([P, PACK, G_W], F32, name="g32")
             lst = offs_t[:, g * G_W // 16 : (g + 1) * G_W // 16]
             nc.vector.tensor_tensor(g32[g][:, j, :], dy[j][:].indirect(lst), gate_t[g][:], MULT)
 
-        def interleave(dst, src, copy, c0=0, c1=H // 4):
-            copy(
-                dst[:].rearrange("p (c i j) -> p c j i", i=4, j=PACK)[:, c0:c1],
-                src[:].rearrange("p j (c i) -> p c j i", i=4)[:, c0:c1],
-            )
-
         def pack_g(g):
-            gt = work.tile([P, G_W * PACK], BF16, name="gb", bufs=1, align_bytes=64)
-            interleave(gt, g32.pop(g), nc.vector.tensor_copy)
-            gb[g] = gt
+            gb[g] = work.tile([P, G_W * PACK], BF16, name="gb", bufs=1, align_bytes=64)
+            interleave(gb[g], g32.pop(g)[:], nc.vector.tensor_copy)
 
         def quant_g(g):
             nc.vector.quantize_mx(out=g_q[g][0][:].bitcast(FP8X4), scales=g_q[g][1][:], in_=gb.pop(g)[:])
@@ -131,26 +110,23 @@ def tile_moe_bdx_mlp_relu2_kernel(tc, dyT, a, w2, w1, gate, offs, pos1, pos2, ou
         wb = {}
         w_q = {}
 
-        def gpsimd_copy(dst, src):
-            nc.gpsimd.tensor_scalar(dst, src, 1.0, 0.0, MULT, ADD)
-
         def pack(u):
-            while u not in raw:
-                advance(1)
-            wt = work.tile([P, H * PACK], BF16, name="wb", bufs=5, align_bytes=64)
+            wb[u] = work.tile([P, H * PACK], BF16, name="wb", bufs=10, align_bytes=64)
             if u < E:
                 nc.scalar.copy(
-                    wt[:].rearrange("p (t m j) -> p m j t", t=PACK, j=PACK),
-                    raw[u][:].rearrange("p j (m t) -> p m j t", t=PACK),
+                    wb[u][:].rearrange("p (t m j) -> p m j t", t=PACK, j=PACK),
+                    planes(u).rearrange("p j (m t) -> p m j t", t=PACK),
                 )
+            elif (u - E) % PER_Q == PER_Q - 1 and E + PER_Q <= u < UNITS - 1:
+                cut = VECTOR_EXPERTS * P // 4
+                interleave(wb[u], planes(u), nc.vector.tensor_copy, c1=cut)
+                interleave(wb[u], planes(u), nc.scalar.copy, c0=cut)
             else:
-                interleave(wt, raw[u], gpsimd_copy, c1=GPSIMD_COLS)
-                interleave(wt, raw[u], nc.scalar.copy, c0=GPSIMD_COLS)
-            wb[u] = wt
+                interleave(wb[u], planes(u), nc.scalar.copy)
 
         def quant(u):
-            wc = work.tile([P, H], U32, name="wc", bufs=3, align_bytes=64)
-            ws = work.tile([P, H], U8, name="ws", bufs=3, align_bytes=64)
+            wc = work.tile([P, H], U32, name="wc", bufs=4, align_bytes=64)
+            ws = work.tile([P, H], U8, name="ws", bufs=4, align_bytes=64)
             nc.vector.quantize_mx(out=wc[:].bitcast(FP8X4), scales=ws[:], in_=wb.pop(u)[:])
             w_q[u] = (wc, ws)
 
@@ -159,18 +135,17 @@ def tile_moe_bdx_mlp_relu2_kernel(tc, dyT, a, w2, w1, gate, offs, pos1, pos2, ou
 
         def multiply(u):
             wc, ws = w_q.pop(u)
-            bk = psum.tile([P, QUAD, C], F32, name="bank", bufs=6)
+            bank[u] = psum.tile([P, QUAD, C], F32, name="bank")
             for t in range(QUAD):
                 if u < E:
-                    e = u
-                    mc, ms = g_q[e // QUAD]
-                    cols = slice(e % QUAD * C, e % QUAD * C + C)
+                    mc, ms = g_q[u // QUAD]
+                    cols = slice(u % QUAD * C, u % QUAD * C + C)
                 else:
-                    e = (u - E) % (E // QUAD) * QUAD + t
+                    e = (u - E) % PER_Q * QUAD + t
                     mc, ms = da_q[e // 2]
                     cols = slice(e % 2 * C, e % 2 * C + C)
                 nc.tensor.matmul_mx(
-                    out=bk[:, t, :],
+                    out=bank[u][:, t, :],
                     lhsT=wc[:, t * P : (t + 1) * P].bitcast(FP8X4),
                     lhsT_scale=ws[:, t * P : (t + 1) * P],
                     rhs=mc[:, cols].bitcast(FP8X4),
@@ -178,105 +153,68 @@ def tile_moe_bdx_mlp_relu2_kernel(tc, dyT, a, w2, w1, gate, offs, pos1, pos2, ou
                     start=True,
                     stop=True,
                 )
-            bank[u] = bk
 
-        db = {}
-
-        def make_da(e):
-            if e % 2 == 0:
-                dt = work.tile([P, 2 * C * PACK], BF16, name="db", align_bytes=64)
-                db[e // 2] = dt
-            c0 = e % 2 * C
-            nc.vector.scalar_tensor_tensor(
-                db[e // 2][:, c0 * PACK : (c0 + C) * PACK].rearrange("p (n t) -> p n t", t=PACK),
-                a_t[e // 2][:, :, c0 : c0 + C].rearrange("p t n -> p n t"),
-                0.0,
-                bank.pop(e)[:].rearrange("p t n -> p n t"),
-                MAX,
-                MULT,
-            )
-
-        def quant_da(pair):
+        def make_da(pair):
+            db = raw[2 * pair + 2][:].bitcast(BF16)[:, 0 : 2 * C * PACK]
+            for half in range(2):
+                c0 = half * C
+                nc.vector.scalar_tensor_tensor(
+                    db[:, c0 * PACK : (c0 + C) * PACK].rearrange("p (n t) -> p n t", t=PACK),
+                    a_t[pair][:, :, c0 : c0 + C].rearrange("p t n -> p n t"),
+                    0.0,
+                    bank.pop(2 * pair + half)[:].rearrange("p t n -> p n t"),
+                    MAX,
+                    MULT,
+                )
             dc = held.tile([P, 2 * C], U32, name=f"dc{pair}", align_bytes=64)
             ds = held.tile([P, 2 * C], U8, name=f"ds{pair}", align_bytes=64)
-            nc.vector.quantize_mx(out=dc[:].bitcast(FP8X4), scales=ds[:], in_=db.pop(pair)[:])
+            nc.vector.quantize_mx(out=dc[:].bitcast(FP8X4), scales=ds[:], in_=db)
             da_q[pair] = (dc, ds)
 
-        def store_dx(u):
-            q, quad = divmod(u - E, E // QUAD)
-            if quad == 0:
-                d = held.tile([P, S], F32, name=f"dx{q}", tag="plane", bufs=4)
-                dx[q] = d
-            dst = dx[q][:, quad * QUAD * C : (quad + 1) * QUAD * C]
-            src = bank.pop(u)[:].rearrange("p s c -> p (s c)")
-            nc.scalar.activation(dst, src, COPY, scale=2.0)
+        early = held.tile([P, QUARTERS - 1, T], F32)
 
-        picked = {}
+        def combine(q):
+            host = (E + PER_Q * (q + 1)) % RING
+            dx = held.tile([P, S], F32, name=f"dx{q}", tag=f"raw{host}", align_bytes=64)
+            for quad in range(PER_Q):
+                src = bank.pop(E + PER_Q * q + quad)[:].rearrange("p s c -> p (s c)")
+                nc.scalar.activation(dx[:, quad * QUAD * C : (quad + 1) * QUAD * C], src, COPY, scale=2.0)
+            halves = [(slice(h * T // 2, (h + 1) * T // 2), slice(h * T // 32, (h + 1) * T // 32)) for h in range(2)]
+            picked = work.tile([P, T], F32, name="picked", tag="tok", bufs=PACK)
+            for cols, lst in halves:
+                nc.vector.tensor_copy(picked[:, cols], dx[:].indirect(pos1_t[:, lst]))
+            if q < QUARTERS - 1:
+                for cols, lst in halves:
+                    nc.vector.tensor_tensor(early[:, q, cols], dx[:].indirect(pos2_t[:, lst]), picked[:, cols], ADD)
+                if q == QUARTERS - 2:
+                    nc.sync.dma_start(out[0 : (QUARTERS - 1) * P, :].rearrange("(q p) t -> p q t", p=P), early[:])
+            else:
+                last = work.tile([P, T], F32, name="last", tag="tok", bufs=PACK)
+                for cols, lst in halves:
+                    nc.vector.tensor_tensor(last[:, cols], dx[:].indirect(pos2_t[:, lst]), picked[:, cols], ADD)
+                    nc.sync.dma_start(out[q * P : (q + 1) * P, cols], last[:, cols])
 
-        def first(q):
-            def step():
-                rt = work.tile([P, 2, T], F32, name="picked", tag="g32")
-                nc.vector.tensor_copy(rt[:, 0, :], dx[q][:].indirect(pos1_t[:]))
-                picked[q] = rt
-            return step
-
-        def second(q):
-            def step():
-                nc.vector.tensor_copy(picked[q][:, 1, :], dx[q][:].indirect(pos2_t[:]))
-            return step
-
-        def finish(q):
-            def step():
-                rt = work.tile([P, T], F32, name="res")
-                nc.vector.tensor_tensor(rt[:], picked[q][:, 0, :], picked[q][:, 1, :], ADD)
-                nc.sync.dma_start(out[q * P : (q + 1) * P, :], rt[:])
-            return step
-
-        combine = {16: [first(0)], 17: [second(0)], 18: [finish(0)], 19: [first(1)], 20: [second(1)], 21: [finish(1)], 22: [first(2)], 23: [second(2)], 24: [finish(2)]}
-
-        advance(6)
+        for u in range(AHEAD):
+            load(u)
         for j in range(PACK):
             gather(0, j)
-        pack(0)
-        pack_g(0)
-        quant_g(0)
-        quant(0)
-        pack(1)
-        pack(2)
-        for u in range(UNITS + 1):
-            if u < UNITS:
-                advance(2)
-                multiply(u)
-            if u - 1 >= E:
-                store_dx(u - 1)
-            if u + 3 < UNITS:
-                pack(u + 3)
-            if u + 1 < UNITS:
-                quant(u + 1)
-            if u == 0:
-                for j in range(PACK):
-                    gather(1, j)
-                pack_g(1)
-            if u == 1:
-                quant_g(1)
-            if 2 <= u < 2 + PACK:
-                gather(2, u - 2)
-            if u == 1 + PACK:
-                pack_g(2)
-            if u == 2 + PACK:
-                quant_g(2)
-            if 0 < u <= E:
-                make_da(u - 1)
-            if u % 2 == 1 and 3 <= u <= E + 1:
-                quant_da((u - 3) // 2)
-            for step in combine.get(u, ()):
-                step()
-        q = K // P - 1
-        first(q)()
-        st = work.tile([P, T], F32, name="res")
-        for half in range(2):
-            cols = slice(half * T // 2, (half + 1) * T // 2)
-            lst = pos2_t[:, half * T // 32 : (half + 1) * T // 32]
-            nc.vector.tensor_copy(picked[q][:, 1, cols], dx[q][:].indirect(lst))
-            nc.vector.tensor_tensor(st[:, cols], picked[q][:, 0, cols], picked[q][:, 1, cols], ADD)
-            nc.sync.dma_start(out[q * P : (q + 1) * P, cols], st[:, cols])
+        for g in range(1, GROUPS):
+            gather(g, 0)
+            pack_g(g - 1)
+            gather(g, 1)
+            quant_g(g - 1)
+            gather(g, 2)
+            gather(g, 3)
+        pack_g(GROUPS - 1)
+        quant_g(GROUPS - 1)
+        for u in range(UNITS):
+            if u + AHEAD < UNITS:
+                load(u + AHEAD)
+            pack(u)
+            quant(u)
+            multiply(u)
+            if u % 2 == 0 and 2 <= u <= E:
+                make_da(u // 2 - 1)
+            if u > E and (u - E) % PER_Q == 0:
+                combine((u - E) // PER_Q - 1)
+        combine(QUARTERS - 1)

@@ -22,15 +22,15 @@ BYTES = 4 * (N * T + H * S + 2 * E * N * H + S + K * T) + 2 * 128 * (S + 2 * T) 
 P = 128
 PACK = 4
 G_W = 512
-A_W = 256
+A_W = 512
 GROUPS = S // G_W
 QUAD = 4
 QUARTERS = K // P
-PER_Q = E // QUAD
 UNITS = 2 * E
 RING = 12
 AHEAD = 6
-VECTOR_EXPERTS = 3
+WHOLE = E - QUAD
+FIRST_Q = E + WHOLE
 
 
 def tile_moe_bdx_mlp_relu2_kernel(tc, dyT, a, w2, w1, gate, offs, pos1, pos2, out):
@@ -70,20 +70,22 @@ def tile_moe_bdx_mlp_relu2_kernel(tc, dyT, a, w2, w1, gate, offs, pos1, pos2, ou
 
         def load(u):
             raw[u] = held.tile([P, PACK * H], F32, name=f"raw{u}", tag=f"raw{u % RING}", align_bytes=64)
-            if u < E:
-                nc.sync.dma_start(raw[u][:], w2[u].rearrange("(p j) i -> p (j i)", j=PACK))
-                if u % 2 == 1:
-                    pair = u // 2
-                    a_t[pair] = held.tile([P, PACK, A_W], F32, name=f"a{pair}")
-                    nc.sync.dma_start(a_t[pair][:], a_rows[:, :, pair * A_W : (pair + 1) * A_W])
-                if u == E - 1:
-                    nc.sync.dma_start(pos1_t[:], pos1)
-                    nc.sync.dma_start(pos2_t[:], pos2)
+            if u < FIRST_Q:
+                matrix = w2[u] if u < E else w1[u - E]
+                nc.sync.dma_start(raw[u][:], matrix.rearrange("(p j) i -> p (j i)", j=PACK))
             else:
-                q, quad = divmod(u - E, PER_Q)
+                q = u - FIRST_Q
+                dst = raw[u][:].rearrange("p (s j c) -> p s j c", s=QUAD, j=PACK)
                 for s in range(QUAD):
-                    rows = w1[quad * QUAD + s].rearrange("(p j) k -> p j k", j=PACK)
-                    nc.sync.dma_start(planes(u)[:, :, s * P : (s + 1) * P], rows[:, :, q * P : (q + 1) * P])
+                    rows = w1[WHOLE + s].rearrange("(p j) k -> p j k", j=PACK)
+                    nc.sync.dma_start(dst[:, s], rows[:, :, q * P : (q + 1) * P])
+            if u < E and u % 3 == 0 and u > 0:
+                g = u // 3 - 1
+                a_t[g] = held.tile([P, PACK, A_W], F32, name=f"a{g}")
+                nc.sync.dma_start(a_t[g][:], a_rows[:, :, g * A_W : (g + 1) * A_W])
+            if u == E - 1:
+                nc.sync.dma_start(pos1_t[:], pos1)
+                nc.sync.dma_start(pos2_t[:], pos2)
 
         def interleave(dst, src, copy, c0=0, c1=H // 4):
             copy(
@@ -117,12 +119,16 @@ def tile_moe_bdx_mlp_relu2_kernel(tc, dyT, a, w2, w1, gate, offs, pos1, pos2, ou
                     wb[u][:].rearrange("p (t m j) -> p m j t", t=PACK, j=PACK),
                     planes(u).rearrange("p j (m t) -> p m j t", t=PACK),
                 )
-            elif (u - E) % PER_Q == PER_Q - 1 and E + PER_Q <= u < UNITS - 1:
-                cut = VECTOR_EXPERTS * P // 4
-                interleave(wb[u], planes(u), nc.vector.tensor_copy, c1=cut)
-                interleave(wb[u], planes(u), nc.scalar.copy, c0=cut)
-            else:
+            elif u < FIRST_Q:
                 interleave(wb[u], planes(u), nc.scalar.copy)
+            else:
+                dst = wb[u][:].rearrange("p (s c i j) -> p s c j i", s=QUAD, i=4, j=PACK)
+                src = raw[u][:].rearrange("p (s j c i) -> p s c j i", s=QUAD, i=4, j=PACK)
+                if u == FIRST_Q:
+                    nc.scalar.copy(dst[:, 0:2], src[:, 0:2])
+                    nc.vector.tensor_copy(dst[:, 2:4], src[:, 2:4])
+                else:
+                    nc.scalar.copy(dst, src)
 
         def quant(u):
             wc = work.tile([P, H], U32, name="wc", bufs=4, align_bytes=64)
@@ -135,17 +141,23 @@ def tile_moe_bdx_mlp_relu2_kernel(tc, dyT, a, w2, w1, gate, offs, pos1, pos2, ou
 
         def multiply(u):
             wc, ws = w_q.pop(u)
-            bank[u] = psum.tile([P, QUAD, C], F32, name="bank")
+            whole = E <= u < FIRST_Q
+            if not whole:
+                bank[u] = psum.tile([P, QUAD, C], F32, name="bank")
+            elif u % 2 == 0:
+                bank[u] = psum.tile([P, QUAD, C], F32, name="bank")
+                bank[u + 1] = psum.tile([P, QUAD, C], F32, name="bank")
             for t in range(QUAD):
                 if u < E:
                     mc, ms = g_q[u // QUAD]
                     cols = slice(u % QUAD * C, u % QUAD * C + C)
                 else:
-                    e = (u - E) % PER_Q * QUAD + t
+                    e = u - E if whole else WHOLE + t
                     mc, ms = da_q[e // 2]
                     cols = slice(e % 2 * C, e % 2 * C + C)
+                dst = bank[u - u % 2 + t // 2][:, t % 2 * 2 + u % 2, :] if whole else bank[u][:, t, :]
                 nc.tensor.matmul_mx(
-                    out=bank[u][:, t, :],
+                    out=dst,
                     lhsT=wc[:, t * P : (t + 1) * P].bitcast(FP8X4),
                     lhsT_scale=ws[:, t * P : (t + 1) * P],
                     rhs=mc[:, cols].bitcast(FP8X4),
@@ -158,9 +170,10 @@ def tile_moe_bdx_mlp_relu2_kernel(tc, dyT, a, w2, w1, gate, offs, pos1, pos2, ou
             db = raw[2 * pair + 2][:].bitcast(BF16)[:, 0 : 2 * C * PACK]
             for half in range(2):
                 c0 = half * C
+                a0 = pair % 2 * 2 * C + c0
                 nc.vector.scalar_tensor_tensor(
                     db[:, c0 * PACK : (c0 + C) * PACK].rearrange("p (n t) -> p n t", t=PACK),
-                    a_t[pair][:, :, c0 : c0 + C].rearrange("p t n -> p n t"),
+                    a_t[pair // 2][:, :, a0 : a0 + C].rearrange("p t n -> p n t"),
                     0.0,
                     bank.pop(2 * pair + half)[:].rearrange("p t n -> p n t"),
                     MAX,
@@ -173,12 +186,23 @@ def tile_moe_bdx_mlp_relu2_kernel(tc, dyT, a, w2, w1, gate, offs, pos1, pos2, ou
 
         early = held.tile([P, QUARTERS - 1, T], F32)
 
+        dxs = {}
+
+        def read_pair(u):
+            c0 = (u - E) * C
+            for q in range(QUARTERS):
+                src = bank[u + q // 2][:].rearrange("p s c -> p (s c)")[:, q % 2 * 2 * C : (q % 2 + 1) * 2 * C]
+                nc.vector.tensor_scalar_mul(dxs[q][:, c0 : c0 + 2 * C], src, 2.0)
+
+        def read_quarter(q):
+            src = bank[FIRST_Q + q][:].rearrange("p s c -> p (s c)")
+            if q == 0:
+                nc.vector.tensor_scalar_mul(dxs[q][:, WHOLE * C :], src, 2.0)
+            else:
+                nc.scalar.activation(dxs[q][:, WHOLE * C :], src, COPY, scale=2.0)
+
         def combine(q):
-            host = (E + PER_Q * (q + 1)) % RING
-            dx = held.tile([P, S], F32, name=f"dx{q}", tag=f"raw{host}", align_bytes=64)
-            for quad in range(PER_Q):
-                src = bank.pop(E + PER_Q * q + quad)[:].rearrange("p s c -> p (s c)")
-                nc.scalar.activation(dx[:, quad * QUAD * C : (quad + 1) * QUAD * C], src, COPY, scale=2.0)
+            dx = dxs[q]
             halves = [(slice(h * T // 2, (h + 1) * T // 2), slice(h * T // 32, (h + 1) * T // 32)) for h in range(2)]
             picked = work.tile([P, T], F32, name="picked", tag="tok", bufs=PACK)
             for cols, lst in halves:
@@ -215,6 +239,14 @@ def tile_moe_bdx_mlp_relu2_kernel(tc, dyT, a, w2, w1, gate, offs, pos1, pos2, ou
             multiply(u)
             if u % 2 == 0 and 2 <= u <= E:
                 make_da(u // 2 - 1)
-            if u > E and (u - E) % PER_Q == 0:
-                combine((u - E) // PER_Q - 1)
+            if u == E:
+                for q in range(2):
+                    dxs[q] = work.tile([P, S], F32, name=f"dx{q}", tag="g32")
+                    dxs[q + 2] = held.tile([P, S], F32, name=f"dx{q + 2}", tag=f"a{q}")
+            if E + 2 <= u <= FIRST_Q and u % 2 == 0:
+                read_pair(u - 2)
+            if u > FIRST_Q:
+                read_quarter(u - FIRST_Q - 1)
+                combine(u - FIRST_Q - 1)
+        read_quarter(QUARTERS - 1)
         combine(QUARTERS - 1)

@@ -1,6 +1,7 @@
 from contextlib import ExitStack
 
 import concourse.mybir as mybir
+from concourse.masks import make_identity
 
 K, T, E, C, H, N = 512, 768, 12, 128, 512, 512
 S = E * C
@@ -31,6 +32,7 @@ RING = 12
 AHEAD = 6
 WHOLE = E - QUAD
 FIRST_Q = E + WHOLE
+A_BEHIND = (3, 7, 11)
 
 
 def tile_moe_bdx_mlp_relu2_kernel(tc, dyT, a, w2, w1, gate, offs, pos1, pos2, out):
@@ -56,11 +58,18 @@ def tile_moe_bdx_mlp_relu2_kernel(tc, dyT, a, w2, w1, gate, offs, pos1, pos2, ou
         a_rows = a.rearrange("(p j) s -> p j s", j=PACK)
 
         nc.sync.dma_start(offs_t[:], offs)
-        nc.sync.dma_start(gate_t[0][:], gate[0:P, 0:G_W])
+        gate_cols = held.tile([P, GROUPS, PACK], F32)
+        nc.sync.dma_start(gate_cols[:], gate[0, :].rearrange("(g k c) -> k g c", g=GROUPS, c=PACK))
         for j in range(PACK):
             nc.sync.dma_start(dy[j][:], dy_rows[:, j, :])
-        for g in range(1, GROUPS):
-            nc.sync.dma_start(gate_t[g][:], gate[0:P, g * G_W : (g + 1) * G_W])
+        identity = held.tile([P, P], F32)
+        make_identity(nc, identity[:])
+        for g in range(GROUPS):
+            spread = psum.tile([P, PACK, P], F32, name="bank")
+            for c in range(PACK):
+                nc.tensor.transpose(spread[:, c, :], gate_cols[:, g, c : c + 1].to_broadcast([P, P]), identity[:])
+            copy = nc.vector.tensor_copy if g < GROUPS - 1 else nc.scalar.copy
+            copy(gate_t[g][:].rearrange("p (k c) -> p k c", c=PACK), spread[:].rearrange("p c k -> p k c"))
 
         raw = {}
         a_t = {}
@@ -79,8 +88,8 @@ def tile_moe_bdx_mlp_relu2_kernel(tc, dyT, a, w2, w1, gate, offs, pos1, pos2, ou
                 for s in range(QUAD):
                     rows = w1[WHOLE + s].rearrange("(p j) k -> p j k", j=PACK)
                     nc.sync.dma_start(dst[:, s], rows[:, :, q * P : (q + 1) * P])
-            if u < E and u % 3 == 0 and u > 0:
-                g = u // 3 - 1
+            if u in A_BEHIND:
+                g = A_BEHIND.index(u)
                 a_t[g] = held.tile([P, PACK, A_W], F32, name=f"a{g}")
                 nc.sync.dma_start(a_t[g][:], a_rows[:, :, g * A_W : (g + 1) * A_W])
             if u == E - 1:
@@ -124,11 +133,9 @@ def tile_moe_bdx_mlp_relu2_kernel(tc, dyT, a, w2, w1, gate, offs, pos1, pos2, ou
             else:
                 dst = wb[u][:].rearrange("p (s c i j) -> p s c j i", s=QUAD, i=4, j=PACK)
                 src = raw[u][:].rearrange("p (s j c i) -> p s c j i", s=QUAD, i=4, j=PACK)
-                if u == FIRST_Q:
-                    nc.scalar.copy(dst[:, 0:2], src[:, 0:2])
-                    nc.vector.tensor_copy(dst[:, 2:4], src[:, 2:4])
-                else:
-                    nc.scalar.copy(dst, src)
+                copy = nc.vector.tensor_copy if u == FIRST_Q else nc.scalar.copy
+                copy(dst[:, 0:2], src[:, 0:2])
+                copy(dst[:, 2:4], src[:, 2:4])
 
         def quant(u):
             wc = work.tile([P, H], U32, name="wc", bufs=4, align_bytes=64)
@@ -188,22 +195,48 @@ def tile_moe_bdx_mlp_relu2_kernel(tc, dyT, a, w2, w1, gate, offs, pos1, pos2, ou
 
         dxs = {}
 
-        def read_pair(u):
+        def read_pair(u, quarters=range(QUARTERS)):
             c0 = (u - E) * C
-            for q in range(QUARTERS):
+            for q in quarters:
                 src = bank[u + q // 2][:].rearrange("p s c -> p (s c)")[:, q % 2 * 2 * C : (q % 2 + 1) * 2 * C]
-                nc.vector.tensor_scalar_mul(dxs[q][:, c0 : c0 + 2 * C], src, 2.0)
+                if u == FIRST_Q - 2 and q > 0:
+                    nc.scalar.activation(dxs[q][:, c0 : c0 + 2 * C], src, COPY, scale=2.0)
+                else:
+                    nc.vector.tensor_scalar_mul(dxs[q][:, c0 : c0 + 2 * C], src, 2.0)
 
         def read_quarter(q):
             src = bank[FIRST_Q + q][:].rearrange("p s c -> p (s c)")
-            if q == 0:
-                nc.vector.tensor_scalar_mul(dxs[q][:, WHOLE * C :], src, 2.0)
-            else:
-                nc.scalar.activation(dxs[q][:, WHOLE * C :], src, COPY, scale=2.0)
+            nc.scalar.activation(dxs[q][:, WHOLE * C :], src, COPY, scale=2.0)
+
+        def first_quarter():
+            for pair in range(WHOLE // 2, E // 2):
+                c0 = (2 * pair - WHOLE) * P
+                wc = work.tile([P, 2 * P], U32, name="wc", bufs=4, align_bytes=64)
+                ws = work.tile([P, 2 * P], U8, name="ws", bufs=4, align_bytes=64)
+                src = wb[FIRST_Q][:, c0 * PACK : (c0 + 2 * P) * PACK]
+                nc.vector.quantize_mx(out=wc[:].bitcast(FP8X4), scales=ws[:], in_=src)
+                if pair == WHOLE // 2:
+                    read_pair(FIRST_Q - 2, (0,))
+                sums = psum.tile([P, 2, C], F32, name="bank")
+                mc, ms = da_q[pair]
+                for t in range(2):
+                    cols = slice(t * P, (t + 1) * P)
+                    nc.tensor.matmul_mx(
+                        out=sums[:, t, :],
+                        lhsT=wc[:, cols].bitcast(FP8X4),
+                        lhsT_scale=ws[:, cols],
+                        rhs=mc[:, cols].bitcast(FP8X4),
+                        rhs_scale=ms[:, cols],
+                        start=True,
+                        stop=True,
+                    )
+                dst = dxs[0][:, 2 * pair * C : (2 * pair + 2) * C]
+                nc.vector.tensor_scalar_mul(dst, sums[:].rearrange("p s c -> p (s c)"), 2.0)
 
         def combine(q):
             dx = dxs[q]
-            halves = [(slice(h * T // 2, (h + 1) * T // 2), slice(h * T // 32, (h + 1) * T // 32)) for h in range(2)]
+            cut = T // 2 if q < QUARTERS - 1 else 3 * T // 4
+            halves = [(slice(a0, a1), slice(a0 // 16, a1 // 16)) for a0, a1 in ((0, cut), (cut, T))]
             picked = work.tile([P, T], F32, name="picked", tag="tok", bufs=PACK)
             for cols, lst in halves:
                 nc.vector.tensor_copy(picked[:, cols], dx[:].indirect(pos1_t[:, lst]))
@@ -235,6 +268,11 @@ def tile_moe_bdx_mlp_relu2_kernel(tc, dyT, a, w2, w1, gate, offs, pos1, pos2, ou
             if u + AHEAD < UNITS:
                 load(u + AHEAD)
             pack(u)
+            if u == FIRST_Q:
+                first_quarter()
+                continue
+            if u == FIRST_Q + 1:
+                read_pair(FIRST_Q - 2, (1, 2, 3))
             quant(u)
             multiply(u)
             if u % 2 == 0 and 2 <= u <= E:
@@ -243,10 +281,11 @@ def tile_moe_bdx_mlp_relu2_kernel(tc, dyT, a, w2, w1, gate, offs, pos1, pos2, ou
                 for q in range(2):
                     dxs[q] = work.tile([P, S], F32, name=f"dx{q}", tag="g32")
                     dxs[q + 2] = held.tile([P, S], F32, name=f"dx{q + 2}", tag=f"a{q}")
-            if E + 2 <= u <= FIRST_Q and u % 2 == 0:
+            if E + 2 <= u < FIRST_Q and u % 2 == 0:
                 read_pair(u - 2)
             if u > FIRST_Q:
-                read_quarter(u - FIRST_Q - 1)
+                if u > FIRST_Q + 1:
+                    read_quarter(u - FIRST_Q - 1)
                 combine(u - FIRST_Q - 1)
         read_quarter(QUARTERS - 1)
         combine(QUARTERS - 1)

@@ -33,6 +33,7 @@ AHEAD = 6
 WHOLE = E - QUAD
 FIRST_Q = E + WHOLE
 A_BEHIND = (3, 7, 11)
+ORDER = [*range(0, 8), *range(12, 16), *range(8, 12), *range(16, 24)]
 
 
 def tile_moe_bdx_mlp_relu2_kernel(tc, dyT, a, w2, w1, gate, offs, pos1, pos2, out):
@@ -62,14 +63,13 @@ def tile_moe_bdx_mlp_relu2_kernel(tc, dyT, a, w2, w1, gate, offs, pos1, pos2, ou
         nc.sync.dma_start(gate_cols[:], gate[0, :].rearrange("(g k c) -> k g c", g=GROUPS, c=PACK))
         for j in range(PACK):
             nc.sync.dma_start(dy[j][:], dy_rows[:, j, :])
-        identity = held.tile([P, P], F32)
+        identity = held.tile([P, P], F32, tag="first", align_bytes=64)
         make_identity(nc, identity[:])
         for g in range(GROUPS):
             spread = psum.tile([P, PACK, P], F32, name="bank")
             for c in range(PACK):
                 nc.tensor.transpose(spread[:, c, :], gate_cols[:, g, c : c + 1].to_broadcast([P, P]), identity[:])
-            copy = nc.vector.tensor_copy if g < GROUPS - 1 else nc.scalar.copy
-            copy(gate_t[g][:].rearrange("p (k c) -> p k c", c=PACK), spread[:].rearrange("p c k -> p k c"))
+            nc.scalar.copy(gate_t[g][:].rearrange("p (k c) -> p k c", c=PACK), spread[:].rearrange("p c k -> p k c"))
 
         raw = {}
         a_t = {}
@@ -78,7 +78,7 @@ def tile_moe_bdx_mlp_relu2_kernel(tc, dyT, a, w2, w1, gate, offs, pos1, pos2, ou
             return raw[u][:].rearrange("p (j c) -> p j c", j=PACK)
 
         def load(u):
-            raw[u] = held.tile([P, PACK * H], F32, name=f"raw{u}", tag=f"raw{u % RING}", align_bytes=64)
+            raw[u] = held.tile([P, PACK * H], F32, name=f"raw{u}", tag=f"raw{ORDER.index(u) % RING}", align_bytes=64)
             if u < FIRST_Q:
                 matrix = w2[u] if u < E else w1[u - E]
                 nc.sync.dma_start(raw[u][:], matrix.rearrange("(p j) i -> p (j i)", j=PACK))
@@ -122,7 +122,10 @@ def tile_moe_bdx_mlp_relu2_kernel(tc, dyT, a, w2, w1, gate, offs, pos1, pos2, ou
         w_q = {}
 
         def pack(u):
-            wb[u] = work.tile([P, H * PACK], BF16, name="wb", bufs=10, align_bytes=64)
+            if u == 0:
+                wb[u] = held.tile([P, H * PACK], BF16, name="wb0", tag="first", align_bytes=64)
+            else:
+                wb[u] = work.tile([P, H * PACK], BF16, name="wb", bufs=10, align_bytes=64)
             if u < E:
                 nc.scalar.copy(
                     wb[u][:].rearrange("p (t m j) -> p m j t", t=PACK, j=PACK),
@@ -133,18 +136,23 @@ def tile_moe_bdx_mlp_relu2_kernel(tc, dyT, a, w2, w1, gate, offs, pos1, pos2, ou
             else:
                 dst = wb[u][:].rearrange("p (s c i j) -> p s c j i", s=QUAD, i=4, j=PACK)
                 src = raw[u][:].rearrange("p (s j c i) -> p s c j i", s=QUAD, i=4, j=PACK)
-                copy = nc.vector.tensor_copy if u == FIRST_Q else nc.scalar.copy
-                copy(dst[:, 0:2], src[:, 0:2])
-                copy(dst[:, 2:4], src[:, 2:4])
+                if u == FIRST_Q:
+                    nc.vector.tensor_copy(dst[:, 0:2], src[:, 0:2])
+                    nc.vector.tensor_copy(dst[:, 2], src[:, 2])
+                    nc.vector.tensor_copy(dst[:, 3], src[:, 3])
+                else:
+                    nc.scalar.copy(dst[:, 0:2], src[:, 0:2])
+                    nc.scalar.copy(dst[:, 2:4], src[:, 2:4])
 
         def quant(u):
             wc = work.tile([P, H], U32, name="wc", bufs=4, align_bytes=64)
             ws = work.tile([P, H], U8, name="ws", bufs=4, align_bytes=64)
-            nc.vector.quantize_mx(out=wc[:].bitcast(FP8X4), scales=ws[:], in_=wb.pop(u)[:])
+            nc.vector.quantize_mx(out=wc[:].bitcast(FP8X4), scales=ws[:], in_=wb[u][:])
             w_q[u] = (wc, ws)
 
         bank = {}
         da_q = {}
+        staged = {}
 
         def multiply(u):
             wc, ws = w_q.pop(u)
@@ -174,7 +182,7 @@ def tile_moe_bdx_mlp_relu2_kernel(tc, dyT, a, w2, w1, gate, offs, pos1, pos2, ou
                 )
 
         def make_da(pair):
-            db = raw[2 * pair + 2][:].bitcast(BF16)[:, 0 : 2 * C * PACK]
+            db = raw[ORDER[ORDER.index(2 * pair + 1) + 1]][:].bitcast(BF16)[:, 0 : 2 * C * PACK]
             for half in range(2):
                 c0 = half * C
                 a0 = pair % 2 * 2 * C + c0
@@ -186,12 +194,14 @@ def tile_moe_bdx_mlp_relu2_kernel(tc, dyT, a, w2, w1, gate, offs, pos1, pos2, ou
                     MAX,
                     MULT,
                 )
+            staged[pair] = db
+
+        def quant_da(pair):
+            db = staged.pop(pair)
             dc = held.tile([P, 2 * C], U32, name=f"dc{pair}", align_bytes=64)
             ds = held.tile([P, 2 * C], U8, name=f"ds{pair}", align_bytes=64)
             nc.vector.quantize_mx(out=dc[:].bitcast(FP8X4), scales=ds[:], in_=db)
             da_q[pair] = (dc, ds)
-
-        early = held.tile([P, QUARTERS - 1, T], F32)
 
         dxs = {}
 
@@ -209,20 +219,18 @@ def tile_moe_bdx_mlp_relu2_kernel(tc, dyT, a, w2, w1, gate, offs, pos1, pos2, ou
             nc.scalar.activation(dxs[q][:, WHOLE * C :], src, COPY, scale=2.0)
 
         def first_quarter():
+            bank[FIRST_Q] = psum.tile([P, QUAD, C], F32, name="bank")
             for pair in range(WHOLE // 2, E // 2):
-                c0 = (2 * pair - WHOLE) * P
+                s0 = 2 * pair - WHOLE
                 wc = work.tile([P, 2 * P], U32, name="wc", bufs=4, align_bytes=64)
                 ws = work.tile([P, 2 * P], U8, name="ws", bufs=4, align_bytes=64)
-                src = wb[FIRST_Q][:, c0 * PACK : (c0 + 2 * P) * PACK]
+                src = wb[FIRST_Q][:, s0 * P * PACK : (s0 + 2) * P * PACK]
                 nc.vector.quantize_mx(out=wc[:].bitcast(FP8X4), scales=ws[:], in_=src)
-                if pair == WHOLE // 2:
-                    read_pair(FIRST_Q - 2, (0,))
-                sums = psum.tile([P, 2, C], F32, name="bank")
                 mc, ms = da_q[pair]
                 for t in range(2):
                     cols = slice(t * P, (t + 1) * P)
                     nc.tensor.matmul_mx(
-                        out=sums[:, t, :],
+                        out=bank[FIRST_Q][:, s0 + t, :],
                         lhsT=wc[:, cols].bitcast(FP8X4),
                         lhsT_scale=ws[:, cols],
                         rhs=mc[:, cols].bitcast(FP8X4),
@@ -230,8 +238,6 @@ def tile_moe_bdx_mlp_relu2_kernel(tc, dyT, a, w2, w1, gate, offs, pos1, pos2, ou
                         start=True,
                         stop=True,
                     )
-                dst = dxs[0][:, 2 * pair * C : (2 * pair + 2) * C]
-                nc.vector.tensor_scalar_mul(dst, sums[:].rearrange("p s c -> p (s c)"), 2.0)
 
         def combine(q):
             dx = dxs[q]
@@ -241,17 +247,17 @@ def tile_moe_bdx_mlp_relu2_kernel(tc, dyT, a, w2, w1, gate, offs, pos1, pos2, ou
             for cols, lst in halves:
                 nc.vector.tensor_copy(picked[:, cols], dx[:].indirect(pos1_t[:, lst]))
             if q < QUARTERS - 1:
+                res = wb[FIRST_Q + q + 1][:].bitcast(F32)
                 for cols, lst in halves:
-                    nc.vector.tensor_tensor(early[:, q, cols], dx[:].indirect(pos2_t[:, lst]), picked[:, cols], ADD)
-                if q == QUARTERS - 2:
-                    nc.sync.dma_start(out[0 : (QUARTERS - 1) * P, :].rearrange("(q p) t -> p q t", p=P), early[:])
+                    nc.vector.tensor_tensor(res[:, cols], dx[:].indirect(pos2_t[:, lst]), picked[:, cols], ADD)
+                nc.sync.dma_start(out[q * P : (q + 1) * P, :], res[:, 0:T])
             else:
                 last = work.tile([P, T], F32, name="last", tag="tok", bufs=PACK)
                 for cols, lst in halves:
                     nc.vector.tensor_tensor(last[:, cols], dx[:].indirect(pos2_t[:, lst]), picked[:, cols], ADD)
                     nc.sync.dma_start(out[q * P : (q + 1) * P, cols], last[:, cols])
 
-        for u in range(AHEAD):
+        for u in ORDER[:AHEAD]:
             load(u)
         for j in range(PACK):
             gather(0, j)
@@ -264,28 +270,36 @@ def tile_moe_bdx_mlp_relu2_kernel(tc, dyT, a, w2, w1, gate, offs, pos1, pos2, ou
             gather(g, 3)
         pack_g(GROUPS - 1)
         quant_g(GROUPS - 1)
-        for u in range(UNITS):
-            if u + AHEAD < UNITS:
-                load(u + AHEAD)
-            pack(u)
+        for step, u in enumerate(ORDER):
+            if step + AHEAD < UNITS:
+                load(ORDER[step + AHEAD])
+            before = ORDER[step - 1]
             if u == FIRST_Q:
-                first_quarter()
+                src = bank[u][:].rearrange("p s c -> p (s c)")
+                nc.vector.tensor_scalar_mul(dxs[0][:, WHOLE * C :], src, 2.0)
+                read_pair(FIRST_Q - 2, (0,))
                 continue
+            if u > FIRST_Q + 1:
+                read_quarter(u - FIRST_Q - 1)
+            pack(u)
+            if u == FIRST_Q - 1:
+                pack(FIRST_Q)
+                first_quarter()
             if u == FIRST_Q + 1:
                 read_pair(FIRST_Q - 2, (1, 2, 3))
             quant(u)
+            for pair in list(staged):
+                quant_da(pair)
             multiply(u)
-            if u % 2 == 0 and 2 <= u <= E:
-                make_da(u // 2 - 1)
+            if before < E and before % 2 == 1:
+                make_da(before // 2)
             if u == E:
                 for q in range(2):
                     dxs[q] = work.tile([P, S], F32, name=f"dx{q}", tag="g32")
                     dxs[q + 2] = held.tile([P, S], F32, name=f"dx{q + 2}", tag=f"a{q}")
-            if E + 2 <= u < FIRST_Q and u % 2 == 0:
-                read_pair(u - 2)
+            if E <= before < FIRST_Q - 2 and before % 2 == 1:
+                read_pair(before - 1)
             if u > FIRST_Q:
-                if u > FIRST_Q + 1:
-                    read_quarter(u - FIRST_Q - 1)
                 combine(u - FIRST_Q - 1)
         read_quarter(QUARTERS - 1)
         combine(QUARTERS - 1)

@@ -22,18 +22,23 @@ BYTES = 4 * (N * T + H * S + 2 * E * N * H + S + K * T) + 2 * 128 * (S + 2 * T) 
 
 P = 128
 PACK = 4
-G_W = 512
-A_W = 512
-GROUPS = S // G_W
+LINE = 4
+STRIPE = 16
 QUAD = 4
+GROUP = QUAD * C
+GROUPS = S // GROUP
 QUARTERS = K // P
+
 UNITS = 2 * E
-RING = 12
-AHEAD = 6
 WHOLE = E - QUAD
 FIRST_Q = E + WHOLE
-A_BEHIND = (3, 7, 11)
-ORDER = [*range(0, 8), *range(12, 16), *range(8, 12), *range(16, 24)]
+LAST_PAIR = FIRST_Q - 2
+ORDER = [*range(0, 2 * QUAD), *range(E, E + QUAD), *range(2 * QUAD, E), *range(E + QUAD, UNITS)]
+RING = 12
+AHEAD = RING // 2
+PACKED_BUFS = 10
+CODE_BUFS = 4
+LAST_CUT = 3 * T // 4
 
 
 def tile_moe_bdx_mlp_relu2_kernel(tc, dyT, a, w2, w1, gate, offs, pos1, pos2, out):
@@ -43,14 +48,14 @@ def tile_moe_bdx_mlp_relu2_kernel(tc, dyT, a, w2, w1, gate, offs, pos1, pos2, ou
         work = ctx.enter_context(tc.tile_pool(name="work", bufs=2))
         psum = ctx.enter_context(tc.psum_pool(name="psum", bufs=8))
 
-        offs_t = held.tile([P, S // 16], U16)
-        pos1_t = held.tile([P, T // 16], U16)
-        pos2_t = held.tile([P, T // 16], U16)
-        gate_t = [held.tile([P, G_W], F32, name=f"gate{g}") for g in range(GROUPS)]
+        offs_t = held.tile([P, S // STRIPE], U16)
+        pos1_t = held.tile([P, T // STRIPE], U16)
+        pos2_t = held.tile([P, T // STRIPE], U16)
+        gate_t = [held.tile([P, GROUP], F32, name=f"gate{g}") for g in range(GROUPS)]
         g_q = [
             (
-                held.tile([P, G_W], U32, name=f"gc{g}", align_bytes=64),
-                held.tile([P, G_W], U8, name=f"gs{g}", align_bytes=64),
+                held.tile([P, GROUP], U32, name=f"gc{g}", align_bytes=64),
+                held.tile([P, GROUP], U8, name=f"gs{g}", align_bytes=64),
             )
             for g in range(GROUPS)
         ]
@@ -59,23 +64,20 @@ def tile_moe_bdx_mlp_relu2_kernel(tc, dyT, a, w2, w1, gate, offs, pos1, pos2, ou
         a_rows = a.rearrange("(p j) s -> p j s", j=PACK)
 
         nc.sync.dma_start(offs_t[:], offs)
-        gate_cols = held.tile([P, GROUPS, PACK], F32)
-        nc.sync.dma_start(gate_cols[:], gate[0, :].rearrange("(g k c) -> k g c", g=GROUPS, c=PACK))
+        gate_cols = held.tile([P, GROUPS, QUAD], F32)
+        nc.sync.dma_start(gate_cols[:], gate[0, :].rearrange("(g r c) -> r g c", g=GROUPS, c=QUAD))
         for j in range(PACK):
             nc.sync.dma_start(dy[j][:], dy_rows[:, j, :])
         identity = held.tile([P, P], F32, tag="first", align_bytes=64)
         make_identity(nc, identity[:])
         for g in range(GROUPS):
-            spread = psum.tile([P, PACK, P], F32, name="bank")
-            for c in range(PACK):
+            spread = psum.tile([P, QUAD, P], F32, name="bank")
+            for c in range(QUAD):
                 nc.tensor.transpose(spread[:, c, :], gate_cols[:, g, c : c + 1].to_broadcast([P, P]), identity[:])
-            nc.scalar.copy(gate_t[g][:].rearrange("p (k c) -> p k c", c=PACK), spread[:].rearrange("p c k -> p k c"))
+            nc.scalar.copy(gate_t[g][:].rearrange("p (r c) -> p r c", c=QUAD), spread[:].rearrange("p c r -> p r c"))
 
         raw = {}
         a_t = {}
-
-        def planes(u):
-            return raw[u][:].rearrange("p (j c) -> p j c", j=PACK)
 
         def load(u):
             raw[u] = held.tile([P, PACK * H], F32, name=f"raw{u}", tag=f"raw{ORDER.index(u) % RING}", align_bytes=64)
@@ -84,222 +86,219 @@ def tile_moe_bdx_mlp_relu2_kernel(tc, dyT, a, w2, w1, gate, offs, pos1, pos2, ou
                 nc.sync.dma_start(raw[u][:], matrix.rearrange("(p j) i -> p (j i)", j=PACK))
             else:
                 q = u - FIRST_Q
-                dst = raw[u][:].rearrange("p (s j c) -> p s j c", s=QUAD, j=PACK)
+                slabs = raw[u][:].rearrange("p (s j c) -> p s j c", s=QUAD, j=PACK)
                 for s in range(QUAD):
                     rows = w1[WHOLE + s].rearrange("(p j) k -> p j k", j=PACK)
-                    nc.sync.dma_start(dst[:, s], rows[:, :, q * P : (q + 1) * P])
-            if u in A_BEHIND:
-                g = A_BEHIND.index(u)
-                a_t[g] = held.tile([P, PACK, A_W], F32, name=f"a{g}")
-                nc.sync.dma_start(a_t[g][:], a_rows[:, :, g * A_W : (g + 1) * A_W])
+                    nc.sync.dma_start(slabs[:, s], rows[:, :, q * P : (q + 1) * P])
+            if u < E and u % QUAD == QUAD - 1:
+                g = u // QUAD
+                a_t[g] = held.tile([P, PACK, GROUP], F32, name=f"a{g}")
+                nc.sync.dma_start(a_t[g][:], a_rows[:, :, g * GROUP : (g + 1) * GROUP])
             if u == E - 1:
                 nc.sync.dma_start(pos1_t[:], pos1)
                 nc.sync.dma_start(pos2_t[:], pos2)
 
-        def interleave(dst, src, copy, c0=0, c1=H // 4):
+        def interleave(copy, dst, planes):
             copy(
-                dst[:].rearrange("p (c i j) -> p c j i", i=4, j=PACK)[:, c0:c1],
-                src.rearrange("p j (c i) -> p c j i", i=4)[:, c0:c1],
+                dst[:].rearrange("p (c i j) -> p c j i", i=LINE, j=PACK),
+                planes.rearrange("p j (c i) -> p c j i", i=LINE),
+            )
+
+        def quantise(src, columns):
+            codes = work.tile([P, columns], U32, name="wc", bufs=CODE_BUFS, align_bytes=64)
+            scales = work.tile([P, columns], U8, name="ws", bufs=CODE_BUFS, align_bytes=64)
+            nc.vector.quantize_mx(out=codes[:].bitcast(FP8X4), scales=scales[:], in_=src)
+            return codes, scales
+
+        def one_pass(dst, weights, t, moving, place):
+            rows = slice(t * P, (t + 1) * P)
+            cols = slice(place * C, (place + 1) * C)
+            nc.tensor.matmul_mx(
+                out=dst,
+                lhsT=weights[0][:, rows].bitcast(FP8X4),
+                lhsT_scale=weights[1][:, rows],
+                rhs=moving[0][:, cols].bitcast(FP8X4),
+                rhs_scale=moving[1][:, cols],
+                start=True,
+                stop=True,
             )
 
         g32 = {}
         gb = {}
 
-        def gather(g, j):
+        def gather_g(g, j):
             if j == 0:
-                g32[g] = work.tile([P, PACK, G_W], F32, name="g32")
-            lst = offs_t[:, g * G_W // 16 : (g + 1) * G_W // 16]
-            nc.vector.tensor_tensor(g32[g][:, j, :], dy[j][:].indirect(lst), gate_t[g][:], MULT)
+                g32[g] = work.tile([P, PACK, GROUP], F32, name="g32")
+            entries = offs_t[:, g * GROUP // STRIPE : (g + 1) * GROUP // STRIPE]
+            nc.vector.tensor_tensor(g32[g][:, j, :], dy[j][:].indirect(entries), gate_t[g][:], MULT)
 
         def pack_g(g):
-            gb[g] = work.tile([P, G_W * PACK], BF16, name="gb", bufs=1, align_bytes=64)
-            interleave(gb[g], g32.pop(g)[:], nc.vector.tensor_copy)
+            gb[g] = work.tile([P, GROUP * PACK], BF16, name="gb", bufs=1, align_bytes=64)
+            interleave(nc.vector.tensor_copy, gb[g], g32[g][:])
 
-        def quant_g(g):
-            nc.vector.quantize_mx(out=g_q[g][0][:].bitcast(FP8X4), scales=g_q[g][1][:], in_=gb.pop(g)[:])
+        def quantise_g(g):
+            nc.vector.quantize_mx(out=g_q[g][0][:].bitcast(FP8X4), scales=g_q[g][1][:], in_=gb[g][:])
 
-        wb = {}
-        w_q = {}
+        packed = {}
 
-        def pack(u):
+        def packed_tile(u):
             if u == 0:
-                wb[u] = held.tile([P, H * PACK], BF16, name="wb0", tag="first", align_bytes=64)
+                packed[u] = held.tile([P, H * PACK], BF16, name="wb0", tag="first", align_bytes=64)
             else:
-                wb[u] = work.tile([P, H * PACK], BF16, name="wb", bufs=10, align_bytes=64)
+                packed[u] = work.tile([P, H * PACK], BF16, name="wb", bufs=PACKED_BUFS, align_bytes=64)
+
+        def pack_matrix(u):
+            packed_tile(u)
+            planes = raw[u][:].rearrange("p (j c) -> p j c", j=PACK)
             if u < E:
                 nc.scalar.copy(
-                    wb[u][:].rearrange("p (t m j) -> p m j t", t=PACK, j=PACK),
-                    planes(u).rearrange("p j (m t) -> p m j t", t=PACK),
+                    packed[u][:].rearrange("p (t m j) -> p m j t", t=PACK, j=PACK),
+                    planes.rearrange("p j (m t) -> p m j t", t=PACK),
                 )
-            elif u < FIRST_Q:
-                interleave(wb[u], planes(u), nc.scalar.copy)
             else:
-                dst = wb[u][:].rearrange("p (s c i j) -> p s c j i", s=QUAD, i=4, j=PACK)
-                src = raw[u][:].rearrange("p (s j c i) -> p s c j i", s=QUAD, i=4, j=PACK)
-                if u == FIRST_Q:
-                    nc.vector.tensor_copy(dst[:, 0:2], src[:, 0:2])
-                    nc.vector.tensor_copy(dst[:, 2], src[:, 2])
-                    nc.vector.tensor_copy(dst[:, 3], src[:, 3])
-                else:
-                    nc.scalar.copy(dst[:, 0:2], src[:, 0:2])
-                    nc.scalar.copy(dst[:, 2:4], src[:, 2:4])
+                interleave(nc.scalar.copy, packed[u], planes)
 
-        def quant(u):
-            wc = work.tile([P, H], U32, name="wc", bufs=4, align_bytes=64)
-            ws = work.tile([P, H], U8, name="ws", bufs=4, align_bytes=64)
-            nc.vector.quantize_mx(out=wc[:].bitcast(FP8X4), scales=ws[:], in_=wb[u][:])
-            w_q[u] = (wc, ws)
+        def pack_slabs(copy, u, parts):
+            dst = packed[u][:].rearrange("p (s c i j) -> p s c j i", s=QUAD, i=LINE, j=PACK)
+            src = raw[u][:].rearrange("p (s j c i) -> p s c j i", s=QUAD, i=LINE, j=PACK)
+            for part in parts:
+                copy(dst[:, part], src[:, part])
 
         bank = {}
         da_q = {}
         staged = {}
 
-        def multiply(u):
-            wc, ws = w_q.pop(u)
-            whole = E <= u < FIRST_Q
-            if not whole:
-                bank[u] = psum.tile([P, QUAD, C], F32, name="bank")
-            elif u % 2 == 0:
-                bank[u] = psum.tile([P, QUAD, C], F32, name="bank")
-                bank[u + 1] = psum.tile([P, QUAD, C], F32, name="bank")
+        def new_banks(u, count):
+            for b in range(count):
+                bank[u + b] = psum.tile([P, QUAD, C], F32, name="bank")
+
+        def multiply(u, weights):
+            if u < E or u >= FIRST_Q:
+                new_banks(u, 1)
+            elif u == E:
+                new_banks(u, QUARTERS)
+            elif u >= E + QUAD and u % 2 == 0:
+                new_banks(u, 2)
             for t in range(QUAD):
                 if u < E:
-                    mc, ms = g_q[u // QUAD]
-                    cols = slice(u % QUAD * C, u % QUAD * C + C)
+                    one_pass(bank[u][:, t, :], weights, t, g_q[u // QUAD], u % QUAD)
+                elif u < E + QUAD:
+                    one_pass(bank[E + t][:, u - E, :], weights, t, da_q[(u - E) // 2], u % 2)
+                elif u < FIRST_Q:
+                    dst = bank[u - u % 2 + t // 2][:, t % 2 * 2 + u % 2, :]
+                    one_pass(dst, weights, t, da_q[(u - E) // 2], u % 2)
                 else:
-                    e = u - E if whole else WHOLE + t
-                    mc, ms = da_q[e // 2]
-                    cols = slice(e % 2 * C, e % 2 * C + C)
-                dst = bank[u - u % 2 + t // 2][:, t % 2 * 2 + u % 2, :] if whole else bank[u][:, t, :]
-                nc.tensor.matmul_mx(
-                    out=dst,
-                    lhsT=wc[:, t * P : (t + 1) * P].bitcast(FP8X4),
-                    lhsT_scale=ws[:, t * P : (t + 1) * P],
-                    rhs=mc[:, cols].bitcast(FP8X4),
-                    rhs_scale=ms[:, cols],
-                    start=True,
-                    stop=True,
-                )
+                    one_pass(bank[u][:, t, :], weights, t, da_q[(WHOLE + t) // 2], t % 2)
 
         def make_da(pair):
-            db = raw[ORDER[ORDER.index(2 * pair + 1) + 1]][:].bitcast(BF16)[:, 0 : 2 * C * PACK]
+            follower = ORDER[ORDER.index(2 * pair + 1) + 1]
+            staged[pair] = raw[follower][:].bitcast(BF16)[:, 0 : 2 * C * PACK]
             for half in range(2):
-                c0 = half * C
-                a0 = pair % 2 * 2 * C + c0
+                e = 2 * pair + half
                 nc.vector.scalar_tensor_tensor(
-                    db[:, c0 * PACK : (c0 + C) * PACK].rearrange("p (n t) -> p n t", t=PACK),
-                    a_t[pair // 2][:, :, a0 : a0 + C].rearrange("p t n -> p n t"),
+                    staged[pair][:, half * C * PACK : (half + 1) * C * PACK].rearrange("p (n t) -> p n t", t=PACK),
+                    a_t[e // QUAD][:, :, e % QUAD * C : (e % QUAD + 1) * C].rearrange("p t n -> p n t"),
                     0.0,
-                    bank.pop(2 * pair + half)[:].rearrange("p t n -> p n t"),
+                    bank[e][:].rearrange("p t n -> p n t"),
                     MAX,
                     MULT,
                 )
-            staged[pair] = db
 
-        def quant_da(pair):
-            db = staged.pop(pair)
-            dc = held.tile([P, 2 * C], U32, name=f"dc{pair}", align_bytes=64)
-            ds = held.tile([P, 2 * C], U8, name=f"ds{pair}", align_bytes=64)
-            nc.vector.quantize_mx(out=dc[:].bitcast(FP8X4), scales=ds[:], in_=db)
-            da_q[pair] = (dc, ds)
+        def quantise_da(pair):
+            codes = held.tile([P, 2 * C], U32, name=f"dc{pair}", align_bytes=64)
+            scales = held.tile([P, 2 * C], U8, name=f"ds{pair}", align_bytes=64)
+            nc.vector.quantize_mx(out=codes[:].bitcast(FP8X4), scales=scales[:], in_=staged.pop(pair))
+            da_q[pair] = (codes, scales)
 
-        dxs = {}
+        dx = {}
 
-        def read_pair(u, quarters=range(QUARTERS)):
-            c0 = (u - E) * C
+        def twice_on_vector(dst, src):
+            nc.vector.tensor_scalar_mul(dst, src, 2.0)
+
+        def twice_on_scalar(dst, src):
+            nc.scalar.activation(dst, src, COPY, scale=2.0)
+
+        def read(twice, sums, q, expert, count):
+            twice(dx[q][:, expert * C : (expert + count) * C], sums.rearrange("p s c -> p (s c)"))
+
+        def read_pair(twice, u, quarters):
             for q in quarters:
-                src = bank[u + q // 2][:].rearrange("p s c -> p (s c)")[:, q % 2 * 2 * C : (q % 2 + 1) * 2 * C]
-                if u == FIRST_Q - 2 and q > 0:
-                    nc.scalar.activation(dxs[q][:, c0 : c0 + 2 * C], src, COPY, scale=2.0)
-                else:
-                    nc.vector.tensor_scalar_mul(dxs[q][:, c0 : c0 + 2 * C], src, 2.0)
+                read(twice, bank[u + q // 2][:, q % 2 * 2 : q % 2 * 2 + 2, :], q, u - E, 2)
 
-        def read_quarter(q):
-            src = bank[FIRST_Q + q][:].rearrange("p s c -> p (s c)")
-            nc.scalar.activation(dxs[q][:, WHOLE * C :], src, COPY, scale=2.0)
+        def half_of_quarter_0(half):
+            weights = quantise(packed[FIRST_Q][:, half * 2 * P * PACK : (half + 1) * 2 * P * PACK], 2 * P)
+            sums = psum.tile([P, 2, C], F32, name="bank")
+            for t in range(2):
+                one_pass(sums[:, t, :], weights, t, da_q[WHOLE // 2 + half], t)
+            return sums
 
-        def first_quarter():
-            bank[FIRST_Q] = psum.tile([P, QUAD, C], F32, name="bank")
-            for pair in range(WHOLE // 2, E // 2):
-                s0 = 2 * pair - WHOLE
-                wc = work.tile([P, 2 * P], U32, name="wc", bufs=4, align_bytes=64)
-                ws = work.tile([P, 2 * P], U8, name="ws", bufs=4, align_bytes=64)
-                src = wb[FIRST_Q][:, s0 * P * PACK : (s0 + 2) * P * PACK]
-                nc.vector.quantize_mx(out=wc[:].bitcast(FP8X4), scales=ws[:], in_=src)
-                mc, ms = da_q[pair]
-                for t in range(2):
-                    cols = slice(t * P, (t + 1) * P)
-                    nc.tensor.matmul_mx(
-                        out=bank[FIRST_Q][:, s0 + t, :],
-                        lhsT=wc[:, cols].bitcast(FP8X4),
-                        lhsT_scale=ws[:, cols],
-                        rhs=mc[:, cols].bitcast(FP8X4),
-                        rhs_scale=ms[:, cols],
-                        start=True,
-                        stop=True,
-                    )
+        def combine(q, picked, res, cuts):
+            pieces = [(slice(t0, t1), slice(t0 // STRIPE, t1 // STRIPE)) for t0, t1 in zip(cuts, cuts[1:])]
+            for cols, entries in pieces:
+                nc.vector.tensor_copy(picked[:, cols], dx[q][:].indirect(pos1_t[:, entries]))
+            for cols, entries in pieces:
+                nc.vector.tensor_tensor(res[:, cols], dx[q][:].indirect(pos2_t[:, entries]), picked[:, cols], ADD)
+                nc.sync.dma_start(out[q * P : (q + 1) * P, cols], res[:, cols])
 
-        def combine(q):
-            dx = dxs[q]
-            cut = T // 2 if q < QUARTERS - 1 else 3 * T // 4
-            halves = [(slice(a0, a1), slice(a0 // 16, a1 // 16)) for a0, a1 in ((0, cut), (cut, T))]
-            picked = work.tile([P, T], F32, name="picked", tag="tok", bufs=PACK)
-            for cols, lst in halves:
-                nc.vector.tensor_copy(picked[:, cols], dx[:].indirect(pos1_t[:, lst]))
-            if q < QUARTERS - 1:
-                res = wb[FIRST_Q + q + 1][:].bitcast(F32)
-                for cols, lst in halves:
-                    nc.vector.tensor_tensor(res[:, cols], dx[:].indirect(pos2_t[:, lst]), picked[:, cols], ADD)
-                nc.sync.dma_start(out[q * P : (q + 1) * P, :], res[:, 0:T])
-            else:
-                last = work.tile([P, T], F32, name="last", tag="tok", bufs=PACK)
-                for cols, lst in halves:
-                    nc.vector.tensor_tensor(last[:, cols], dx[:].indirect(pos2_t[:, lst]), picked[:, cols], ADD)
-                    nc.sync.dma_start(out[q * P : (q + 1) * P, cols], last[:, cols])
+        def token_tile():
+            return work.tile([P, T], F32, name="token", tag="tok", bufs=PACK)
 
         for u in ORDER[:AHEAD]:
             load(u)
+
         for j in range(PACK):
-            gather(0, j)
+            gather_g(0, j)
         for g in range(1, GROUPS):
-            gather(g, 0)
+            gather_g(g, 0)
             pack_g(g - 1)
-            gather(g, 1)
-            quant_g(g - 1)
-            gather(g, 2)
-            gather(g, 3)
+            gather_g(g, 1)
+            quantise_g(g - 1)
+            gather_g(g, 2)
+            gather_g(g, 3)
         pack_g(GROUPS - 1)
-        quant_g(GROUPS - 1)
-        for step, u in enumerate(ORDER):
+        quantise_g(GROUPS - 1)
+
+        for step, u in enumerate(ORDER[:FIRST_Q]):
             if step + AHEAD < UNITS:
                 load(ORDER[step + AHEAD])
             before = ORDER[step - 1]
-            if u == FIRST_Q:
-                src = bank[u][:].rearrange("p s c -> p (s c)")
-                nc.vector.tensor_scalar_mul(dxs[0][:, WHOLE * C :], src, 2.0)
-                read_pair(FIRST_Q - 2, (0,))
-                continue
-            if u > FIRST_Q + 1:
-                read_quarter(u - FIRST_Q - 1)
-            pack(u)
+            pack_matrix(u)
             if u == FIRST_Q - 1:
-                pack(FIRST_Q)
-                first_quarter()
-            if u == FIRST_Q + 1:
-                read_pair(FIRST_Q - 2, (1, 2, 3))
-            quant(u)
+                packed_tile(FIRST_Q)
+                pack_slabs(nc.vector.tensor_copy, FIRST_Q, (slice(0, 2), 2))
+                early_sums = half_of_quarter_0(0)
+            weights = quantise(packed[u][:], H)
             for pair in list(staged):
-                quant_da(pair)
-            multiply(u)
+                quantise_da(pair)
+            multiply(u, weights)
             if before < E and before % 2 == 1:
                 make_da(before // 2)
             if u == E:
                 for q in range(2):
-                    dxs[q] = work.tile([P, S], F32, name=f"dx{q}", tag="g32")
-                    dxs[q + 2] = held.tile([P, S], F32, name=f"dx{q + 2}", tag=f"a{q}")
-            if E <= before < FIRST_Q - 2 and before % 2 == 1:
-                read_pair(before - 1)
-            if u > FIRST_Q:
-                combine(u - FIRST_Q - 1)
-        read_quarter(QUARTERS - 1)
-        combine(QUARTERS - 1)
+                    dx[q] = work.tile([P, S], F32, name=f"dx{q}", tag="g32")
+                    dx[q + 2] = held.tile([P, S], F32, name=f"dx{q + 2}", tag=f"a{q}")
+            if before == E + QUAD - 1:
+                for q in range(QUARTERS):
+                    read(twice_on_vector, bank[E + q][:], q, 0, QUAD)
+            if u == LAST_PAIR:
+                read_pair(twice_on_vector, LAST_PAIR - 2, range(QUARTERS))
+
+        pack_slabs(nc.vector.tensor_copy, FIRST_Q, (3,))
+        read(twice_on_vector, early_sums[:], 0, WHOLE, 2)
+        late_sums = half_of_quarter_0(1)
+        read_pair(twice_on_vector, LAST_PAIR, (0,))
+        read(twice_on_vector, late_sums[:], 0, WHOLE + 2, 2)
+
+        for q in range(QUARTERS - 1):
+            u = FIRST_Q + q + 1
+            if q > 0:
+                read(twice_on_scalar, bank[u - 1][:], q, WHOLE, QUAD)
+            packed_tile(u)
+            pack_slabs(nc.scalar.copy, u, (slice(0, 2), 2, 3))
+            if q == 0:
+                read_pair(twice_on_scalar, LAST_PAIR, range(1, QUARTERS))
+            multiply(u, quantise(packed[u][:], H))
+            combine(q, token_tile(), packed[u][:].bitcast(F32), (0, T))
+        q = QUARTERS - 1
+        read(twice_on_scalar, bank[UNITS - 1][:], q, WHOLE, QUAD)
+        combine(q, token_tile(), token_tile(), (0, LAST_CUT, T))

@@ -32,11 +32,14 @@ QUARTERS = K // P
 UNITS = 2 * E
 WHOLE = E - QUAD
 FIRST_Q = E + WHOLE
+CUT = FIRST_Q - 1
 LAST_PAIR = FIRST_Q - 2
-ORDER = [*range(0, 2 * QUAD), *range(E, E + QUAD), *range(2 * QUAD, E), *range(E + QUAD, UNITS)]
+ORDER = list(range(UNITS))
+SHARED = (E + 1, E + 4)
+A_AFTER = 4
 RING = 12
 AHEAD = RING // 2
-PACKED_BUFS = 10
+PACKED_BUFS = 8
 CODE_BUFS = 4
 LAST_CUT = 3 * T // 4
 
@@ -77,30 +80,32 @@ def tile_moe_bdx_mlp_relu2_kernel(tc, dyT, a, w2, w1, gate, offs, pos1, pos2, ou
             nc.scalar.copy(gate_t[g][:].rearrange("p (r c) -> p r c", c=QUAD), spread[:].rearrange("p c r -> p r c"))
 
         raw = {}
-        a_t = {}
+        a_t = held.tile([P, PACK, S], F32)
+
+        def load_slab(u, s, expert, q):
+            slabs = raw[u][:].rearrange("p (s j c) -> p s j c", s=QUAD, j=PACK)
+            rows = w1[expert].rearrange("(p j) k -> p j k", j=PACK)
+            nc.sync.dma_start(slabs[:, s], rows[:, :, q * P : (q + 1) * P])
 
         def load(u):
             raw[u] = held.tile([P, PACK * H], F32, name=f"raw{u}", tag=f"raw{ORDER.index(u) % RING}", align_bytes=64)
-            if u < FIRST_Q:
+            if u < CUT:
                 matrix = w2[u] if u < E else w1[u - E]
                 nc.sync.dma_start(raw[u][:], matrix.rearrange("(p j) i -> p (j i)", j=PACK))
-            else:
+            elif u > CUT:
                 q = u - FIRST_Q
-                slabs = raw[u][:].rearrange("p (s j c) -> p s j c", s=QUAD, j=PACK)
+                load_slab(CUT, q, CUT - E, q)
                 for s in range(QUAD):
-                    rows = w1[WHOLE + s].rearrange("(p j) k -> p j k", j=PACK)
-                    nc.sync.dma_start(slabs[:, s], rows[:, :, q * P : (q + 1) * P])
-            if u < E and u % QUAD == QUAD - 1:
-                g = u // QUAD
-                a_t[g] = held.tile([P, PACK, GROUP], F32, name=f"a{g}")
-                nc.sync.dma_start(a_t[g][:], a_rows[:, :, g * GROUP : (g + 1) * GROUP])
+                    load_slab(u, s, WHOLE + s, q)
+            if u == A_AFTER:
+                nc.sync.dma_start(a_t[:], a_rows)
             if u == E - 1:
                 nc.sync.dma_start(pos1_t[:], pos1)
                 nc.sync.dma_start(pos2_t[:], pos2)
 
         def interleave(copy, dst, planes):
             copy(
-                dst[:].rearrange("p (c i j) -> p c j i", i=LINE, j=PACK),
+                dst.rearrange("p (c i j) -> p c j i", i=LINE, j=PACK),
                 planes.rearrange("p j (c i) -> p c j i", i=LINE),
             )
 
@@ -134,7 +139,7 @@ def tile_moe_bdx_mlp_relu2_kernel(tc, dyT, a, w2, w1, gate, offs, pos1, pos2, ou
 
         def pack_g(g):
             gb[g] = work.tile([P, GROUP * PACK], BF16, name="gb", bufs=1, align_bytes=64)
-            interleave(nc.vector.tensor_copy, gb[g], g32[g][:])
+            interleave(nc.scalar.copy if g else nc.vector.tensor_copy, gb[g][:], g32[g][:])
 
         def quantise_g(g):
             nc.vector.quantize_mx(out=g_q[g][0][:].bitcast(FP8X4), scales=g_q[g][1][:], in_=gb[g][:])
@@ -155,11 +160,14 @@ def tile_moe_bdx_mlp_relu2_kernel(tc, dyT, a, w2, w1, gate, offs, pos1, pos2, ou
                     packed[u][:].rearrange("p (t m j) -> p m j t", t=PACK, j=PACK),
                     planes.rearrange("p j (m t) -> p m j t", t=PACK),
                 )
+            elif u in SHARED:
+                interleave(nc.scalar.copy, packed[u][:, : H * PACK // 2], planes[:, :, : H // 2])
+                interleave(nc.vector.tensor_copy, packed[u][:, H * PACK // 2 :], planes[:, :, H // 2 :])
             else:
-                interleave(nc.scalar.copy, packed[u], planes)
+                interleave(nc.scalar.copy, packed[u][:], planes)
 
-        def pack_slabs(copy, u, parts):
-            dst = packed[u][:].rearrange("p (s c i j) -> p s c j i", s=QUAD, i=LINE, j=PACK)
+        def pack_slabs(copy, u, parts, home=None):
+            dst = packed[home or u][:].rearrange("p (s c i j) -> p s c j i", s=QUAD, i=LINE, j=PACK)
             src = raw[u][:].rearrange("p (s j c i) -> p s c j i", s=QUAD, i=LINE, j=PACK)
             for part in parts:
                 copy(dst[:, part], src[:, part])
@@ -197,7 +205,7 @@ def tile_moe_bdx_mlp_relu2_kernel(tc, dyT, a, w2, w1, gate, offs, pos1, pos2, ou
                 e = 2 * pair + half
                 nc.vector.scalar_tensor_tensor(
                     staged[pair][:, half * C * PACK : (half + 1) * C * PACK].rearrange("p (n t) -> p n t", t=PACK),
-                    a_t[e // QUAD][:, :, e % QUAD * C : (e % QUAD + 1) * C].rearrange("p t n -> p n t"),
+                    a_t[:, :, e * C : (e + 1) * C].rearrange("p t n -> p n t"),
                     0.0,
                     bank[e][:].rearrange("p t n -> p n t"),
                     MAX,
@@ -226,11 +234,15 @@ def tile_moe_bdx_mlp_relu2_kernel(tc, dyT, a, w2, w1, gate, offs, pos1, pos2, ou
                 read(twice, bank[u + q // 2][:, q % 2 * 2 : q % 2 * 2 + 2, :], q, u - E, 2)
 
         def half_of_quarter_0(half):
-            weights = quantise(packed[FIRST_Q][:, half * 2 * P * PACK : (half + 1) * 2 * P * PACK], 2 * P)
+            weights = quantise(packed[LAST_PAIR if half else FIRST_Q][:, half * 2 * P * PACK : (half + 1) * 2 * P * PACK], 2 * P)
             sums = psum.tile([P, 2, C], F32, name="bank")
             for t in range(2):
                 one_pass(sums[:, t, :], weights, t, da_q[WHOLE // 2 + half], t)
             return sums
+
+        def multiply_cut(q):
+            weights = quantise(packed[CUT][:, q * P * PACK : (q + 1) * P * PACK], P)
+            one_pass(bank[LAST_PAIR + q // 2][:, q % 2 * 2 + 1, :], weights, 0, da_q[(CUT - E) // 2], 1)
 
         def combine(q, picked, res, cuts):
             pieces = [(slice(t0, t1), slice(t0 // STRIPE, t1 // STRIPE)) for t0, t1 in zip(cuts, cuts[1:])]
@@ -258,15 +270,18 @@ def tile_moe_bdx_mlp_relu2_kernel(tc, dyT, a, w2, w1, gate, offs, pos1, pos2, ou
         pack_g(GROUPS - 1)
         quantise_g(GROUPS - 1)
 
-        for step, u in enumerate(ORDER[:FIRST_Q]):
+        for step, u in enumerate(ORDER[:CUT]):
             if step + AHEAD < UNITS:
                 load(ORDER[step + AHEAD])
             before = ORDER[step - 1]
             pack_matrix(u)
-            if u == FIRST_Q - 1:
+            if u == LAST_PAIR:
+                read_pair(twice_on_vector, LAST_PAIR - 2, (0,))
+                read_pair(twice_on_scalar, LAST_PAIR - 2, range(1, QUARTERS))
+                packed_tile(CUT)
+                pack_slabs(nc.vector.tensor_copy, CUT, (0,))
                 packed_tile(FIRST_Q)
-                pack_slabs(nc.vector.tensor_copy, FIRST_Q, (slice(0, 2), 2))
-                early_sums = half_of_quarter_0(0)
+                pack_slabs(nc.vector.tensor_copy, FIRST_Q, (slice(0, 2),))
             weights = quantise(packed[u][:], H)
             for pair in list(staged):
                 quantise_da(pair)
@@ -276,29 +291,32 @@ def tile_moe_bdx_mlp_relu2_kernel(tc, dyT, a, w2, w1, gate, offs, pos1, pos2, ou
             if u == E:
                 for q in range(2):
                     dx[q] = work.tile([P, S], F32, name=f"dx{q}", tag="g32")
-                    dx[q + 2] = held.tile([P, S], F32, name=f"dx{q + 2}", tag=f"a{q}")
+                    dx[q + 2] = held.tile([P, S], F32, name=f"dx{q + 2}")
             if before == E + QUAD - 1:
                 for q in range(QUARTERS):
                     read(twice_on_vector, bank[E + q][:], q, 0, QUAD)
-            if u == LAST_PAIR:
-                read_pair(twice_on_vector, LAST_PAIR - 2, range(QUARTERS))
+        multiply_cut(0)
+        pack_slabs(nc.vector.tensor_copy, FIRST_Q, (2,), LAST_PAIR)
+        early_sums = half_of_quarter_0(0)
 
-        pack_slabs(nc.vector.tensor_copy, FIRST_Q, (3,))
-        read(twice_on_vector, early_sums[:], 0, WHOLE, 2)
-        late_sums = half_of_quarter_0(1)
+        pack_slabs(nc.vector.tensor_copy, FIRST_Q, (3,), LAST_PAIR)
         read_pair(twice_on_vector, LAST_PAIR, (0,))
+        late_sums = half_of_quarter_0(1)
+        read(twice_on_vector, early_sums[:], 0, WHOLE, 2)
         read(twice_on_vector, late_sums[:], 0, WHOLE + 2, 2)
 
         for q in range(QUARTERS - 1):
             u = FIRST_Q + q + 1
             if q > 0:
+                read_pair(twice_on_scalar, LAST_PAIR, (q,))
                 read(twice_on_scalar, bank[u - 1][:], q, WHOLE, QUAD)
+            pack_slabs(nc.scalar.copy, CUT, (q + 1,))
             packed_tile(u)
             pack_slabs(nc.scalar.copy, u, (slice(0, 2), 2, 3))
-            if q == 0:
-                read_pair(twice_on_scalar, LAST_PAIR, range(1, QUARTERS))
+            multiply_cut(q + 1)
             multiply(u, quantise(packed[u][:], H))
             combine(q, token_tile(), packed[u][:].bitcast(F32), (0, T))
         q = QUARTERS - 1
+        read_pair(twice_on_scalar, LAST_PAIR, (q,))
         read(twice_on_scalar, bank[UNITS - 1][:], q, WHOLE, QUAD)
         combine(q, token_tile(), token_tile(), (0, LAST_CUT, T))

@@ -39,7 +39,7 @@ SHARED = (E + 1, E + 4)
 A_AFTER = 4
 RING = 12
 AHEAD = RING // 2
-PACKED_BUFS = 8
+PACKED_BUFS = 9
 CODE_BUFS = 4
 LAST_CUT = 3 * T // 4
 
@@ -67,16 +67,18 @@ def tile_moe_bdx_mlp_relu2_kernel(tc, dyT, a, w2, w1, gate, offs, pos1, pos2, ou
         a_rows = a.rearrange("(p j) s -> p j s", j=PACK)
 
         nc.sync.dma_start(offs_t[:], offs)
-        gate_cols = held.tile([P, GROUPS, QUAD], F32)
-        nc.sync.dma_start(gate_cols[:], gate[0, :].rearrange("(g r c) -> r g c", g=GROUPS, c=QUAD))
+        gate_cols = held.tile([P, GROUPS - 1, QUAD], F32)
         for j in range(PACK):
             nc.sync.dma_start(dy[j][:], dy_rows[:, j, :])
+            if j == 0:
+                nc.sync.dma_start(gate_t[0][:], gate[:P, :GROUP])
+                nc.sync.dma_start(gate_cols[:], gate[0, GROUP:].rearrange("(g r c) -> r g c", g=GROUPS - 1, c=QUAD))
         identity = held.tile([P, P], F32, tag="first", align_bytes=64)
         make_identity(nc, identity[:])
-        for g in range(GROUPS):
+        for g in range(1, GROUPS):
             spread = psum.tile([P, QUAD, P], F32, name="bank")
             for c in range(QUAD):
-                nc.tensor.transpose(spread[:, c, :], gate_cols[:, g, c : c + 1].to_broadcast([P, P]), identity[:])
+                nc.tensor.transpose(spread[:, c, :], gate_cols[:, g - 1, c : c + 1].to_broadcast([P, P]), identity[:])
             nc.scalar.copy(gate_t[g][:].rearrange("p (r c) -> p r c", c=QUAD), spread[:].rearrange("p c r -> p r c"))
 
         raw = {}
@@ -138,11 +140,12 @@ def tile_moe_bdx_mlp_relu2_kernel(tc, dyT, a, w2, w1, gate, offs, pos1, pos2, ou
             nc.vector.tensor_tensor(g32[g][:, j, :], dy[j][:].indirect(entries), gate_t[g][:], MULT)
 
         def pack_g(g):
-            gb[g] = work.tile([P, GROUP * PACK], BF16, name="gb", bufs=1, align_bytes=64)
-            interleave(nc.scalar.copy if g else nc.vector.tensor_copy, gb[g][:], g32[g][:])
+            home, half = (0, 0) if g == 0 else (A_AFTER, g - 1)
+            gb[g] = raw[home][:].bitcast(BF16)[:, half * GROUP * PACK : (half + 1) * GROUP * PACK]
+            interleave(nc.scalar.copy, gb[g], g32[g][:])
 
         def quantise_g(g):
-            nc.vector.quantize_mx(out=g_q[g][0][:].bitcast(FP8X4), scales=g_q[g][1][:], in_=gb[g][:])
+            nc.vector.quantize_mx(out=g_q[g][0][:].bitcast(FP8X4), scales=g_q[g][1][:], in_=gb[g])
 
         packed = {}
 
@@ -234,7 +237,7 @@ def tile_moe_bdx_mlp_relu2_kernel(tc, dyT, a, w2, w1, gate, offs, pos1, pos2, ou
                 read(twice, bank[u + q // 2][:, q % 2 * 2 : q % 2 * 2 + 2, :], q, u - E, 2)
 
         def half_of_quarter_0(half):
-            weights = quantise(packed[LAST_PAIR if half else FIRST_Q][:, half * 2 * P * PACK : (half + 1) * 2 * P * PACK], 2 * P)
+            weights = quantise(packed[FIRST_Q][:, half * 2 * P * PACK : (half + 1) * 2 * P * PACK], 2 * P)
             sums = psum.tile([P, 2, C], F32, name="bank")
             for t in range(2):
                 one_pass(sums[:, t, :], weights, t, da_q[WHOLE // 2 + half], t)
@@ -258,23 +261,24 @@ def tile_moe_bdx_mlp_relu2_kernel(tc, dyT, a, w2, w1, gate, offs, pos1, pos2, ou
         for u in ORDER[:AHEAD]:
             load(u)
 
-        for j in range(PACK):
-            gather_g(0, j)
-        for g in range(1, GROUPS):
-            gather_g(g, 0)
-            pack_g(g - 1)
-            gather_g(g, 1)
-            quantise_g(g - 1)
-            gather_g(g, 2)
-            gather_g(g, 3)
-        pack_g(GROUPS - 1)
-        quantise_g(GROUPS - 1)
+        for g in range(GROUPS - 1):
+            for j in range(PACK):
+                gather_g(g, j)
 
         for step, u in enumerate(ORDER[:CUT]):
             if step + AHEAD < UNITS:
                 load(ORDER[step + AHEAD])
             before = ORDER[step - 1]
             pack_matrix(u)
+            if u == 0:
+                pack_g(0)
+                for j in range(PACK):
+                    gather_g(GROUPS - 1, j)
+                quantise_g(0)
+            if u == A_AFTER:
+                for g in range(1, GROUPS):
+                    pack_g(g)
+                    quantise_g(g)
             if u == LAST_PAIR:
                 read_pair(twice_on_vector, LAST_PAIR - 2, (0,))
                 read_pair(twice_on_scalar, LAST_PAIR - 2, range(1, QUARTERS))
@@ -296,10 +300,10 @@ def tile_moe_bdx_mlp_relu2_kernel(tc, dyT, a, w2, w1, gate, offs, pos1, pos2, ou
                 for q in range(QUARTERS):
                     read(twice_on_vector, bank[E + q][:], q, 0, QUAD)
         multiply_cut(0)
-        pack_slabs(nc.vector.tensor_copy, FIRST_Q, (2,), LAST_PAIR)
+        pack_slabs(nc.vector.tensor_copy, FIRST_Q, (2,))
         early_sums = half_of_quarter_0(0)
 
-        pack_slabs(nc.vector.tensor_copy, FIRST_Q, (3,), LAST_PAIR)
+        pack_slabs(nc.vector.tensor_copy, FIRST_Q, (3,))
         read_pair(twice_on_vector, LAST_PAIR, (0,))
         late_sums = half_of_quarter_0(1)
         read(twice_on_vector, early_sums[:], 0, WHOLE, 2)

@@ -36,10 +36,11 @@ CUT = FIRST_Q - 1
 LAST_PAIR = FIRST_Q - 2
 ORDER = list(range(UNITS))
 SHARED = (E + 1, E + 4)
-A_AFTER = 4
+SLAB = P * PACK
+A_AFTER = 3
 RING = 12
 AHEAD = RING // 2
-PACKED_BUFS = 9
+PACKED_BUFS = 8
 CODE_BUFS = 4
 LAST_CUT = 3 * T // 4
 
@@ -67,18 +68,16 @@ def tile_moe_bdx_mlp_relu2_kernel(tc, dyT, a, w2, w1, gate, offs, pos1, pos2, ou
         a_rows = a.rearrange("(p j) s -> p j s", j=PACK)
 
         nc.sync.dma_start(offs_t[:], offs)
-        gate_cols = held.tile([P, GROUPS - 1, QUAD], F32)
+        gate_cols = held.tile([P, GROUPS, QUAD], F32)
+        nc.sync.dma_start(gate_cols[:], gate[0, :].rearrange("(g r c) -> r g c", g=GROUPS, c=QUAD))
         for j in range(PACK):
             nc.sync.dma_start(dy[j][:], dy_rows[:, j, :])
-            if j == 0:
-                nc.sync.dma_start(gate_t[0][:], gate[:P, :GROUP])
-                nc.sync.dma_start(gate_cols[:], gate[0, GROUP:].rearrange("(g r c) -> r g c", g=GROUPS - 1, c=QUAD))
         identity = held.tile([P, P], F32, tag="first", align_bytes=64)
         make_identity(nc, identity[:])
-        for g in range(1, GROUPS):
+        for g in range(GROUPS):
             spread = psum.tile([P, QUAD, P], F32, name="bank")
             for c in range(QUAD):
-                nc.tensor.transpose(spread[:, c, :], gate_cols[:, g - 1, c : c + 1].to_broadcast([P, P]), identity[:])
+                nc.tensor.transpose(spread[:, c, :], gate_cols[:, g, c : c + 1].to_broadcast([P, P]), identity[:])
             nc.scalar.copy(gate_t[g][:].rearrange("p (r c) -> p r c", c=QUAD), spread[:].rearrange("p c r -> p r c"))
 
         raw = {}
@@ -111,8 +110,11 @@ def tile_moe_bdx_mlp_relu2_kernel(tc, dyT, a, w2, w1, gate, offs, pos1, pos2, ou
                 planes.rearrange("p j (c i) -> p c j i", i=LINE),
             )
 
-        def quantise(src, columns):
-            codes = work.tile([P, columns], U32, name="wc", bufs=CODE_BUFS, align_bytes=64)
+        def quantise(src, columns, tag=None):
+            if tag:
+                codes = held.tile([P, columns], U32, name="late_codes", tag=tag, align_bytes=64)
+            else:
+                codes = work.tile([P, columns], U32, name="wc", bufs=CODE_BUFS, align_bytes=64)
             scales = work.tile([P, columns], U8, name="ws", bufs=CODE_BUFS, align_bytes=64)
             nc.vector.quantize_mx(out=codes[:].bitcast(FP8X4), scales=scales[:], in_=src)
             return codes, scales
@@ -243,8 +245,19 @@ def tile_moe_bdx_mlp_relu2_kernel(tc, dyT, a, w2, w1, gate, offs, pos1, pos2, ou
                 one_pass(sums[:, t, :], weights, t, da_q[WHOLE // 2 + half], t)
             return sums
 
-        def multiply_cut(q):
-            weights = quantise(packed[CUT][:, q * P * PACK : (q + 1) * P * PACK], P)
+        def raw_slab(u, s):
+            return raw[u][:, s * SLAB : (s + 1) * SLAB]
+
+        def pack_slab(dst, u, s):
+            interleave(nc.scalar.copy, dst, raw_slab(u, s).rearrange("p (j c) -> p j c", j=PACK))
+
+        def multiply_half(u, half, src, tag=None):
+            weights = quantise(src, 2 * P, tag)
+            for t in range(2):
+                one_pass(bank[u][:, 2 * half + t, :], weights, t, da_q[WHOLE // 2 + half], t)
+
+        def multiply_cut(q, src):
+            weights = quantise(src, P)
             one_pass(bank[LAST_PAIR + q // 2][:, q % 2 * 2 + 1, :], weights, 0, da_q[(CUT - E) // 2], 1)
 
         def combine(q, picked, res, cuts):
@@ -299,7 +312,7 @@ def tile_moe_bdx_mlp_relu2_kernel(tc, dyT, a, w2, w1, gate, offs, pos1, pos2, ou
             if before == E + QUAD - 1:
                 for q in range(QUARTERS):
                     read(twice_on_vector, bank[E + q][:], q, 0, QUAD)
-        multiply_cut(0)
+        multiply_cut(0, packed[CUT][:, :SLAB])
         pack_slabs(nc.vector.tensor_copy, FIRST_Q, (2,))
         early_sums = half_of_quarter_0(0)
 
@@ -314,12 +327,18 @@ def tile_moe_bdx_mlp_relu2_kernel(tc, dyT, a, w2, w1, gate, offs, pos1, pos2, ou
             if q > 0:
                 read_pair(twice_on_scalar, LAST_PAIR, (q,))
                 read(twice_on_scalar, bank[u - 1][:], q, WHOLE, QUAD)
-            pack_slabs(nc.scalar.copy, CUT, (q + 1,))
-            packed_tile(u)
-            pack_slabs(nc.scalar.copy, u, (slice(0, 2), 2, 3))
-            multiply_cut(q + 1)
-            multiply(u, quantise(packed[u][:], H))
-            combine(q, token_tile(), packed[u][:].bitcast(F32), (0, T))
+            fifth = raw_slab(u - 1, 2).bitcast(BF16)[:, :SLAB]
+            first_two = raw_slab(u - 1, 3).bitcast(BF16)
+            last_two = held.tile([P, T], F32, name=f"last{q}", tag=f"last{q}", align_bytes=64)
+            pack_slab(fifth, CUT, q + 1)
+            for s in range(QUAD):
+                home = last_two[:].bitcast(BF16) if s // 2 else first_two
+                pack_slab(home[:, s % 2 * SLAB : (s % 2 + 1) * SLAB], u, s)
+            multiply_cut(q + 1, fifth)
+            new_banks(u, 1)
+            multiply_half(u, 0, first_two)
+            multiply_half(u, 1, last_two[:].bitcast(BF16)[:, : 2 * SLAB], f"last{q + 1}")
+            combine(q, token_tile(), last_two[:], (0, T))
         q = QUARTERS - 1
         read_pair(twice_on_scalar, LAST_PAIR, (q,))
         read(twice_on_scalar, bank[UNITS - 1][:], q, WHOLE, QUAD)

@@ -28,21 +28,21 @@ QUAD = 4
 GROUP = QUAD * C
 GROUPS = S // GROUP
 QUARTERS = K // P
+SLAB = PACK * P
 
 UNITS = 2 * E
-WHOLE = E - QUAD
-FIRST_Q = E + WHOLE
+LATE = E - QUAD
+FIRST_Q = E + LATE
 CUT = FIRST_Q - 1
-LAST_PAIR = FIRST_Q - 2
-ORDER = list(range(UNITS))
-SHARED = (E + 1, E + 4)
-SLAB = P * PACK
-A_AFTER = 3
+LAST_WHOLE = CUT - 1
+SHARED = (E, E + 1, E + 3)
+A_AFTER = QUAD - 1
 RING = 12
 AHEAD = RING // 2
 PACKED_BUFS = 8
 CODE_BUFS = 4
-LAST_CUT = 3 * T // 4
+LAST_PICKS = (0, 2 * T // 3, T)
+LAST_STORES = (0, 2 * T // 3, T - 4 * STRIPE, T)
 
 
 def tile_moe_bdx_mlp_relu2_kernel(tc, dyT, a, w2, w1, gate, offs, pos1, pos2, out):
@@ -67,10 +67,11 @@ def tile_moe_bdx_mlp_relu2_kernel(tc, dyT, a, w2, w1, gate, offs, pos1, pos2, ou
         dy_rows = dyT.rearrange("(p j) t -> p j t", j=PACK)
         a_rows = a.rearrange("(p j) s -> p j s", j=PACK)
 
+        nc.sync.dma_start(dy[0][:], dy_rows[:, 0, :])
+        gate_cols = held.tile([P, GROUPS, 2 * QUAD], F32)
+        nc.sync.dma_start(gate_cols[:, :, :QUAD], gate[0, :].rearrange("(g r c) -> r g c", g=GROUPS, c=QUAD))
         nc.sync.dma_start(offs_t[:], offs)
-        gate_cols = held.tile([P, GROUPS, QUAD], F32)
-        nc.sync.dma_start(gate_cols[:], gate[0, :].rearrange("(g r c) -> r g c", g=GROUPS, c=QUAD))
-        for j in range(PACK):
+        for j in range(1, PACK):
             nc.sync.dma_start(dy[j][:], dy_rows[:, j, :])
         identity = held.tile([P, P], F32, tag="first", align_bytes=64)
         make_identity(nc, identity[:])
@@ -83,21 +84,30 @@ def tile_moe_bdx_mlp_relu2_kernel(tc, dyT, a, w2, w1, gate, offs, pos1, pos2, ou
         raw = {}
         a_t = held.tile([P, PACK, S], F32)
 
+        def raw_slab(u, s):
+            return raw[u][:, s * SLAB : (s + 1) * SLAB]
+
         def load_slab(u, s, expert, q):
-            slabs = raw[u][:].rearrange("p (s j c) -> p s j c", s=QUAD, j=PACK)
             rows = w1[expert].rearrange("(p j) k -> p j k", j=PACK)
-            nc.sync.dma_start(slabs[:, s], rows[:, :, q * P : (q + 1) * P])
+            nc.sync.dma_start(raw_slab(u, s).rearrange("p (j c) -> p j c", j=PACK), rows[:, :, q * P : (q + 1) * P])
 
         def load(u):
-            raw[u] = held.tile([P, PACK * H], F32, name=f"raw{u}", tag=f"raw{ORDER.index(u) % RING}", align_bytes=64)
-            if u < CUT:
-                matrix = w2[u] if u < E else w1[u - E]
-                nc.sync.dma_start(raw[u][:], matrix.rearrange("(p j) i -> p (j i)", j=PACK))
-            elif u > CUT:
+            if u % 2 == 0:
+                both = held.tile([P, 2 * PACK * H], F32, name=f"raw{u}", tag=f"raw{u % RING}", align_bytes=64)
+                raw[u] = both[:, : PACK * H]
+                raw[u + 1] = both[:, PACK * H :]
+                if u < E:
+                    nc.sync.dma_start(
+                        both[:].rearrange("p (e x) -> p e x", e=2),
+                        w2[u : u + 2].rearrange("e (p j) i -> p e (j i)", j=PACK),
+                    )
+            if E <= u < CUT:
+                nc.sync.dma_start(raw[u], w1[u - E].rearrange("(p j) k -> p (j k)", j=PACK))
+            if u > CUT:
                 q = u - FIRST_Q
                 load_slab(CUT, q, CUT - E, q)
                 for s in range(QUAD):
-                    load_slab(u, s, WHOLE + s, q)
+                    load_slab(u, s, LATE + s, q)
             if u == A_AFTER:
                 nc.sync.dma_start(a_t[:], a_rows)
             if u == E - 1:
@@ -142,9 +152,12 @@ def tile_moe_bdx_mlp_relu2_kernel(tc, dyT, a, w2, w1, gate, offs, pos1, pos2, ou
             nc.vector.tensor_tensor(g32[g][:, j, :], dy[j][:].indirect(entries), gate_t[g][:], MULT)
 
         def pack_g(g):
-            home, half = (0, 0) if g == 0 else (A_AFTER, g - 1)
-            gb[g] = raw[home][:].bitcast(BF16)[:, half * GROUP * PACK : (half + 1) * GROUP * PACK]
-            interleave(nc.scalar.copy, gb[g], g32[g][:])
+            if g == 0:
+                gb[g] = held.tile([P, GROUP * PACK], BF16, name="gb", tag="last0", align_bytes=64)[:]
+                interleave(nc.vector.tensor_copy, gb[g], g32[g][:])
+            else:
+                gb[g] = raw[A_AFTER].bitcast(BF16)[:, (g - 1) * GROUP * PACK : g * GROUP * PACK]
+                interleave(nc.scalar.copy, gb[g], g32[g][:])
 
         def quantise_g(g):
             nc.vector.quantize_mx(out=g_q[g][0][:].bitcast(FP8X4), scales=g_q[g][1][:], in_=gb[g])
@@ -159,7 +172,7 @@ def tile_moe_bdx_mlp_relu2_kernel(tc, dyT, a, w2, w1, gate, offs, pos1, pos2, ou
 
         def pack_matrix(u):
             packed_tile(u)
-            planes = raw[u][:].rearrange("p (j c) -> p j c", j=PACK)
+            planes = raw[u].rearrange("p (j c) -> p j c", j=PACK)
             if u < E:
                 nc.scalar.copy(
                     packed[u][:].rearrange("p (t m j) -> p m j t", t=PACK, j=PACK),
@@ -171,11 +184,13 @@ def tile_moe_bdx_mlp_relu2_kernel(tc, dyT, a, w2, w1, gate, offs, pos1, pos2, ou
             else:
                 interleave(nc.scalar.copy, packed[u][:], planes)
 
-        def pack_slabs(copy, u, parts, home=None):
-            dst = packed[home or u][:].rearrange("p (s c i j) -> p s c j i", s=QUAD, i=LINE, j=PACK)
-            src = raw[u][:].rearrange("p (s j c i) -> p s c j i", s=QUAD, i=LINE, j=PACK)
-            for part in parts:
-                copy(dst[:, part], src[:, part])
+        def pack_on_vector(u, slabs):
+            dst = packed[u][:].rearrange("p (s c i j) -> p s c j i", s=QUAD, i=LINE, j=PACK)
+            src = raw[u].rearrange("p (s j c i) -> p s c j i", s=QUAD, i=LINE, j=PACK)
+            nc.vector.tensor_copy(dst[:, slabs], src[:, slabs])
+
+        def pack_on_scalar(dst, u, s):
+            interleave(nc.scalar.copy, dst, raw_slab(u, s).rearrange("p (j c) -> p j c", j=PACK))
 
         bank = {}
         da_q = {}
@@ -186,7 +201,7 @@ def tile_moe_bdx_mlp_relu2_kernel(tc, dyT, a, w2, w1, gate, offs, pos1, pos2, ou
                 bank[u + b] = psum.tile([P, QUAD, C], F32, name="bank")
 
         def multiply(u, weights):
-            if u < E or u >= FIRST_Q:
+            if u < E:
                 new_banks(u, 1)
             elif u == E:
                 new_banks(u, QUARTERS)
@@ -197,15 +212,12 @@ def tile_moe_bdx_mlp_relu2_kernel(tc, dyT, a, w2, w1, gate, offs, pos1, pos2, ou
                     one_pass(bank[u][:, t, :], weights, t, g_q[u // QUAD], u % QUAD)
                 elif u < E + QUAD:
                     one_pass(bank[E + t][:, u - E, :], weights, t, da_q[(u - E) // 2], u % 2)
-                elif u < FIRST_Q:
+                else:
                     dst = bank[u - u % 2 + t // 2][:, t % 2 * 2 + u % 2, :]
                     one_pass(dst, weights, t, da_q[(u - E) // 2], u % 2)
-                else:
-                    one_pass(bank[u][:, t, :], weights, t, da_q[(WHOLE + t) // 2], t % 2)
 
         def make_da(pair):
-            follower = ORDER[ORDER.index(2 * pair + 1) + 1]
-            staged[pair] = raw[follower][:].bitcast(BF16)[:, 0 : 2 * C * PACK]
+            staged[pair] = raw[2 * pair + 2].bitcast(BF16)[:, 0 : 2 * C * PACK]
             for half in range(2):
                 e = 2 * pair + half
                 nc.vector.scalar_tensor_tensor(
@@ -239,107 +251,104 @@ def tile_moe_bdx_mlp_relu2_kernel(tc, dyT, a, w2, w1, gate, offs, pos1, pos2, ou
                 read(twice, bank[u + q // 2][:, q % 2 * 2 : q % 2 * 2 + 2, :], q, u - E, 2)
 
         def half_of_quarter_0(half):
-            weights = quantise(packed[FIRST_Q][:, half * 2 * P * PACK : (half + 1) * 2 * P * PACK], 2 * P)
+            weights = quantise(packed[FIRST_Q][:, half * 2 * SLAB : (half + 1) * 2 * SLAB], 2 * P)
             sums = psum.tile([P, 2, C], F32, name="bank")
             for t in range(2):
-                one_pass(sums[:, t, :], weights, t, da_q[WHOLE // 2 + half], t)
+                one_pass(sums[:, t, :], weights, t, da_q[LATE // 2 + half], t)
             return sums
-
-        def raw_slab(u, s):
-            return raw[u][:, s * SLAB : (s + 1) * SLAB]
-
-        def pack_slab(dst, u, s):
-            interleave(nc.scalar.copy, dst, raw_slab(u, s).rearrange("p (j c) -> p j c", j=PACK))
 
         def multiply_half(u, half, src, tag=None):
             weights = quantise(src, 2 * P, tag)
             for t in range(2):
-                one_pass(bank[u][:, 2 * half + t, :], weights, t, da_q[WHOLE // 2 + half], t)
+                one_pass(bank[u][:, 2 * half + t, :], weights, t, da_q[LATE // 2 + half], t)
 
         def multiply_cut(q, src):
             weights = quantise(src, P)
-            one_pass(bank[LAST_PAIR + q // 2][:, q % 2 * 2 + 1, :], weights, 0, da_q[(CUT - E) // 2], 1)
+            one_pass(bank[LAST_WHOLE + q // 2][:, q % 2 * 2 + 1, :], weights, 0, da_q[(CUT - E) // 2], 1)
 
-        def combine(q, picked, res, cuts):
-            pieces = [(slice(t0, t1), slice(t0 // STRIPE, t1 // STRIPE)) for t0, t1 in zip(cuts, cuts[1:])]
-            for cols, entries in pieces:
+        def pieces(cuts):
+            return [(slice(t0, t1), slice(t0 // STRIPE, t1 // STRIPE)) for t0, t1 in zip(cuts, cuts[1:])]
+
+        def combine(q, picked, res, picks, stores):
+            for cols, entries in pieces(picks):
                 nc.vector.tensor_copy(picked[:, cols], dx[q][:].indirect(pos1_t[:, entries]))
-            for cols, entries in pieces:
+            for cols, entries in pieces(stores):
                 nc.vector.tensor_tensor(res[:, cols], dx[q][:].indirect(pos2_t[:, entries]), picked[:, cols], ADD)
                 nc.sync.dma_start(out[q * P : (q + 1) * P, cols], res[:, cols])
 
         def token_tile():
             return work.tile([P, T], F32, name="token", tag="tok", bufs=PACK)
 
-        for u in ORDER[:AHEAD]:
+        for u in range(AHEAD):
             load(u)
 
-        for g in range(GROUPS - 1):
-            for j in range(PACK):
-                gather_g(g, j)
+        for j in range(PACK):
+            gather_g(0, j)
+        gather_g(1, 0)
+        pack_g(0)
+        gather_g(1, 1)
+        quantise_g(0)
+        gather_g(1, 2)
+        gather_g(1, 3)
+        for j in range(PACK):
+            gather_g(2, j)
 
-        for step, u in enumerate(ORDER[:CUT]):
-            if step + AHEAD < UNITS:
-                load(ORDER[step + AHEAD])
-            before = ORDER[step - 1]
+        for u in range(CUT):
+            if u + AHEAD < UNITS:
+                load(u + AHEAD)
             pack_matrix(u)
-            if u == 0:
-                pack_g(0)
-                for j in range(PACK):
-                    gather_g(GROUPS - 1, j)
-                quantise_g(0)
             if u == A_AFTER:
                 for g in range(1, GROUPS):
                     pack_g(g)
                     quantise_g(g)
-            if u == LAST_PAIR:
-                read_pair(twice_on_vector, LAST_PAIR - 2, (0,))
-                read_pair(twice_on_scalar, LAST_PAIR - 2, range(1, QUARTERS))
+            if u == LAST_WHOLE:
+                read_pair(twice_on_vector, LAST_WHOLE - 2, (0,))
+                read_pair(twice_on_scalar, LAST_WHOLE - 2, range(1, QUARTERS))
                 packed_tile(CUT)
-                pack_slabs(nc.vector.tensor_copy, CUT, (0,))
+                pack_on_vector(CUT, 0)
                 packed_tile(FIRST_Q)
-                pack_slabs(nc.vector.tensor_copy, FIRST_Q, (slice(0, 2),))
+                pack_on_vector(FIRST_Q, slice(0, 2))
             weights = quantise(packed[u][:], H)
             for pair in list(staged):
                 quantise_da(pair)
             multiply(u, weights)
-            if before < E and before % 2 == 1:
-                make_da(before // 2)
+            if 0 < u <= E and u % 2 == 0:
+                make_da(u // 2 - 1)
             if u == E:
                 for q in range(2):
                     dx[q] = work.tile([P, S], F32, name=f"dx{q}", tag="g32")
                     dx[q + 2] = held.tile([P, S], F32, name=f"dx{q + 2}")
-            if before == E + QUAD - 1:
+            if u == E + QUAD:
                 for q in range(QUARTERS):
                     read(twice_on_vector, bank[E + q][:], q, 0, QUAD)
         multiply_cut(0, packed[CUT][:, :SLAB])
-        pack_slabs(nc.vector.tensor_copy, FIRST_Q, (2,))
+        pack_on_vector(FIRST_Q, 2)
         early_sums = half_of_quarter_0(0)
 
-        pack_slabs(nc.vector.tensor_copy, FIRST_Q, (3,))
-        read_pair(twice_on_vector, LAST_PAIR, (0,))
+        pack_on_vector(FIRST_Q, 3)
+        read_pair(twice_on_vector, LAST_WHOLE, (0,))
         late_sums = half_of_quarter_0(1)
-        read(twice_on_vector, early_sums[:], 0, WHOLE, 2)
-        read(twice_on_vector, late_sums[:], 0, WHOLE + 2, 2)
+        read(twice_on_vector, early_sums[:], 0, LATE, 2)
+        read(twice_on_vector, late_sums[:], 0, LATE + 2, 2)
 
         for q in range(QUARTERS - 1):
             u = FIRST_Q + q + 1
             if q > 0:
-                read_pair(twice_on_scalar, LAST_PAIR, (q,))
-                read(twice_on_scalar, bank[u - 1][:], q, WHOLE, QUAD)
-            fifth = raw_slab(u - 1, 2).bitcast(BF16)[:, :SLAB]
+                read_pair(twice_on_scalar, LAST_WHOLE, (q,))
+                read(twice_on_scalar, bank[u - 1][:], q, LATE, QUAD)
+            cut_slab = raw_slab(u - 1, 2).bitcast(BF16)[:, :SLAB]
             first_two = raw_slab(u - 1, 3).bitcast(BF16)
             last_two = held.tile([P, T], F32, name=f"last{q}", tag=f"last{q}", align_bytes=64)
-            pack_slab(fifth, CUT, q + 1)
+            pack_on_scalar(cut_slab, CUT, q + 1)
             for s in range(QUAD):
                 home = last_two[:].bitcast(BF16) if s // 2 else first_two
-                pack_slab(home[:, s % 2 * SLAB : (s % 2 + 1) * SLAB], u, s)
-            multiply_cut(q + 1, fifth)
+                pack_on_scalar(home[:, s % 2 * SLAB : (s % 2 + 1) * SLAB], u, s)
+            multiply_cut(q + 1, cut_slab)
             new_banks(u, 1)
             multiply_half(u, 0, first_two)
             multiply_half(u, 1, last_two[:].bitcast(BF16)[:, : 2 * SLAB], f"last{q + 1}")
-            combine(q, token_tile(), last_two[:], (0, T))
+            combine(q, token_tile(), last_two[:], (0, T), (0, T))
         q = QUARTERS - 1
-        read_pair(twice_on_scalar, LAST_PAIR, (q,))
-        read(twice_on_scalar, bank[UNITS - 1][:], q, WHOLE, QUAD)
-        combine(q, token_tile(), token_tile(), (0, LAST_CUT, T))
+        read_pair(twice_on_scalar, LAST_WHOLE, (q,))
+        read(twice_on_scalar, bank[UNITS - 1][:], q, LATE, QUAD)
+        combine(q, token_tile(), token_tile(), LAST_PICKS, LAST_STORES)

@@ -34,6 +34,7 @@ UNITS = 2 * E
 LATE = E - QUAD
 FIRST_Q = E + LATE
 CUT = FIRST_Q - 1
+SLABS = QUAD + 1
 LAST_WHOLE = CUT - 1
 SHARED = (E, E + 1, E + 3)
 A_AFTER = QUAD - 1
@@ -41,8 +42,8 @@ RING = 12
 AHEAD = RING // 2
 PACKED_BUFS = 8
 CODE_BUFS = 4
-LAST_PICKS = (0, 2 * T // 3, T)
-LAST_STORES = (0, 2 * T // 3, T - 4 * STRIPE, T)
+LAST_PICKS = (0, T // 2, T)
+LAST_STORES = (0, T // 2, T - C, T)
 
 
 def tile_moe_bdx_mlp_relu2_kernel(tc, dyT, a, w2, w1, gate, offs, pos1, pos2, out):
@@ -82,18 +83,18 @@ def tile_moe_bdx_mlp_relu2_kernel(tc, dyT, a, w2, w1, gate, offs, pos1, pos2, ou
             nc.scalar.copy(gate_t[g][:].rearrange("p (r c) -> p r c", c=QUAD), spread[:].rearrange("p c r -> p r c"))
 
         raw = {}
+        two_units = {}
         a_t = held.tile([P, PACK, S], F32)
 
-        def raw_slab(u, s):
-            return raw[u][:, s * SLAB : (s + 1) * SLAB]
-
-        def load_slab(u, s, expert, q):
-            rows = w1[expert].rearrange("(p j) k -> p j k", j=PACK)
-            nc.sync.dma_start(raw_slab(u, s).rearrange("p (j c) -> p j c", j=PACK), rows[:, :, q * P : (q + 1) * P])
+        def raw_slabs(n, count=1):
+            u = CUT + n // QUAD
+            start = (u % 2 * QUAD + n % QUAD) * SLAB
+            return two_units[u - u % 2][:, start : start + count * SLAB]
 
         def load(u):
             if u % 2 == 0:
                 both = held.tile([P, 2 * PACK * H], F32, name=f"raw{u}", tag=f"raw{u % RING}", align_bytes=64)
+                two_units[u] = both
                 raw[u] = both[:, : PACK * H]
                 raw[u + 1] = both[:, PACK * H :]
                 if u < E:
@@ -103,11 +104,11 @@ def tile_moe_bdx_mlp_relu2_kernel(tc, dyT, a, w2, w1, gate, offs, pos1, pos2, ou
                     )
             if E <= u < CUT:
                 nc.sync.dma_start(raw[u], w1[u - E].rearrange("(p j) k -> p (j k)", j=PACK))
-            if u > CUT:
-                q = u - FIRST_Q
-                load_slab(CUT, q, CUT - E, q)
-                for s in range(QUAD):
-                    load_slab(u, s, LATE + s, q)
+            if u >= CUT:
+                for n in range((u - CUT) * QUAD, (u - CUT + 1) * QUAD):
+                    q, s = divmod(n, SLABS)
+                    rows = w1[CUT - E + s].rearrange("(p j) k -> p j k", j=PACK)
+                    nc.sync.dma_start(raw_slabs(n).rearrange("p (j c) -> p j c", j=PACK), rows[:, :, q * P : (q + 1) * P])
             if u == A_AFTER:
                 nc.sync.dma_start(a_t[:], a_rows)
             if u == E - 1:
@@ -184,13 +185,11 @@ def tile_moe_bdx_mlp_relu2_kernel(tc, dyT, a, w2, w1, gate, offs, pos1, pos2, ou
             else:
                 interleave(nc.scalar.copy, packed[u][:], planes)
 
-        def pack_on_vector(u, slabs):
-            dst = packed[u][:].rearrange("p (s c i j) -> p s c j i", s=QUAD, i=LINE, j=PACK)
-            src = raw[u].rearrange("p (s j c i) -> p s c j i", s=QUAD, i=LINE, j=PACK)
-            nc.vector.tensor_copy(dst[:, slabs], src[:, slabs])
-
-        def pack_on_scalar(dst, u, s):
-            interleave(nc.scalar.copy, dst, raw_slab(u, s).rearrange("p (j c) -> p j c", j=PACK))
+        def pack_slabs(copy, dst, n, count=1):
+            copy(
+                dst.rearrange("p (s c i j) -> p s c j i", s=count, i=LINE, j=PACK),
+                raw_slabs(n, count).rearrange("p (s j c i) -> p s c j i", s=count, i=LINE, j=PACK),
+            )
 
         bank = {}
         da_q = {}
@@ -305,9 +304,9 @@ def tile_moe_bdx_mlp_relu2_kernel(tc, dyT, a, w2, w1, gate, offs, pos1, pos2, ou
                 read_pair(twice_on_vector, LAST_WHOLE - 2, (0,))
                 read_pair(twice_on_scalar, LAST_WHOLE - 2, range(1, QUARTERS))
                 packed_tile(CUT)
-                pack_on_vector(CUT, 0)
+                pack_slabs(nc.vector.tensor_copy, packed[CUT][:, :SLAB], 0)
                 packed_tile(FIRST_Q)
-                pack_on_vector(FIRST_Q, slice(0, 2))
+                pack_slabs(nc.vector.tensor_copy, packed[FIRST_Q][:, : 2 * SLAB], 1, 2)
             weights = quantise(packed[u][:], H)
             for pair in list(staged):
                 quantise_da(pair)
@@ -322,10 +321,10 @@ def tile_moe_bdx_mlp_relu2_kernel(tc, dyT, a, w2, w1, gate, offs, pos1, pos2, ou
                 for q in range(QUARTERS):
                     read(twice_on_vector, bank[E + q][:], q, 0, QUAD)
         multiply_cut(0, packed[CUT][:, :SLAB])
-        pack_on_vector(FIRST_Q, 2)
+        pack_slabs(nc.vector.tensor_copy, packed[FIRST_Q][:, 2 * SLAB : 3 * SLAB], 3)
         early_sums = half_of_quarter_0(0)
 
-        pack_on_vector(FIRST_Q, 3)
+        pack_slabs(nc.vector.tensor_copy, packed[FIRST_Q][:, 3 * SLAB :], 4)
         read_pair(twice_on_vector, LAST_WHOLE, (0,))
         late_sums = half_of_quarter_0(1)
         read(twice_on_vector, early_sums[:], 0, LATE, 2)
@@ -336,18 +335,20 @@ def tile_moe_bdx_mlp_relu2_kernel(tc, dyT, a, w2, w1, gate, offs, pos1, pos2, ou
             if q > 0:
                 read_pair(twice_on_scalar, LAST_WHOLE, (q,))
                 read(twice_on_scalar, bank[u - 1][:], q, LATE, QUAD)
-            cut_slab = raw_slab(u - 1, 2).bitcast(BF16)[:, :SLAB]
-            first_two = raw_slab(u - 1, 3).bitcast(BF16)
-            last_two = held.tile([P, T], F32, name=f"last{q}", tag=f"last{q}", align_bytes=64)
-            pack_on_scalar(cut_slab, CUT, q + 1)
+            n = SLABS * (q + 1)
+            cut_slab = raw_slabs(n - 1 if q else 1)[:, SLAB // 2 :].bitcast(BF16)
+            first_two = raw_slabs(n).bitcast(BF16)
+            last_two = held.tile([P, 2 * SLAB], BF16, name=f"last{q}", tag=f"last{q}", align_bytes=64)
+            res = raw_slabs(n + QUAD - 1, 2)[:, :T]
+            pack_slabs(nc.scalar.copy, cut_slab, n)
             for s in range(QUAD):
-                home = last_two[:].bitcast(BF16) if s // 2 else first_two
-                pack_on_scalar(home[:, s % 2 * SLAB : (s % 2 + 1) * SLAB], u, s)
+                home = last_two[:] if s // 2 else first_two
+                pack_slabs(nc.scalar.copy, home[:, s % 2 * SLAB : (s % 2 + 1) * SLAB], n + 1 + s)
             multiply_cut(q + 1, cut_slab)
             new_banks(u, 1)
             multiply_half(u, 0, first_two)
-            multiply_half(u, 1, last_two[:].bitcast(BF16)[:, : 2 * SLAB], f"last{q + 1}")
-            combine(q, token_tile(), last_two[:], (0, T), (0, T))
+            multiply_half(u, 1, last_two[:], f"last{q + 1}")
+            combine(q, token_tile(), res, (0, T), (0, T))
         q = QUARTERS - 1
         read_pair(twice_on_scalar, LAST_WHOLE, (q,))
         read(twice_on_scalar, bank[UNITS - 1][:], q, LATE, QUAD)

@@ -28,22 +28,20 @@ QUAD = 4
 GROUP = QUAD * C
 GROUPS = S // GROUP
 QUARTERS = K // P
-SLAB = PACK * P
-
+UNIT = PACK * H
 UNITS = 2 * E
-LATE = E - QUAD
-FIRST_Q = E + LATE
-CUT = FIRST_Q - 1
-SLABS = QUAD + 1
-LAST_WHOLE = CUT - 1
-SHARED = (E, E + 1, E + 3)
-A_AFTER = QUAD - 1
-RING = 12
-AHEAD = RING // 2
-PACKED_BUFS = 8
-CODE_BUFS = 4
-LAST_PICKS = (0, T // 2, T)
-LAST_STORES = (0, T // 2, T - C, T)
+LAST = UNITS - 1
+SINGLE = (0, 1, UNITS - 4, UNITS - 3, UNITS - 2, UNITS - 1)
+LEAD = 4
+ORDER = [2 * pair for pair in range(LEAD - 1)]
+ORDER = ORDER + [u for pair in range(LEAD - 1, E // 2) for u in (2 * pair, E + 2 * (pair - LEAD + 1))]
+ORDER = ORDER + [E + 2 * pair for pair in range(E // 2 - LEAD + 1, E // 2)]
+RING = 5
+AHEAD = 3
+PACKED_BUFS = 6
+CODE_BUFS = 6
+V_SHARE = 384
+PIECE = 256
 
 
 def tile_moe_bdx_mlp_relu2_kernel(tc, dyT, a, w2, w1, gate, offs, pos1, pos2, out):
@@ -56,7 +54,6 @@ def tile_moe_bdx_mlp_relu2_kernel(tc, dyT, a, w2, w1, gate, offs, pos1, pos2, ou
         offs_t = held.tile([P, S // STRIPE], U16)
         pos1_t = held.tile([P, T // STRIPE], U16)
         pos2_t = held.tile([P, T // STRIPE], U16)
-        gate_t = [held.tile([P, GROUP], F32, name=f"gate{g}") for g in range(GROUPS)]
         g_q = [
             (
                 held.tile([P, GROUP], U32, name=f"gc{g}", align_bytes=64),
@@ -64,54 +61,45 @@ def tile_moe_bdx_mlp_relu2_kernel(tc, dyT, a, w2, w1, gate, offs, pos1, pos2, ou
             )
             for g in range(GROUPS)
         ]
-        dy = [work.tile([P, T], F32, name=f"dy{j}", tag="tok", bufs=PACK) for j in range(PACK)]
+        dy = [held.tile([P, T], F32, name=f"dy{j}", tag=f"tok{j}") for j in range(PACK)]
         dy_rows = dyT.rearrange("(p j) t -> p j t", j=PACK)
-        a_rows = a.rearrange("(p j) s -> p j s", j=PACK)
 
         nc.sync.dma_start(dy[0][:], dy_rows[:, 0, :])
+        nc.sync.dma_start(offs_t[:], offs)
         gate_cols = held.tile([P, GROUPS, 2 * QUAD], F32)
         nc.sync.dma_start(gate_cols[:, :, :QUAD], gate[0, :].rearrange("(g r c) -> r g c", g=GROUPS, c=QUAD))
-        nc.sync.dma_start(offs_t[:], offs)
         for j in range(1, PACK):
             nc.sync.dma_start(dy[j][:], dy_rows[:, j, :])
-        identity = held.tile([P, P], F32, tag="first", align_bytes=64)
+        identity = held.tile([P, P], F32)
         make_identity(nc, identity[:])
+        spread = []
         for g in range(GROUPS):
-            spread = psum.tile([P, QUAD, P], F32, name="bank")
+            gates = psum.tile([P, QUAD, P], F32, name="bank")
             for c in range(QUAD):
-                nc.tensor.transpose(spread[:, c, :], gate_cols[:, g, c : c + 1].to_broadcast([P, P]), identity[:])
-            nc.scalar.copy(gate_t[g][:].rearrange("p (r c) -> p r c", c=QUAD), spread[:].rearrange("p c r -> p r c"))
+                nc.tensor.transpose(gates[:, c, :], gate_cols[:, g, c : c + 1].to_broadcast([P, P]), identity[:])
+            spread.append(gates)
 
         raw = {}
-        two_units = {}
-        a_t = held.tile([P, PACK, S], F32)
+        a_t = held.tile([P, PACK * S], F32, tag="a")
+        a_planes = a_t[:].rearrange("p (j s) -> p j s", j=PACK)
 
-        def raw_slabs(n, count=1):
-            u = CUT + n // QUAD
-            start = (u % 2 * QUAD + n % QUAD) * SLAB
-            return two_units[u - u % 2][:, start : start + count * SLAB]
-
-        def load(u):
-            if u % 2 == 0:
-                both = held.tile([P, 2 * PACK * H], F32, name=f"raw{u}", tag=f"raw{u % RING}", align_bytes=64)
-                two_units[u] = both
-                raw[u] = both[:, : PACK * H]
-                raw[u + 1] = both[:, PACK * H :]
-                if u < E:
-                    nc.sync.dma_start(
-                        both[:].rearrange("p (e x) -> p e x", e=2),
-                        w2[u : u + 2].rearrange("e (p j) i -> p e (j i)", j=PACK),
-                    )
-            if E <= u < CUT:
-                nc.sync.dma_start(raw[u], w1[u - E].rearrange("(p j) k -> p (j k)", j=PACK))
-            if u >= CUT:
-                for n in range((u - CUT) * QUAD, (u - CUT + 1) * QUAD):
-                    q, s = divmod(n, SLABS)
-                    rows = w1[CUT - E + s].rearrange("(p j) k -> p j k", j=PACK)
-                    nc.sync.dma_start(raw_slabs(n).rearrange("p (j c) -> p j c", j=PACK), rows[:, :, q * P : (q + 1) * P])
-            if u == A_AFTER:
-                nc.sync.dma_start(a_t[:], a_rows)
-            if u == E - 1:
+        def load(step):
+            u = ORDER[step]
+            source, e = (w2, u) if u < E else (w1, u - E)
+            both = held.tile([P, 2 * UNIT], F32, name=f"raw{u}", tag=f"raw{step % RING}", align_bytes=64)
+            raw[u] = both[:, :UNIT]
+            raw[u + 1] = both[:, UNIT:]
+            if u in SINGLE:
+                for half in range(2):
+                    nc.sync.dma_start(raw[u + half], source[e + half].rearrange("(p j) c -> p (j c)", j=PACK))
+            else:
+                nc.sync.dma_start(
+                    both[:].rearrange("p (e x) -> p e x", e=2),
+                    source[e : e + 2].rearrange("e (p j) c -> p e (j c)", j=PACK),
+                )
+            if step == 0:
+                nc.sync.dma_start(a_t[:], a.rearrange("(p j) s -> p (j s)", j=PACK))
+            if step == E // 2:
                 nc.sync.dma_start(pos1_t[:], pos1)
                 nc.sync.dma_start(pos2_t[:], pos2)
 
@@ -121,11 +109,8 @@ def tile_moe_bdx_mlp_relu2_kernel(tc, dyT, a, w2, w1, gate, offs, pos1, pos2, ou
                 planes.rearrange("p j (c i) -> p c j i", i=LINE),
             )
 
-        def quantise(src, columns, tag=None):
-            if tag:
-                codes = held.tile([P, columns], U32, name="late_codes", tag=tag, align_bytes=64)
-            else:
-                codes = work.tile([P, columns], U32, name="wc", bufs=CODE_BUFS, align_bytes=64)
+        def quantise(src, columns):
+            codes = work.tile([P, columns], U32, name="wc", bufs=CODE_BUFS, align_bytes=64)
             scales = work.tile([P, columns], U8, name="ws", bufs=CODE_BUFS, align_bytes=64)
             nc.vector.quantize_mx(out=codes[:].bitcast(FP8X4), scales=scales[:], in_=src)
             return codes, scales
@@ -143,95 +128,65 @@ def tile_moe_bdx_mlp_relu2_kernel(tc, dyT, a, w2, w1, gate, offs, pos1, pos2, ou
                 stop=True,
             )
 
-        g32 = {}
+        def scalar_gather(dst, src):
+            nc.scalar.activation(dst, src, COPY)
+
+        g32 = [held.tile([P, PACK, GROUP], F32, name=f"g32_{g}", tag=f"slots{g}")[:] for g in range(GROUPS - 1)]
+
+        def gather_g(copy, g, j):
+            entries = offs_t[:, g * GROUP // STRIPE : (g + 1) * GROUP // STRIPE]
+            copy(g32[g][:, j, :], dy[j][:].indirect(entries))
+
         gb = {}
 
-        def gather_g(g, j):
-            if j == 0:
-                g32[g] = work.tile([P, PACK, GROUP], F32, name="g32")
-            entries = offs_t[:, g * GROUP // STRIPE : (g + 1) * GROUP // STRIPE]
-            nc.vector.tensor_tensor(g32[g][:, j, :], dy[j][:].indirect(entries), gate_t[g][:], MULT)
-
-        def pack_g(g):
-            if g == 0:
-                gb[g] = held.tile([P, GROUP * PACK], BF16, name="gb", tag="last0", align_bytes=64)[:]
-                interleave(nc.vector.tensor_copy, gb[g], g32[g][:])
-            else:
-                gb[g] = raw[A_AFTER].bitcast(BF16)[:, (g - 1) * GROUP * PACK : g * GROUP * PACK]
-                interleave(nc.scalar.copy, gb[g], g32[g][:])
+        def weigh_g(g):
+            gb[g] = work.tile([P, GROUP * PACK], BF16, name="gb", align_bytes=64)
+            nc.vector.tensor_tensor(
+                gb[g][:].rearrange("p (c i j) -> p c j i", i=LINE, j=PACK),
+                g32[g].rearrange("p j (c i) -> p c j i", i=LINE),
+                spread[g][:].rearrange("p i c -> p c i").unsqueeze(2).to_broadcast([P, P, PACK, LINE]),
+                MULT,
+            )
 
         def quantise_g(g):
-            nc.vector.quantize_mx(out=g_q[g][0][:].bitcast(FP8X4), scales=g_q[g][1][:], in_=gb[g])
+            nc.vector.quantize_mx(out=g_q[g][0][:].bitcast(FP8X4), scales=g_q[g][1][:], in_=gb[g][:])
 
-        packed = {}
-
-        def packed_tile(u):
-            if u == 0:
-                packed[u] = held.tile([P, H * PACK], BF16, name="wb0", tag="first", align_bytes=64)
-            else:
-                packed[u] = work.tile([P, H * PACK], BF16, name="wb", bufs=PACKED_BUFS, align_bytes=64)
-
-        def pack_matrix(u):
-            packed_tile(u)
+        def pack(u):
+            packed = work.tile([P, UNIT], BF16, name="wb", bufs=PACKED_BUFS, align_bytes=64)
             planes = raw[u].rearrange("p (j c) -> p j c", j=PACK)
+            copy = nc.scalar.copy if (u % 2 or u == 0) and u < UNITS - 4 else nc.vector.tensor_copy
             if u < E:
-                nc.scalar.copy(
-                    packed[u][:].rearrange("p (t m j) -> p m j t", t=PACK, j=PACK),
+                copy(
+                    packed[:].rearrange("p (t m j) -> p m j t", t=PACK, j=PACK),
                     planes.rearrange("p j (m t) -> p m j t", t=PACK),
                 )
-            elif u in SHARED:
-                interleave(nc.scalar.copy, packed[u][:, : H * PACK // 2], planes[:, :, : H // 2])
-                interleave(nc.vector.tensor_copy, packed[u][:, H * PACK // 2 :], planes[:, :, H // 2 :])
+            elif u == UNITS - 4:
+                interleave(nc.vector.tensor_copy, packed[:, : V_SHARE * PACK], planes[:, :, :V_SHARE])
+                interleave(nc.scalar.copy, packed[:, V_SHARE * PACK :], planes[:, :, V_SHARE:])
             else:
-                interleave(nc.scalar.copy, packed[u][:], planes)
-
-        def pack_slabs(copy, dst, n, count=1):
-            copy(
-                dst.rearrange("p (s c i j) -> p s c j i", s=count, i=LINE, j=PACK),
-                raw_slabs(n, count).rearrange("p (s j c i) -> p s c j i", s=count, i=LINE, j=PACK),
-            )
+                interleave(copy, packed[:], planes)
+            return packed
 
         bank = {}
         da_q = {}
-        staged = {}
 
-        def new_banks(u, count):
-            for b in range(count):
-                bank[u + b] = psum.tile([P, QUAD, C], F32, name="bank")
+        def new_bank():
+            return psum.tile([P, QUAD, C], F32, name="bank")
 
-        def multiply(u, weights):
-            if u < E:
-                new_banks(u, 1)
-            elif u == E:
-                new_banks(u, QUARTERS)
-            elif u >= E + QUAD and u % 2 == 0:
-                new_banks(u, 2)
-            for t in range(QUAD):
-                if u < E:
-                    one_pass(bank[u][:, t, :], weights, t, g_q[u // QUAD], u % QUAD)
-                elif u < E + QUAD:
-                    one_pass(bank[E + t][:, u - E, :], weights, t, da_q[(u - E) // 2], u % 2)
-                else:
-                    dst = bank[u - u % 2 + t // 2][:, t % 2 * 2 + u % 2, :]
-                    one_pass(dst, weights, t, da_q[(u - E) // 2], u % 2)
-
-        def make_da(pair):
-            staged[pair] = raw[2 * pair + 2].bitcast(BF16)[:, 0 : 2 * C * PACK]
+        def make_da(pair, staged):
             for half in range(2):
                 e = 2 * pair + half
                 nc.vector.scalar_tensor_tensor(
-                    staged[pair][:, half * C * PACK : (half + 1) * C * PACK].rearrange("p (n t) -> p n t", t=PACK),
-                    a_t[:, :, e * C : (e + 1) * C].rearrange("p t n -> p n t"),
+                    staged[:, half * C * PACK : (half + 1) * C * PACK].rearrange("p (n t) -> p n t", t=PACK),
+                    a_planes[:, :, e * C : (e + 1) * C].rearrange("p t n -> p n t"),
                     0.0,
                     bank[e][:].rearrange("p t n -> p n t"),
                     MAX,
                     MULT,
                 )
-
-        def quantise_da(pair):
             codes = held.tile([P, 2 * C], U32, name=f"dc{pair}", align_bytes=64)
             scales = held.tile([P, 2 * C], U8, name=f"ds{pair}", align_bytes=64)
-            nc.vector.quantize_mx(out=codes[:].bitcast(FP8X4), scales=scales[:], in_=staged.pop(pair))
+            nc.vector.quantize_mx(out=codes[:].bitcast(FP8X4), scales=scales[:], in_=staged)
             da_q[pair] = (codes, scales)
 
         dx = {}
@@ -245,111 +200,84 @@ def tile_moe_bdx_mlp_relu2_kernel(tc, dyT, a, w2, w1, gate, offs, pos1, pos2, ou
         def read(twice, sums, q, expert, count):
             twice(dx[q][:, expert * C : (expert + count) * C], sums.rearrange("p s c -> p (s c)"))
 
-        def read_pair(twice, u, quarters):
-            for q in quarters:
-                read(twice, bank[u + q // 2][:, q % 2 * 2 : q % 2 * 2 + 2, :], q, u - E, 2)
+        def first_layer(u):
+            weights = quantise(pack(u)[:], H)
+            bank[u] = new_bank()
+            for t in range(QUAD):
+                one_pass(bank[u][:, t, :], weights, t, g_q[u // QUAD], u % QUAD)
 
-        def half_of_quarter_0(half):
-            weights = quantise(packed[FIRST_Q][:, half * 2 * SLAB : (half + 1) * 2 * SLAB], 2 * P)
-            sums = psum.tile([P, 2, C], F32, name="bank")
-            for t in range(2):
-                one_pass(sums[:, t, :], weights, t, da_q[LATE // 2 + half], t)
-            return sums
-
-        def multiply_half(u, half, src, tag=None):
-            weights = quantise(src, 2 * P, tag)
-            for t in range(2):
-                one_pass(bank[u][:, 2 * half + t, :], weights, t, da_q[LATE // 2 + half], t)
-
-        def multiply_cut(q, src):
-            weights = quantise(src, P)
-            one_pass(bank[LAST_WHOLE + q // 2][:, q % 2 * 2 + 1, :], weights, 0, da_q[(CUT - E) // 2], 1)
-
-        def pieces(cuts):
-            return [(slice(t0, t1), slice(t0 // STRIPE, t1 // STRIPE)) for t0, t1 in zip(cuts, cuts[1:])]
-
-        def combine(q, picked, res, picks, stores):
-            for cols, entries in pieces(picks):
-                nc.vector.tensor_copy(picked[:, cols], dx[q][:].indirect(pos1_t[:, entries]))
-            for cols, entries in pieces(stores):
-                nc.vector.tensor_tensor(res[:, cols], dx[q][:].indirect(pos2_t[:, entries]), picked[:, cols], ADD)
-                nc.sync.dma_start(out[q * P : (q + 1) * P, cols], res[:, cols])
-
-        def token_tile():
-            return work.tile([P, T], F32, name="token", tag="tok", bufs=PACK)
-
-        for u in range(AHEAD):
-            load(u)
-
-        for j in range(PACK):
-            gather_g(0, j)
-        gather_g(1, 0)
-        pack_g(0)
-        gather_g(1, 1)
-        quantise_g(0)
-        gather_g(1, 2)
-        gather_g(1, 3)
-        for j in range(PACK):
-            gather_g(2, j)
-
-        for u in range(CUT):
-            if u + AHEAD < UNITS:
-                load(u + AHEAD)
-            pack_matrix(u)
-            if u == A_AFTER:
-                for g in range(1, GROUPS):
-                    pack_g(g)
-                    quantise_g(g)
-            if u == LAST_WHOLE:
-                read_pair(twice_on_vector, LAST_WHOLE - 2, (0,))
-                read_pair(twice_on_scalar, LAST_WHOLE - 2, range(1, QUARTERS))
-                packed_tile(CUT)
-                pack_slabs(nc.vector.tensor_copy, packed[CUT][:, :SLAB], 0)
-                packed_tile(FIRST_Q)
-                pack_slabs(nc.vector.tensor_copy, packed[FIRST_Q][:, : 2 * SLAB], 1, 2)
-            weights = quantise(packed[u][:], H)
-            for pair in list(staged):
-                quantise_da(pair)
-            multiply(u, weights)
-            if 0 < u <= E and u % 2 == 0:
-                make_da(u // 2 - 1)
-            if u == E:
-                for q in range(2):
-                    dx[q] = work.tile([P, S], F32, name=f"dx{q}", tag="g32")
-                    dx[q + 2] = held.tile([P, S], F32, name=f"dx{q + 2}")
-            if u == E + QUAD:
+        def second_layer(pair):
+            banks = [new_bank() for half in range(2)]
+            for place in range(2):
+                weights = quantise(pack(E + 2 * pair + place)[:], H)
                 for q in range(QUARTERS):
-                    read(twice_on_vector, bank[E + q][:], q, 0, QUAD)
-        multiply_cut(0, packed[CUT][:, :SLAB])
-        pack_slabs(nc.vector.tensor_copy, packed[FIRST_Q][:, 2 * SLAB : 3 * SLAB], 3)
-        early_sums = half_of_quarter_0(0)
+                    one_pass(banks[q // 2][:, q % 2 * 2 + place, :], weights, q, da_q[pair], place)
+            for q in range(QUARTERS):
+                read(twice_on_scalar, banks[q // 2][:, q % 2 * 2 : q % 2 * 2 + 2, :], q, 2 * pair, 2)
 
-        pack_slabs(nc.vector.tensor_copy, packed[FIRST_Q][:, 3 * SLAB :], 4)
-        read_pair(twice_on_vector, LAST_WHOLE, (0,))
-        late_sums = half_of_quarter_0(1)
-        read(twice_on_vector, early_sums[:], 0, LATE, 2)
-        read(twice_on_vector, late_sums[:], 0, LATE + 2, 2)
+        for step in range(AHEAD):
+            load(step)
 
-        for q in range(QUARTERS - 1):
-            u = FIRST_Q + q + 1
-            if q > 0:
-                read_pair(twice_on_scalar, LAST_WHOLE, (q,))
-                read(twice_on_scalar, bank[u - 1][:], q, LATE, QUAD)
-            n = SLABS * (q + 1)
-            cut_slab = raw_slabs(n - 1 if q else 1)[:, SLAB // 2 :].bitcast(BF16)
-            first_two = raw_slabs(n).bitcast(BF16)
-            last_two = held.tile([P, 2 * SLAB], BF16, name=f"last{q}", tag=f"last{q}", align_bytes=64)
-            res = raw_slabs(n + QUAD - 1, 2)[:, :T]
-            pack_slabs(nc.scalar.copy, cut_slab, n)
-            for s in range(QUAD):
-                home = last_two[:] if s // 2 else first_two
-                pack_slabs(nc.scalar.copy, home[:, s % 2 * SLAB : (s % 2 + 1) * SLAB], n + 1 + s)
-            multiply_cut(q + 1, cut_slab)
-            new_banks(u, 1)
-            multiply_half(u, 0, first_two)
-            multiply_half(u, 1, last_two[:], f"last{q + 1}")
-            combine(q, token_tile(), res, (0, T), (0, T))
-        q = QUARTERS - 1
-        read_pair(twice_on_scalar, LAST_WHOLE, (q,))
-        read(twice_on_scalar, bank[UNITS - 1][:], q, LATE, QUAD)
-        combine(q, token_tile(), token_tile(), LAST_PICKS, LAST_STORES)
+        for j in range(PACK):
+            gather_g(nc.vector.tensor_copy, 0, j)
+            gather_g(scalar_gather, 1, j)
+        for g in range(GROUPS - 1):
+            weigh_g(g)
+            quantise_g(g)
+        for q in range(QUARTERS):
+            dx[q] = held.tile([P, S], F32, name=f"dx{q}", tag=f"slots{q}")
+
+        for step in range(E - 1):
+            if step + AHEAD < E:
+                load(step + AHEAD)
+            u = ORDER[step]
+            if u < E:
+                first_layer(u)
+                first_layer(u + 1)
+            else:
+                second_layer((u - E) // 2)
+            if step > 1 and ORDER[step - 1] < E:
+                make_da(ORDER[step - 1] // 2, raw[u + 1].bitcast(BF16)[:, : 2 * C * PACK])
+            if step == 0:
+                first_da = held.tile([P, 2 * C * PACK], BF16, align_bytes=64)
+                make_da(0, first_da[:])
+                g32.append(raw[1].rearrange("p (j s) -> p j s", j=PACK))
+                for j in range(PACK):
+                    gather_g(scalar_gather, 2, j)
+                weigh_g(2)
+                quantise_g(2)
+
+        pair = E // 2 - 1
+        banks = [new_bank() for b in range(3)]
+        home = [banks[0][:, 0:2, :], banks[1][:, 0:2, :], banks[2][:, 0:2, :], banks[2][:, 2:4, :]]
+        weights = quantise(pack(LAST - 1)[:], H)
+        for q in range(QUARTERS):
+            one_pass(home[q][:, 0, :], weights, q, da_q[pair], 0)
+        planes = raw[LAST].rearrange("p (j c) -> p j c", j=PACK)
+        first = work.tile([P, P * PACK], BF16, name="wb", bufs=PACKED_BUFS, align_bytes=64)
+        rest = work.tile([P, 3 * P * PACK], BF16, name="wb", bufs=PACKED_BUFS, align_bytes=64)
+        interleave(nc.vector.tensor_copy, first[:], planes[:, :, :P])
+        interleave(nc.scalar.copy, rest[:, 2 * P * PACK :], planes[:, :, 3 * P :])
+        weights = quantise(first[:], P)
+        one_pass(home[0][:, 1, :], weights, 0, da_q[pair], 1)
+        read(twice_on_scalar, home[0], 0, 2 * pair, 2)
+        interleave(nc.vector.tensor_copy, rest[:, : 2 * P * PACK], planes[:, :, P : 3 * P])
+        weights = quantise(rest[:], 3 * P)
+        for q in range(1, QUARTERS):
+            one_pass(home[q][:, 1, :], weights, q - 1, da_q[pair], 1)
+        for q in range(1, QUARTERS):
+            read(twice_on_vector, home[q], q, 2 * pair, 2)
+
+        res = held.tile([P, QUARTERS * T], F32, tag="a")
+        for q in range(QUARTERS):
+            picked = held.tile([P, T], F32, name=f"picked{q}", tag=f"tok{q}")
+            for t0 in range(0, T, PIECE):
+                cols = slice(t0, t0 + PIECE)
+                entries = slice(t0 // STRIPE, (t0 + PIECE) // STRIPE)
+                place = slice(q * T + t0, q * T + t0 + PIECE)
+                scalar_gather(picked[:, cols], dx[q][:].indirect(pos1_t[:, entries]))
+                nc.vector.tensor_tensor(res[:, place], dx[q][:].indirect(pos2_t[:, entries]), picked[:, cols], ADD)
+                if q == QUARTERS - 1:
+                    nc.sync.dma_start(out[q * P : (q + 1) * P, cols], res[:, place])
+            if q < QUARTERS - 1:
+                nc.sync.dma_start(out[q * P : (q + 1) * P, :], res[:, q * T : (q + 1) * T])

@@ -31,8 +31,11 @@ QUARTERS = K // P
 UNIT = PACK * H
 UNITS = 2 * E
 LAST = UNITS - 1
-SINGLE = (0, 1, UNITS - 4, UNITS - 3, UNITS - 2, UNITS - 1)
-LEAD = 4
+SINGLE = (0, 1)
+CUT = 6
+HALF = UNIT // 2
+BOTH_ON_SCALAR = (0, 4, 8)
+LEAD = 5
 ORDER = [2 * pair for pair in range(LEAD - 1)]
 ORDER = ORDER + [u for pair in range(LEAD - 1, E // 2) for u in (2 * pair, E + 2 * (pair - LEAD + 1))]
 ORDER = ORDER + [E + 2 * pair for pair in range(E // 2 - LEAD + 1, E // 2)]
@@ -40,8 +43,10 @@ RING = 5
 AHEAD = 3
 PACKED_BUFS = 6
 CODE_BUFS = 6
-V_SHARE = 384
-PIECE = 256
+LATE_GROUPS = (((6, 7), (8, 9)), ((6, 7), (8,), (9,)))
+LATE_ON_SCALAR = ((0, 7), (0, 9), (1, 9), (1, 10))
+CUTS = (0, 256, 512, T)
+LAST_CUTS = (0, 256, 512, 640, T)
 
 
 def tile_moe_bdx_mlp_relu2_kernel(tc, dyT, a, w2, w1, gate, offs, pos1, pos2, out):
@@ -80,6 +85,7 @@ def tile_moe_bdx_mlp_relu2_kernel(tc, dyT, a, w2, w1, gate, offs, pos1, pos2, ou
             spread.append(gates)
 
         raw = {}
+        late = {}
         a_t = held.tile([P, PACK * S], F32, tag="a")
         a_planes = a_t[:].rearrange("p (j s) -> p j s", j=PACK)
 
@@ -89,7 +95,16 @@ def tile_moe_bdx_mlp_relu2_kernel(tc, dyT, a, w2, w1, gate, offs, pos1, pos2, ou
             both = held.tile([P, 2 * UNIT], F32, name=f"raw{u}", tag=f"raw{step % RING}", align_bytes=64)
             raw[u] = both[:, :UNIT]
             raw[u + 1] = both[:, UNIT:]
-            if u in SINGLE:
+            if u >= E + CUT:
+                for n in range(QUAD):
+                    half, place = divmod(2 * (e - CUT) + n, E - CUT)
+                    rows = w1[CUT + place].rearrange("(p j) c -> p j c", j=PACK)
+                    late[half, CUT + place] = both[:, n * HALF : (n + 1) * HALF]
+                    nc.sync.dma_start(
+                        late[half, CUT + place].rearrange("p (j c) -> p j c", j=PACK),
+                        rows[:, :, half * K // 2 : (half + 1) * K // 2],
+                    )
+            elif u in SINGLE:
                 for half in range(2):
                     nc.sync.dma_start(raw[u + half], source[e + half].rearrange("(p j) c -> p (j c)", j=PACK))
             else:
@@ -154,15 +169,12 @@ def tile_moe_bdx_mlp_relu2_kernel(tc, dyT, a, w2, w1, gate, offs, pos1, pos2, ou
         def pack(u):
             packed = work.tile([P, UNIT], BF16, name="wb", bufs=PACKED_BUFS, align_bytes=64)
             planes = raw[u].rearrange("p (j c) -> p j c", j=PACK)
-            copy = nc.scalar.copy if (u % 2 or u == 0) and u < UNITS - 4 else nc.vector.tensor_copy
+            copy = nc.scalar.copy if u % 2 or u in BOTH_ON_SCALAR else nc.vector.tensor_copy
             if u < E:
                 copy(
                     packed[:].rearrange("p (t m j) -> p m j t", t=PACK, j=PACK),
                     planes.rearrange("p j (m t) -> p m j t", t=PACK),
                 )
-            elif u == UNITS - 4:
-                interleave(nc.vector.tensor_copy, packed[:, : V_SHARE * PACK], planes[:, :, :V_SHARE])
-                interleave(nc.scalar.copy, packed[:, V_SHARE * PACK :], planes[:, :, V_SHARE:])
             else:
                 interleave(copy, packed[:], planes)
             return packed
@@ -227,7 +239,7 @@ def tile_moe_bdx_mlp_relu2_kernel(tc, dyT, a, w2, w1, gate, offs, pos1, pos2, ou
         for q in range(QUARTERS):
             dx[q] = held.tile([P, S], F32, name=f"dx{q}", tag=f"slots{q}")
 
-        for step in range(E - 1):
+        for step in range((E + CUT) // 2):
             if step + AHEAD < E:
                 load(step + AHEAD)
             u = ORDER[step]
@@ -237,7 +249,8 @@ def tile_moe_bdx_mlp_relu2_kernel(tc, dyT, a, w2, w1, gate, offs, pos1, pos2, ou
             else:
                 second_layer((u - E) // 2)
             if step > 1 and ORDER[step - 1] < E:
-                make_da(ORDER[step - 1] // 2, raw[u + 1].bitcast(BF16)[:, : 2 * C * PACK])
+                first_on_scalar = u if u in BOTH_ON_SCALAR else u + 1
+                make_da(ORDER[step - 1] // 2, raw[first_on_scalar].bitcast(BF16)[:, : 2 * C * PACK])
             if step == 0:
                 first_da = held.tile([P, 2 * C * PACK], BF16, align_bytes=64)
                 make_da(0, first_da[:])
@@ -247,37 +260,40 @@ def tile_moe_bdx_mlp_relu2_kernel(tc, dyT, a, w2, w1, gate, offs, pos1, pos2, ou
                 weigh_g(2)
                 quantise_g(2)
 
-        pair = E // 2 - 1
-        banks = [new_bank() for b in range(3)]
-        home = [banks[0][:, 0:2, :], banks[1][:, 0:2, :], banks[2][:, 0:2, :], banks[2][:, 2:4, :]]
-        weights = quantise(pack(LAST - 1)[:], H)
-        for q in range(QUARTERS):
-            one_pass(home[q][:, 0, :], weights, q, da_q[pair], 0)
-        planes = raw[LAST].rearrange("p (j c) -> p j c", j=PACK)
-        first = work.tile([P, P * PACK], BF16, name="wb", bufs=PACKED_BUFS, align_bytes=64)
-        rest = work.tile([P, 3 * P * PACK], BF16, name="wb", bufs=PACKED_BUFS, align_bytes=64)
-        interleave(nc.vector.tensor_copy, first[:], planes[:, :, :P])
-        interleave(nc.scalar.copy, rest[:, 2 * P * PACK :], planes[:, :, 3 * P :])
-        weights = quantise(first[:], P)
-        one_pass(home[0][:, 1, :], weights, 0, da_q[pair], 1)
-        read(twice_on_scalar, home[0], 0, 2 * pair, 2)
-        interleave(nc.vector.tensor_copy, rest[:, : 2 * P * PACK], planes[:, :, P : 3 * P])
-        weights = quantise(rest[:], 3 * P)
-        for q in range(1, QUARTERS):
-            one_pass(home[q][:, 1, :], weights, q - 1, da_q[pair], 1)
-        for q in range(1, QUARTERS):
-            read(twice_on_vector, home[q], q, 2 * pair, 2)
+        def late_experts(half, experts, banks, first):
+            packed = work.tile([P, HALF * len(experts)], BF16, name="wb", bufs=PACKED_BUFS, align_bytes=64)
+            for n, e in enumerate(experts):
+                copy = nc.scalar.copy if (half, e) in LATE_ON_SCALAR else nc.vector.tensor_copy
+                planes = late[half, e].rearrange("p (j c) -> p j c", j=PACK)
+                interleave(copy, packed[:, n * HALF : (n + 1) * HALF], planes)
+            weights = quantise(packed[:], len(experts) * K // 2)
+            for n, e in enumerate(experts):
+                for t in range(2):
+                    one_pass(banks[t][:, e - first, :], weights, 2 * n + t, da_q[e // 2], e % 2)
 
-        res = held.tile([P, QUARTERS * T], F32, tag="a")
+        for half in range(2):
+            banks = [new_bank() for t in range(2)]
+            for experts in LATE_GROUPS[half]:
+                late_experts(half, experts, banks, CUT)
+            for t in range(2):
+                read(twice_on_scalar, banks[t][:], 2 * half + t, CUT, QUAD)
+            banks = [new_bank() for t in range(2)]
+            for e in range(CUT + QUAD, E):
+                late_experts(half, [e], banks, CUT + QUAD)
+            read(twice_on_scalar, banks[0][:, 0:2, :], 2 * half, CUT + QUAD, 2)
+            read(twice_on_scalar if half else twice_on_vector, banks[1][:, 0:2, :], 2 * half + 1, CUT + QUAD, 2)
+
+        results = held.tile([P, QUARTERS * T], F32, tag="a")
         for q in range(QUARTERS):
             picked = held.tile([P, T], F32, name=f"picked{q}", tag=f"tok{q}")
-            for t0 in range(0, T, PIECE):
-                cols = slice(t0, t0 + PIECE)
-                entries = slice(t0 // STRIPE, (t0 + PIECE) // STRIPE)
-                place = slice(q * T + t0, q * T + t0 + PIECE)
+            res = late[1, E - 1][:, :T] if q == 1 else results[:, q * T : (q + 1) * T]
+            cuts = LAST_CUTS if q == QUARTERS - 1 else CUTS
+            for t0, t1 in zip(cuts, cuts[1:]):
+                cols = slice(t0, t1)
+                entries = slice(t0 // STRIPE, t1 // STRIPE)
                 scalar_gather(picked[:, cols], dx[q][:].indirect(pos1_t[:, entries]))
-                nc.vector.tensor_tensor(res[:, place], dx[q][:].indirect(pos2_t[:, entries]), picked[:, cols], ADD)
+                nc.vector.tensor_tensor(res[:, cols], dx[q][:].indirect(pos2_t[:, entries]), picked[:, cols], ADD)
                 if q == QUARTERS - 1:
-                    nc.sync.dma_start(out[q * P : (q + 1) * P, cols], res[:, place])
+                    nc.sync.dma_start(out[q * P : (q + 1) * P, cols], res[:, cols])
             if q < QUARTERS - 1:
-                nc.sync.dma_start(out[q * P : (q + 1) * P, :], res[:, q * T : (q + 1) * T])
+                nc.sync.dma_start(out[q * P : (q + 1) * P, :], res)

@@ -31,11 +31,11 @@ QUARTERS = K // P
 UNIT = PACK * H
 UNITS = 2 * E
 LAST = UNITS - 1
-SINGLE = (0, 1)
+SINGLE = (0, 1, E + 4, E + 5)
 CUT = 6
 HALF = UNIT // 2
-BOTH_ON_SCALAR = (0, 4, 8)
-LEAD = 5
+ON_VECTOR = (2, 6, 10, E, E + 2, E + 5)
+LEAD = 6
 ORDER = [2 * pair for pair in range(LEAD - 1)]
 ORDER = ORDER + [u for pair in range(LEAD - 1, E // 2) for u in (2 * pair, E + 2 * (pair - LEAD + 1))]
 ORDER = ORDER + [E + 2 * pair for pair in range(E // 2 - LEAD + 1, E // 2)]
@@ -44,7 +44,7 @@ AHEAD = 3
 PACKED_BUFS = 6
 CODE_BUFS = 6
 LATE_GROUPS = (((6, 7), (8, 9)), ((6, 7), (8,), (9,)))
-LATE_ON_SCALAR = ((0, 7), (0, 9), (1, 9), (1, 10))
+LATE_ON_SCALAR = ((0, 7), (0, 10), (1, 9), (1, 10))
 CUTS = (0, 256, 512, T)
 LAST_CUTS = (0, 256, 512, 640, T)
 
@@ -169,7 +169,7 @@ def tile_moe_bdx_mlp_relu2_kernel(tc, dyT, a, w2, w1, gate, offs, pos1, pos2, ou
         def pack(u):
             packed = work.tile([P, UNIT], BF16, name="wb", bufs=PACKED_BUFS, align_bytes=64)
             planes = raw[u].rearrange("p (j c) -> p j c", j=PACK)
-            copy = nc.scalar.copy if u % 2 or u in BOTH_ON_SCALAR else nc.vector.tensor_copy
+            copy = nc.vector.tensor_copy if u in ON_VECTOR else nc.scalar.copy
             if u < E:
                 copy(
                     packed[:].rearrange("p (t m j) -> p m j t", t=PACK, j=PACK),
@@ -249,7 +249,7 @@ def tile_moe_bdx_mlp_relu2_kernel(tc, dyT, a, w2, w1, gate, offs, pos1, pos2, ou
             else:
                 second_layer((u - E) // 2)
             if step > 1 and ORDER[step - 1] < E:
-                first_on_scalar = u if u in BOTH_ON_SCALAR else u + 1
+                first_on_scalar = u + 1 if u in ON_VECTOR else u
                 make_da(ORDER[step - 1] // 2, raw[first_on_scalar].bitcast(BF16)[:, : 2 * C * PACK])
             if step == 0:
                 first_da = held.tile([P, 2 * C * PACK], BF16, align_bytes=64)

@@ -34,6 +34,7 @@ LAST = UNITS - 1
 SINGLE = (0, 1, E + 4, E + 5)
 CUT = 6
 HALF = UNIT // 2
+SLAB = UNIT // 4
 ON_VECTOR = (2, 6, 10, E, E + 2, E + 5)
 LEAD = 6
 ORDER = [2 * pair for pair in range(LEAD - 1)]
@@ -45,8 +46,13 @@ PACKED_BUFS = 6
 CODE_BUFS = 6
 LATE_GROUPS = (((6, 7), (8, 9)), ((6, 7), (8,), (9,)))
 LATE_ON_SCALAR = ((0, 7), (0, 10), (1, 9), (1, 10))
-CUTS = (0, 256, 512, T)
-LAST_CUTS = (0, 256, 512, 640, T)
+PICKS = ((0, 256, T), (0, T), (0, 256, 512, T), (0, 256, 512, 640, T))
+STORES = (
+    ((None, 0, 256, T),),
+    ((11, 0, 384, T),),
+    ((None, 0, 256, 512, T),),
+    ((None, 0, 256), (None, 256, 512), (None, 512, 640), (None, 640, T)),
+)
 
 
 def tile_moe_bdx_mlp_relu2_kernel(tc, dyT, a, w2, w1, gate, offs, pos1, pos2, out):
@@ -86,6 +92,7 @@ def tile_moe_bdx_mlp_relu2_kernel(tc, dyT, a, w2, w1, gate, offs, pos1, pos2, ou
 
         raw = {}
         late = {}
+        slab = {}
         a_t = held.tile([P, PACK * S], F32, tag="a")
         a_planes = a_t[:].rearrange("p (j s) -> p j s", j=PACK)
 
@@ -100,10 +107,15 @@ def tile_moe_bdx_mlp_relu2_kernel(tc, dyT, a, w2, w1, gate, offs, pos1, pos2, ou
                     half, place = divmod(2 * (e - CUT) + n, E - CUT)
                     rows = w1[CUT + place].rearrange("(p j) c -> p j c", j=PACK)
                     late[half, CUT + place] = both[:, n * HALF : (n + 1) * HALF]
-                    nc.sync.dma_start(
-                        late[half, CUT + place].rearrange("p (j c) -> p j c", j=PACK),
-                        rows[:, :, half * K // 2 : (half + 1) * K // 2],
-                    )
+                    if (half, CUT + place) == (0, E - 1):
+                        for q in range(2):
+                            slab[q] = late[0, E - 1][:, q * SLAB : (q + 1) * SLAB].rearrange("p (j c) -> p j c", j=PACK)
+                            nc.sync.dma_start(slab[q], rows[:, :, q * P : (q + 1) * P])
+                    else:
+                        nc.sync.dma_start(
+                            late[half, CUT + place].rearrange("p (j c) -> p j c", j=PACK),
+                            rows[:, :, half * K // 2 : (half + 1) * K // 2],
+                        )
             elif u in SINGLE:
                 for half in range(2):
                     nc.sync.dma_start(raw[u + half], source[e + half].rearrange("(p j) c -> p (j c)", j=PACK))
@@ -271,6 +283,7 @@ def tile_moe_bdx_mlp_relu2_kernel(tc, dyT, a, w2, w1, gate, offs, pos1, pos2, ou
                 for t in range(2):
                     one_pass(banks[t][:, e - first, :], weights, 2 * n + t, da_q[e // 2], e % 2)
 
+        last = {}
         for half in range(2):
             banks = [new_bank() for t in range(2)]
             for experts in LATE_GROUPS[half]:
@@ -278,22 +291,33 @@ def tile_moe_bdx_mlp_relu2_kernel(tc, dyT, a, w2, w1, gate, offs, pos1, pos2, ou
             for t in range(2):
                 read(twice_on_scalar, banks[t][:], 2 * half + t, CUT, QUAD)
             banks = [new_bank() for t in range(2)]
-            for e in range(CUT + QUAD, E):
-                late_experts(half, [e], banks, CUT + QUAD)
-            read(twice_on_scalar, banks[0][:, 0:2, :], 2 * half, CUT + QUAD, 2)
-            read(twice_on_scalar if half else twice_on_vector, banks[1][:, 0:2, :], 2 * half + 1, CUT + QUAD, 2)
+            late_experts(half, [E - 2], banks, E - 2)
+            if half:
+                late_experts(half, [E - 1], banks, E - 2)
+            else:
+                for q in range(2):
+                    packed = work.tile([P, SLAB], BF16, name="wb", bufs=PACKED_BUFS, align_bytes=64)
+                    interleave(nc.vector.tensor_copy, packed[:], slab[q])
+                    one_pass(banks[q][:, 1, :], quantise(packed[:], P), 0, da_q[E // 2 - 1], 1)
+            for t in range(2):
+                last[2 * half + t] = banks[t][:, 0:2, :]
+            read(twice_on_scalar, last[2 * half], 2 * half, CUT + QUAD, 2)
+            if half == 0:
+                read(twice_on_vector, last[1], 1, CUT + QUAD, 2)
 
         results = held.tile([P, QUARTERS * T], F32, tag="a")
         for q in range(QUARTERS):
             picked = held.tile([P, T], F32, name=f"picked{q}", tag=f"tok{q}")
-            res = late[1, E - 1][:, :T] if q == 1 else results[:, q * T : (q + 1) * T]
-            cuts = LAST_CUTS if q == QUARTERS - 1 else CUTS
-            for t0, t1 in zip(cuts, cuts[1:]):
-                cols = slice(t0, t1)
-                entries = slice(t0 // STRIPE, t1 // STRIPE)
-                scalar_gather(picked[:, cols], dx[q][:].indirect(pos1_t[:, entries]))
-                nc.vector.tensor_tensor(res[:, cols], dx[q][:].indirect(pos2_t[:, entries]), picked[:, cols], ADD)
-                if q == QUARTERS - 1:
-                    nc.sync.dma_start(out[q * P : (q + 1) * P, cols], res[:, cols])
-            if q < QUARTERS - 1:
-                nc.sync.dma_start(out[q * P : (q + 1) * P, :], res)
+            if q == QUARTERS - 1:
+                read(twice_on_scalar, last[q], q, CUT + QUAD, 2)
+            for t0, t1 in zip(PICKS[q], PICKS[q][1:]):
+                scalar_gather(picked[:, t0:t1], dx[q][:].indirect(pos1_t[:, t0 // STRIPE : t1 // STRIPE]))
+            for stored in STORES[q]:
+                home = results[:, q * T : (q + 1) * T] if stored[0] is None else late[1, stored[0]][:, :T]
+                cuts = stored[1:]
+                for t0, t1 in zip(cuts, cuts[1:]):
+                    cols = slice(t0, t1)
+                    entries = slice(t0 // STRIPE, t1 // STRIPE)
+                    nc.vector.tensor_tensor(home[:, cols], dx[q][:].indirect(pos2_t[:, entries]), picked[:, cols], ADD)
+                cols = slice(cuts[0], cuts[-1])
+                nc.sync.dma_start(out[q * P : (q + 1) * P, cols], home[:, cols])

@@ -33,6 +33,7 @@ UNITS = 2 * E
 LAST = UNITS - 1
 SINGLE = (0, 1, E + 4, E + 5)
 CUT = 6
+SHARED = E + CUT - 2
 HALF = UNIT // 2
 SLAB = UNIT // 4
 ON_VECTOR = (2, 6, 10, E, E + 2, E + 5)
@@ -187,6 +188,9 @@ def tile_moe_bdx_mlp_relu2_kernel(tc, dyT, a, w2, w1, gate, offs, pos1, pos2, ou
                     packed[:].rearrange("p (t m j) -> p m j t", t=PACK, j=PACK),
                     planes.rearrange("p j (m t) -> p m j t", t=PACK),
                 )
+            elif u == SHARED:
+                interleave(nc.vector.tensor_copy, packed[:, :HALF], planes[:, :, : K // 2])
+                interleave(nc.scalar.copy, packed[:, HALF:], planes[:, :, K // 2 :])
             else:
                 interleave(copy, packed[:], planes)
             return packed
@@ -230,14 +234,25 @@ def tile_moe_bdx_mlp_relu2_kernel(tc, dyT, a, w2, w1, gate, offs, pos1, pos2, ou
             for t in range(QUAD):
                 one_pass(bank[u][:, t, :], weights, t, g_q[u // QUAD], u % QUAD)
 
+        four = []
+
         def second_layer(pair):
-            banks = [new_bank() for half in range(2)]
+            if pair == 0:
+                four.extend(new_bank() for q in range(QUARTERS))
+            if pair < 2:
+                homes = [four[q][:, 2 * pair : 2 * pair + 2, :] for q in range(QUARTERS)]
+            else:
+                banks = [new_bank() for half in range(2)]
+                homes = [banks[q // 2][:, q % 2 * 2 : q % 2 * 2 + 2, :] for q in range(QUARTERS)]
             for place in range(2):
                 weights = quantise(pack(E + 2 * pair + place)[:], H)
                 for q in range(QUARTERS):
-                    one_pass(banks[q // 2][:, q % 2 * 2 + place, :], weights, q, da_q[pair], place)
+                    one_pass(homes[q][:, place, :], weights, q, da_q[pair], place)
             for q in range(QUARTERS):
-                read(twice_on_scalar, banks[q // 2][:, q % 2 * 2 : q % 2 * 2 + 2, :], q, 2 * pair, 2)
+                if pair == 1:
+                    read(twice_on_scalar, four[q][:], q, 0, QUAD)
+                if pair == 2:
+                    read(twice_on_scalar, homes[q], q, QUAD, 2)
 
         for step in range(AHEAD):
             load(step)
@@ -303,7 +318,7 @@ def tile_moe_bdx_mlp_relu2_kernel(tc, dyT, a, w2, w1, gate, offs, pos1, pos2, ou
                 last[2 * half + t] = banks[t][:, 0:2, :]
             read(twice_on_scalar, last[2 * half], 2 * half, CUT + QUAD, 2)
             if half == 0:
-                read(twice_on_vector, last[1], 1, CUT + QUAD, 2)
+                read(twice_on_scalar, last[1], 1, CUT + QUAD, 2)
 
         results = held.tile([P, QUARTERS * T], F32, tag="a")
         for q in range(QUARTERS):

@@ -31,7 +31,7 @@ QUARTERS = K // P
 UNIT = PACK * H
 UNITS = 2 * E
 LAST = UNITS - 1
-SINGLE = (0, 1, E + 4, E + 5)
+SINGLE = (E + 4, E + 5)
 CUT = 6
 SHARED = E + CUT - 2
 HALF = UNIT // 2
@@ -46,11 +46,11 @@ AHEAD = 3
 PACKED_BUFS = 6
 CODE_BUFS = 6
 LATE_GROUPS = (((6, 7), (8, 9)), ((6, 7), (8,), (9,)))
-LATE_ON_SCALAR = ((0, 7), (0, 10), (1, 9), (1, 10))
+LATE_ON_SCALAR = ((0, 7), (0, 10), (1, 9))
 PICKS = ((0, 256, T), (0, T), (0, 256, 512, T), (0, 256, 512, 640, T))
 STORES = (
     ((None, 0, 256, T),),
-    ((11, 0, 384, T),),
+    ((11, 0, T),),
     ((None, 0, 256, 512, T),),
     ((None, 0, 256), (None, 256, 512), (None, 512, 640), (None, 640, T)),
 )
@@ -79,7 +79,7 @@ def tile_moe_bdx_mlp_relu2_kernel(tc, dyT, a, w2, w1, gate, offs, pos1, pos2, ou
         nc.sync.dma_start(dy[0][:], dy_rows[:, 0, :])
         nc.sync.dma_start(offs_t[:], offs)
         gate_cols = held.tile([P, GROUPS, 2 * QUAD], F32)
-        nc.sync.dma_start(gate_cols[:, :, :QUAD], gate[0, :].rearrange("(g r c) -> r g c", g=GROUPS, c=QUAD))
+        nc.scalar.dma_start(gate_cols[:, :, :QUAD], gate[0, :].rearrange("(g r c) -> r g c", g=GROUPS, c=QUAD))
         for j in range(1, PACK):
             nc.sync.dma_start(dy[j][:], dy_rows[:, j, :])
         identity = held.tile([P, P], F32)
@@ -306,10 +306,18 @@ def tile_moe_bdx_mlp_relu2_kernel(tc, dyT, a, w2, w1, gate, offs, pos1, pos2, ou
             for t in range(2):
                 read(twice_on_scalar, banks[t][:], 2 * half + t, CUT, QUAD)
             banks = [new_bank() for t in range(2)]
-            late_experts(half, [E - 2], banks, E - 2)
             if half:
-                late_experts(half, [E - 1], banks, E - 2)
+                tiles = [work.tile([P, HALF], BF16, name="wb", bufs=PACKED_BUFS, align_bytes=64) for t in range(2)]
+                for n, copy in enumerate((nc.scalar.copy, nc.vector.tensor_copy)):
+                    planes = late[1, E - 2 + n].rearrange("p (j c) -> p j c", j=PACK)
+                    for t in range(2):
+                        interleave(copy, tiles[t][:, n * SLAB : (n + 1) * SLAB], planes[:, :, t * P : (t + 1) * P])
+                for t in range(2):
+                    weights = quantise(tiles[t][:], 2 * P)
+                    for n in range(2):
+                        one_pass(banks[t][:, n, :], weights, n, da_q[E // 2 - 1], n)
             else:
+                late_experts(half, [E - 2], banks, E - 2)
                 for q in range(2):
                     packed = work.tile([P, SLAB], BF16, name="wb", bufs=PACKED_BUFS, align_bytes=64)
                     interleave(nc.vector.tensor_copy, packed[:], slab[q])

@@ -47,10 +47,10 @@ PACKED_BUFS = 6
 CODE_BUFS = 6
 LATE_GROUPS = (((6, 7), (8, 9)), ((6, 7), (8,), (9,)))
 LATE_ON_SCALAR = ((0, 7), (0, 10), (1, 9))
-PICKS = ((0, 256, T), (0, T), (0, 256, 512, T), (0, 256, 512, 640, T))
+PICKS = ((0, 256, 512, T), (0, 384, T), (0, 256, 512, T), (0, 256, 512, 640, T))
 STORES = (
-    ((None, 0, 256, T),),
-    ((11, 0, T),),
+    ((None, 0, 256, 512, T),),
+    ((11, 0, 384, T),),
     ((None, 0, 256, 512, T),),
     ((None, 0, 256), (None, 256, 512), (None, 512, 640), (None, 640, T)),
 )
@@ -308,9 +308,10 @@ def tile_moe_bdx_mlp_relu2_kernel(tc, dyT, a, w2, w1, gate, offs, pos1, pos2, ou
             banks = [new_bank() for t in range(2)]
             if half:
                 tiles = [work.tile([P, HALF], BF16, name="wb", bufs=PACKED_BUFS, align_bytes=64) for t in range(2)]
-                for n, copy in enumerate((nc.scalar.copy, nc.vector.tensor_copy)):
+                for n in range(2):
                     planes = late[1, E - 2 + n].rearrange("p (j c) -> p j c", j=PACK)
                     for t in range(2):
+                        copy = nc.scalar.copy if n + t == 0 else nc.vector.tensor_copy
                         interleave(copy, tiles[t][:, n * SLAB : (n + 1) * SLAB], planes[:, :, t * P : (t + 1) * P])
                 for t in range(2):
                     weights = quantise(tiles[t][:], 2 * P)
@@ -328,19 +329,22 @@ def tile_moe_bdx_mlp_relu2_kernel(tc, dyT, a, w2, w1, gate, offs, pos1, pos2, ou
             if half == 0:
                 read(twice_on_scalar, last[1], 1, CUT + QUAD, 2)
 
+        found = {}
         results = held.tile([P, QUARTERS * T], F32, tag="a")
         for q in range(QUARTERS):
             picked = held.tile([P, T], F32, name=f"picked{q}", tag=f"tok{q}")
             if q == QUARTERS - 1:
                 read(twice_on_scalar, last[q], q, CUT + QUAD, 2)
             for t0, t1 in zip(PICKS[q], PICKS[q][1:]):
-                scalar_gather(picked[:, t0:t1], dx[q][:].indirect(pos1_t[:, t0 // STRIPE : t1 // STRIPE]))
+                held_back = q == 1 and t0 > 0
+                found[q, t0] = late[1, 9][:, t0:t1] if held_back else picked[:, t0:t1]
+                scalar_gather(found[q, t0], dx[q][:].indirect(pos1_t[:, t0 // STRIPE : t1 // STRIPE]))
             for stored in STORES[q]:
                 home = results[:, q * T : (q + 1) * T] if stored[0] is None else late[1, stored[0]][:, :T]
                 cuts = stored[1:]
                 for t0, t1 in zip(cuts, cuts[1:]):
                     cols = slice(t0, t1)
                     entries = slice(t0 // STRIPE, t1 // STRIPE)
-                    nc.vector.tensor_tensor(home[:, cols], dx[q][:].indirect(pos2_t[:, entries]), picked[:, cols], ADD)
+                    nc.vector.tensor_tensor(home[:, cols], dx[q][:].indirect(pos2_t[:, entries]), found[q, t0], ADD)
                 cols = slice(cuts[0], cuts[-1])
                 nc.sync.dma_start(out[q * P : (q + 1) * P, cols], home[:, cols])

from contextlib import ExitStack

import concourse.mybir as mybir
from concourse.masks import make_identity

K, T, E, C, H, N = 512, 768, 12, 128, 512, 512
S = E * C

F32 = mybir.dt.float32
BF16 = mybir.dt.bfloat16
U32 = mybir.dt.uint32
U16 = mybir.dt.uint16
U8 = mybir.dt.uint8
FP8X4 = mybir.dt.float8_e4m3fn_x4
MULT = mybir.AluOpType.mult
ADD = mybir.AluOpType.add
MAX = mybir.AluOpType.max
COPY = mybir.ActivationFunctionType.Copy

FLOPS = 2 * 2 * S * N * H
BYTES = 4 * (N * T + H * S + 2 * E * N * H + S + K * T) + 2 * 128 * (S + 2 * T) // 16

P = 128
PACK = 4
LINE = 4
STRIPE = 16
QUAD = 4
GROUP = QUAD * C
GROUPS = S // GROUP
QUARTERS = K // P
UNIT = PACK * H
UNITS = 2 * E
LAST = UNITS - 1
SINGLE = (E + 4, E + 5)
CUT = 6
SHARED = E + CUT - 2
HALF = UNIT // 2
SLAB = UNIT // 4
ON_VECTOR = (2, 6, 10, E, E + 2, E + 5)
LEAD = 6
ORDER = [2 * pair for pair in range(LEAD - 1)]
ORDER = ORDER + [u for pair in range(LEAD - 1, E // 2) for u in (2 * pair, E + 2 * (pair - LEAD + 1))]
ORDER = ORDER + [E + 2 * pair for pair in range(E // 2 - LEAD + 1, E // 2)]
RING = 5
AHEAD = 3
PACKED_BUFS = 6
CODE_BUFS = 6
LATE_GROUPS = (((6, 7), (8, 9)), ((6, 7), (8,), (9,)))
LATE_ON_SCALAR = ((0, 7), (0, 10), (1, 9))
PICKS = ((0, 256, 512, T), (0, 384, T), (0, 256, 512, T), (0, 256, 512, 640, T))
STORES = (
    ((None, 0, 256, 512, T),),
    ((11, 0, 384, T),),
    ((None, 0, 256, 512, T),),
    ((None, 0, 256), (None, 256, 512), (None, 512, 640), (None, 640, T)),
)


def tile_moe_bdx_mlp_relu2_kernel(tc, dyT, a, w2, w1, gate, offs, pos1, pos2, out):
    nc = tc.nc
    with ExitStack() as ctx:
        held = ctx.enter_context(tc.tile_pool(name="held", bufs=1))
        work = ctx.enter_context(tc.tile_pool(name="work", bufs=2))
        psum = ctx.enter_context(tc.psum_pool(name="psum", bufs=8))

        offs_t = held.tile([P, S // STRIPE], U16)
        pos1_t = held.tile([P, T // STRIPE], U16)
        pos2_t = held.tile([P, T // STRIPE], U16)
        g_q = [
            (
                held.tile([P, GROUP], U32, name=f"gc{g}", align_bytes=64),
                held.tile([P, GROUP], U8, name=f"gs{g}", align_bytes=64),
            )
            for g in range(GROUPS)
        ]
        dy = [held.tile([P, T], F32, name=f"dy{j}", tag=f"tok{j}") for j in range(PACK)]
        dy_rows = dyT.rearrange("(p j) t -> p j t", j=PACK)

        nc.sync.dma_start(dy[0][:], dy_rows[:, 0, :])
        nc.sync.dma_start(offs_t[:], offs)
        gate_cols = held.tile([P, GROUPS, 2 * QUAD], F32)
        nc.scalar.dma_start(gate_cols[:, :, :QUAD], gate[0, :].rearrange("(g r c) -> r g c", g=GROUPS, c=QUAD))
        for j in range(1, PACK):
            nc.sync.dma_start(dy[j][:], dy_rows[:, j, :])
        identity = held.tile([P, P], F32)
        make_identity(nc, identity[:])
        spread = []
        for g in range(GROUPS):
            gates = psum.tile([P, QUAD, P], F32, name="bank")
            for c in range(QUAD):
                nc.tensor.transpose(gates[:, c, :], gate_cols[:, g, c : c + 1].to_broadcast([P, P]), identity[:])
            spread.append(gates)

        raw = {}
        late = {}
        slab = {}
        a_t = held.tile([P, PACK * S], F32, tag="a")
        a_planes = a_t[:].rearrange("p (j s) -> p j s", j=PACK)

        def load(step):
            u = ORDER[step]
            source, e = (w2, u) if u < E else (w1, u - E)
            both = held.tile([P, 2 * UNIT], F32, name=f"raw{u}", tag=f"raw{step % RING}", align_bytes=64)
            raw[u] = both[:, :UNIT]
            raw[u + 1] = both[:, UNIT:]
            if u >= E + CUT:
                for n in range(QUAD):
                    half, place = divmod(2 * (e - CUT) + n, E - CUT)
                    rows = w1[CUT + place].rearrange("(p j) c -> p j c", j=PACK)
                    late[half, CUT + place] = both[:, n * HALF : (n + 1) * HALF]
                    if (half, CUT + place) == (0, E - 1):
                        for q in range(2):
                            slab[q] = late[0, E - 1][:, q * SLAB : (q + 1) * SLAB].rearrange("p (j c) -> p j c", j=PACK)
                            nc.sync.dma_start(slab[q], rows[:, :, q * P : (q + 1) * P])
                    else:
                        nc.sync.dma_start(
                            late[half, CUT + place].rearrange("p (j c) -> p j c", j=PACK),
                            rows[:, :, half * K // 2 : (half + 1) * K // 2],
                        )
            elif u in SINGLE:
                for half in range(2):
                    nc.sync.dma_start(raw[u + half], source[e + half].rearrange("(p j) c -> p (j c)", j=PACK))
            else:
                nc.sync.dma_start(
                    both[:].rearrange("p (e x) -> p e x", e=2),
                    source[e : e + 2].rearrange("e (p j) c -> p e (j c)", j=PACK),
                )
            if step == 0:
                nc.sync.dma_start(a_t[:], a.rearrange("(p j) s -> p (j s)", j=PACK))
            if step == E // 2:
                nc.sync.dma_start(pos1_t[:], pos1)
                nc.sync.dma_start(pos2_t[:], pos2)

        def interleave(copy, dst, planes):
            copy(
                dst.rearrange("p (c i j) -> p c j i", i=LINE, j=PACK),
                planes.rearrange("p j (c i) -> p c j i", i=LINE),
            )

        def quantise(src, columns):
            codes = work.tile([P, columns], U32, name="wc", bufs=CODE_BUFS, align_bytes=64)
            scales = work.tile([P, columns], U8, name="ws", bufs=CODE_BUFS, align_bytes=64)
            nc.vector.quantize_mx(out=codes[:].bitcast(FP8X4), scales=scales[:], in_=src)
            return codes, scales

        def one_pass(dst, weights, t, moving, place):
            rows = slice(t * P, (t + 1) * P)
            cols = slice(place * C, (place + 1) * C)
            nc.tensor.matmul_mx(
                out=dst,
                lhsT=weights[0][:, rows].bitcast(FP8X4),
                lhsT_scale=weights[1][:, rows],
                rhs=moving[0][:, cols].bitcast(FP8X4),
                rhs_scale=moving[1][:, cols],
                start=True,
                stop=True,
            )

        def scalar_gather(dst, src):
            nc.scalar.activation(dst, src, COPY)

        g32 = [held.tile([P, PACK, GROUP], F32, name=f"g32_{g}", tag=f"slots{g}")[:] for g in range(GROUPS - 1)]

        def gather_g(copy, g, j):
            entries = offs_t[:, g * GROUP // STRIPE : (g + 1) * GROUP // STRIPE]
            copy(g32[g][:, j, :], dy[j][:].indirect(entries))

        gb = {}

        def weigh_g(g):
            gb[g] = work.tile([P, GROUP * PACK], BF16, name="gb", align_bytes=64)
            nc.vector.tensor_tensor(
                gb[g][:].rearrange("p (c i j) -> p c j i", i=LINE, j=PACK),
                g32[g].rearrange("p j (c i) -> p c j i", i=LINE),
                spread[g][:].rearrange("p i c -> p c i").unsqueeze(2).to_broadcast([P, P, PACK, LINE]),
                MULT,
            )

        def quantise_g(g):
            nc.vector.quantize_mx(out=g_q[g][0][:].bitcast(FP8X4), scales=g_q[g][1][:], in_=gb[g][:])

        def pack(u):
            packed = work.tile([P, UNIT], BF16, name="wb", bufs=PACKED_BUFS, align_bytes=64)
            planes = raw[u].rearrange("p (j c) -> p j c", j=PACK)
            copy = nc.vector.tensor_copy if u in ON_VECTOR else nc.scalar.copy
            if u < E:
                copy(
                    packed[:].rearrange("p (t m j) -> p m j t", t=PACK, j=PACK),
                    planes.rearrange("p j (m t) -> p m j t", t=PACK),
                )
            elif u == SHARED:
                interleave(nc.vector.tensor_copy, packed[:, :HALF], planes[:, :, : K // 2])
                interleave(nc.scalar.copy, packed[:, HALF:], planes[:, :, K // 2 :])
            else:
                interleave(copy, packed[:], planes)
            return packed

        bank = {}
        da_q = {}

        def new_bank():
            return psum.tile([P, QUAD, C], F32, name="bank")

        def make_da(pair, staged):
            for half in range(2):
                e = 2 * pair + half
                nc.vector.scalar_tensor_tensor(
                    staged[:, half * C * PACK : (half + 1) * C * PACK].rearrange("p (n t) -> p n t", t=PACK),
                    a_planes[:, :, e * C : (e + 1) * C].rearrange("p t n -> p n t"),
                    0.0,
                    bank[e][:].rearrange("p t n -> p n t"),
                    MAX,
                    MULT,
                )
            codes = held.tile([P, 2 * C], U32, name=f"dc{pair}", align_bytes=64)
            scales = held.tile([P, 2 * C], U8, name=f"ds{pair}", align_bytes=64)
            nc.vector.quantize_mx(out=codes[:].bitcast(FP8X4), scales=scales[:], in_=staged)
            da_q[pair] = (codes, scales)

        dx = {}

        def twice_on_vector(dst, src):
            nc.vector.tensor_scalar_mul(dst, src, 2.0)

        def twice_on_scalar(dst, src):
            nc.scalar.activation(dst, src, COPY, scale=2.0)

        def read(twice, sums, q, expert, count):
            twice(dx[q][:, expert * C : (expert + count) * C], sums.rearrange("p s c -> p (s c)"))

        def first_layer(u):
            weights = quantise(pack(u)[:], H)
            bank[u] = new_bank()
            for t in range(QUAD):
                one_pass(bank[u][:, t, :], weights, t, g_q[u // QUAD], u % QUAD)

        four = []

        def second_layer(pair):
            if pair == 0:
                four.extend(new_bank() for q in range(QUARTERS))
            if pair < 2:
                homes = [four[q][:, 2 * pair : 2 * pair + 2, :] for q in range(QUARTERS)]
            else:
                banks = [new_bank() for half in range(2)]
                homes = [banks[q // 2][:, q % 2 * 2 : q % 2 * 2 + 2, :] for q in range(QUARTERS)]
            for place in range(2):
                weights = quantise(pack(E + 2 * pair + place)[:], H)
                for q in range(QUARTERS):
                    one_pass(homes[q][:, place, :], weights, q, da_q[pair], place)
            for q in range(QUARTERS):
                if pair == 1:
                    read(twice_on_scalar, four[q][:], q, 0, QUAD)
                if pair == 2:
                    read(twice_on_scalar, homes[q], q, QUAD, 2)

        for step in range(AHEAD):
            load(step)

        for j in range(PACK):
            gather_g(nc.vector.tensor_copy, 0, j)
            gather_g(scalar_gather, 1, j)
        for g in range(GROUPS - 1):
            weigh_g(g)
            quantise_g(g)
        for q in range(QUARTERS):
            dx[q] = held.tile([P, S], F32, name=f"dx{q}", tag=f"slots{q}")

        for step in range((E + CUT) // 2):
            if step + AHEAD < E:
                load(step + AHEAD)
            u = ORDER[step]
            if u < E:
                first_layer(u)
                first_layer(u + 1)
            else:
                second_layer((u - E) // 2)
            if step > 1 and ORDER[step - 1] < E:
                first_on_scalar = u + 1 if u in ON_VECTOR else u
                make_da(ORDER[step - 1] // 2, raw[first_on_scalar].bitcast(BF16)[:, : 2 * C * PACK])
            if step == 0:
                first_da = held.tile([P, 2 * C * PACK], BF16, align_bytes=64)
                make_da(0, first_da[:])
                g32.append(raw[1].rearrange("p (j s) -> p j s", j=PACK))
                for j in range(PACK):
                    gather_g(scalar_gather, 2, j)
                weigh_g(2)
                quantise_g(2)

        def late_experts(half, experts, banks, first):
            packed = work.tile([P, HALF * len(experts)], BF16, name="wb", bufs=PACKED_BUFS, align_bytes=64)
            for n, e in enumerate(experts):
                copy = nc.scalar.copy if (half, e) in LATE_ON_SCALAR else nc.vector.tensor_copy
                planes = late[half, e].rearrange("p (j c) -> p j c", j=PACK)
                interleave(copy, packed[:, n * HALF : (n + 1) * HALF], planes)
            weights = quantise(packed[:], len(experts) * K // 2)
            for n, e in enumerate(experts):
                for t in range(2):
                    one_pass(banks[t][:, e - first, :], weights, 2 * n + t, da_q[e // 2], e % 2)

        last = {}
        for half in range(2):
            banks = [new_bank() for t in range(2)]
            for experts in LATE_GROUPS[half]:
                late_experts(half, experts, banks, CUT)
            for t in range(2):
                read(twice_on_scalar, banks[t][:], 2 * half + t, CUT, QUAD)
            banks = [new_bank() for t in range(2)]
            if half:
                tiles = [work.tile([P, HALF], BF16, name="wb", bufs=PACKED_BUFS, align_bytes=64) for t in range(2)]
                for n in range(2):
                    planes = late[1, E - 2 + n].rearrange("p (j c) -> p j c", j=PACK)
                    for t in range(2):
                        copy = nc.scalar.copy if n + t == 0 else nc.vector.tensor_copy
                        interleave(copy, tiles[t][:, n * SLAB : (n + 1) * SLAB], planes[:, :, t * P : (t + 1) * P])
                for t in range(2):
                    weights = quantise(tiles[t][:], 2 * P)
                    for n in range(2):
                        one_pass(banks[t][:, n, :], weights, n, da_q[E // 2 - 1], n)
            else:
                late_experts(half, [E - 2], banks, E - 2)
                for q in range(2):
                    packed = work.tile([P, SLAB], BF16, name="wb", bufs=PACKED_BUFS, align_bytes=64)
                    interleave(nc.vector.tensor_copy, packed[:], slab[q])
                    one_pass(banks[q][:, 1, :], quantise(packed[:], P), 0, da_q[E // 2 - 1], 1)
            for t in range(2):
                last[2 * half + t] = banks[t][:, 0:2, :]
            read(twice_on_scalar, last[2 * half], 2 * half, CUT + QUAD, 2)
            if half == 0:
                read(twice_on_scalar, last[1], 1, CUT + QUAD, 2)

        found = {}
        results = held.tile([P, QUARTERS * T], F32, tag="a")
        for q in range(QUARTERS):
            picked = held.tile([P, T], F32, name=f"picked{q}", tag=f"tok{q}")
            if q == QUARTERS - 1:
                read(twice_on_scalar, last[q], q, CUT + QUAD, 2)
            for t0, t1 in zip(PICKS[q], PICKS[q][1:]):
                held_back = q == 1 and t0 > 0
                found[q, t0] = late[1, 9][:, t0:t1] if held_back else picked[:, t0:t1]
                scalar_gather(found[q, t0], dx[q][:].indirect(pos1_t[:, t0 // STRIPE : t1 // STRIPE]))
            for stored in STORES[q]:
                home = results[:, q * T : (q + 1) * T] if stored[0] is None else late[1, stored[0]][:, :T]
                cuts = stored[1:]
                for t0, t1 in zip(cuts, cuts[1:]):
                    cols = slice(t0, t1)
                    entries = slice(t0 // STRIPE, t1 // STRIPE)
                    nc.vector.tensor_tensor(home[:, cols], dx[q][:].indirect(pos2_t[:, entries]), found[q, t0], ADD)
                cols = slice(cuts[0], cuts[-1])
                nc.sync.dma_start(out[q * P : (q + 1) * P, cols], home[:, cols])
